import numpy as np, ml_dtypes
CORES = [242,247,114,119]
N = 4
BF = ml_dtypes.bfloat16
W, H, Q, L, V, TH, TH2 = 4096, 256, 16, 2, 4, 1082, 820
J = Q - L + 1
HALF = (J - 1) // 2
B = HALF + L - 1
def which(s, z):
    return np.maximum(1, np.add.reduce((s <= z[:, None, :]).astype(np.int64), axis=1)) - 1
def place(s, c, k, p):
    sk = np.take_along_axis(s, k[:, None, :], 1); ck = np.take_along_axis(c, k[:, None, :], 1)
    return ((p - sk) * (2 * ck + 1) + 37 * ck) & (W - 1)
def pick(x, f):
    return np.take_along_axis(x, f.reshape(8, 1, -1), 2).reshape(8, 16, -1, H)
def seen(x, s, c, z):
    o = (5 * np.arange(H)) & (H - 1); got = []
    for q in range(N):
        so = s[q][..., o]; co = c[q][..., o]
        got.append(pick(x[q], place(so, co, which(so, z[q]), z[q][:, None, :] + np.arange(Q)[None, :, None] - B)))
    return np.stack(got)
def parts(rng):
    span = rng.integers(116, 141, (N, 8, 1, 1))
    x = 128 + np.floor((rng.random((N, 8, 16, W), dtype=np.float32) - 0.5) * span).astype(np.int64)
    tm = 128 + np.floor((rng.random((N, 8, 16, L, H)) - 0.5) * span[..., None]).astype(np.int64)
    s = np.sort(rng.integers(0, W, (N, 8, 16, H)), axis=2); c = rng.integers(0, 1024, (N, 8, 16, H)); z = rng.integers(16, 3001, (N, 8, H))
    return x, s, c, z, tm
def pack(x, s, c, z, tm):
    return {"xl": np.ascontiguousarray(x).reshape(N, 128, W).astype(np.float32).astype(BF), "s0": np.ascontiguousarray(s).reshape(N, 128, H).astype(np.int32),
            "cf": np.ascontiguousarray(c).reshape(N, 128, H).astype(np.int32), "z0": np.ascontiguousarray(z).astype(np.int32),
            "t0": np.ascontiguousarray(tm).reshape(N, 128, L * H).astype(np.float32).astype(BF)}
def setup_inputs(rng):
    return pack(*parts(rng))
def setup_inputs_spread(rng):
    amps = np.array([4, 16, 32, 64, 96, 128])
    x = np.clip(128 + np.floor((2 * rng.random((N, 8, 16, W), dtype=np.float32) - 1) * rng.choice(amps, (N, 8, 1, W))), 0, 255).astype(np.int64)
    tm = np.clip(128 + np.floor((2 * rng.random((N, 8, 16, L, H)) - 1) * rng.choice(amps, (N, 8, 1, L, H))), 0, 255).astype(np.int64)
    s = np.where(rng.random((N, 8, 1, H)) < 0.5, rng.integers(0, W, (N, 8, 16, H)), np.clip(np.floor(np.exp2(12 * rng.random((N, 8, 16, H)))).astype(np.int64) - 1, 0, W - 1))
    c = np.clip(np.floor(np.exp2(10 * rng.random((N, 8, 16, H)))).astype(np.int64) - 1, 0, 1023)
    z = np.where(rng.random((N, 8, H)) < 0.5, rng.integers(16, 3001, (N, 8, H)), np.clip(np.floor(np.exp2(11.6 * rng.random((N, 8, H)))).astype(np.int64), 16, 3000))
    return pack(x, np.sort(s, axis=2), c, z, tm)
def turns(w, u):
    return np.where((u & 1) == 1, 255 - w, w)
def setup_inputs_ends(rng):
    x = 255 * (rng.random((N, 8, 16, W), dtype=np.float32) < 0.125).astype(np.int64); tm = 255 * (rng.random((N, 8, 16, L, H)) < 0.125).astype(np.int64)
    flip = rng.permutation(np.array([0, 0, 1, 1]))
    for g in range(2, 6):
        if flip[g - 2] == 1: x[:, g] = 255 - x[:, g]; tm[:, g] = 255 - tm[:, g]
    nz = rng.integers(0, 17, (N, 8, 1, H)); low = np.where(np.arange(16).reshape(1, 1, 16, 1) < nz, 0, W - 1)
    s = np.where(rng.random((N, 8, 1, H)) < 0.5, low, (W - 1) * rng.integers(0, 2, (N, 8, 16, H))); s[..., 0] = 0; s[..., H - 1] = W - 1
    c = 1023 * rng.integers(0, 2, (N, 8, 16, H)); z = 16 + 2984 * rng.integers(0, 2, (N, 8, H)); z[..., 0] = 16; z[..., H - 1] = 3000
    level = 255 * int(rng.integers(0, 2)); turn = int(rng.integers(0, 2))
    x[:, 7] = level; rec = 255 * rng.integers(0, 2, (N, 1, 1, H)); rec[..., 0] = 255 - level; rec[..., H - 1] = 255 - level; rec[..., 1] = level; rec[..., H - 2] = level; tm[:, 7] = rec
    for q in range(N): x[q, 0] = 255 * ((q + turn) % 2)
    tm[:, 0] = 255 * rng.integers(0, 2, (N, 1, 1, H))
    x[:, 1, :, 0::2] = 0; x[:, 1, :, 1::2] = 255; tm[:, 1] = 255 * rng.integers(0, 2, (N, 1, L, H))
    code = 255 * rng.integers(0, 2, (16, HALF * N))
    for q in range(N): x[q, 6] = code[:, (np.arange(W) - HALF * q) % (HALF * N)]
    s[:, 6] = 0; c[:, 6] = 0
    b = int(rng.integers(0, N)); s[:, 5] = W - 1; c[:, 5] = 1023; z[:, 5] = 3000; z[b, 5] = 16
    u = np.arange(W) - 4300; col = (u * 2047 + 37 * 1023) & (W - 1)
    far = W - 1 + HALF * (V - 1 - (V - 1) // N)
    p = 255 * rng.integers(0, 2, (16, 1)); other = np.where(rng.permutation(16).reshape(16, 1) < 8, 255 - p, p)
    period = HALF * (N - 1); ring = 255 * rng.integers(0, 2, (16, period)); ring[:, int(u[np.argmin(col)]) % period] = (255 - turns(p, far - HALF))[:, 0]
    for d in range(N):
        near = turns(p if d % 2 == 0 else other, u)
        if d == N - 1: near = np.where((u >= -far - HALF) & (u < -far - HALF + L), turns(p, u), near)
        x[(b + d) % N, 5][:, col] = np.where(u < -2600, near, ring[:, (u + HALF * d) % period])
    y = seen(x, s, c, z)
    tm[:, 6] = y[:, 6, :, J - 1:J - 1 + L]; tm[:, 5] = y[:, 5, :, :L]; tm[b, 5] = turns(other, np.arange(L))[:, :, None]
    return pack(x, s, c, z, tm)
def setup_inputs_corners(rng):
    x, s1, c, z, tm = parts(rng); gs = rng.permutation(8)
    x[:, gs[0]] = 120 + (x[:, gs[0]] & 15); x[:, gs[1]] = rng.integers(0, 256, (N, 16, W))
    kind = rng.integers(0, 8, (N, 8, 1, H)); s = np.where(kind == 1, s1[:, :, 5:6], s1); s = np.where(kind == 2, s1[:, :, ::-1], s); s = np.where(kind == 3, W - 1, s)
    s = np.where(kind == 4, np.arange(16).reshape(1, 1, 16, 1), s); s = np.where(kind == 5, rng.permuted(s1, axis=2), s)
    c = np.where(rng.random((N, 8, 16, H)) < 0.3, rng.choice(np.array([0, 1, 511, 512, 1023]), (N, 8, 16, H)), c)
    so = s[..., (5 * np.arange(H)) & (H - 1)]; near = np.take_along_axis(so, rng.integers(0, 16, (N, 8, 1, H)), 2)[:, :, 0]
    z = np.clip(near + rng.choice(np.array([-6, -1, 0, 1, 5, Q - 1, Q, Q + 1]), (N, 8, H)), 16, 3000)
    y = seen(x, s, c, z); j0 = rng.choice(np.array([0, 1, HALF, J - 1]), (N, 8, 1, 1, H)); m = np.take_along_axis(y, j0 + np.arange(L).reshape(1, 1, 1, L, 1), 3)
    tm = np.where(rng.random((N, 8, 1, 1, H)) < 0.6, m, tm)
    tm[:, gs[2]] = 255 * rng.integers(0, 2, (N, 1, L, H)); tm[:, gs[3]] = m[:, gs[3]]
    tm[:, gs[4]] = 255 * rng.integers(0, 2, (N, 1, L, H)); tm[:, gs[4], :, :, H - 1] = m[:, gs[4], :, :, H - 1]
    return pack(x, s, c, z, tm)
def steps(rng):
    b = TH2 // 16; e = rng.integers(-8, 9, 8)
    return b + np.concatenate([e, -e]) + (np.arange(16) < TH2 - 16 * b).astype(np.int64)
def pairs(rng, total, w):
    a = np.zeros(16, np.int64); a[[0, 9]] = (w + 1) // 2; a[[1, 8]] = w // 2
    rest = total - 2 * w; b = rest // 12; e = rng.integers(-8, 9, 6)
    a[[2, 3, 4, 5, 6, 7, 10, 11, 12, 13, 14, 15]] = b + np.concatenate([e, -e]) + (np.arange(12) < rest - 12 * b).astype(np.int64)
    return a
def setup_inputs_edges(rng):
    x, s, c, z, tm = parts(rng)
    for g in range(8):
        if g % 4 == 1: continue
        p0 = rng.integers(50, 71, 16); p1 = p0 + steps(rng); p2 = p1 + steps(rng); p3 = p2 - steps(rng); p3[int(rng.integers(0, 16))] -= 1
        p = np.stack([p0, p1, p2, p3], axis=1)
        for q in range(N): x[q, g] = p[:, (np.arange(W) + int(rng.integers(0, 4))) & 3]
    w = 257 + 4 * int(rng.integers(0, 6)); p0 = rng.integers(20, 61, 16); p1 = p0 + pairs(rng, TH2 + 1, w); p2 = p1 + rng.integers(1, 4, 16); p3 = p2 - pairs(rng, TH2, w + 2)
    p = np.stack([p0, p1, p2, p3], axis=1)
    for q in range(N): x[q, 5] = p[:, (np.arange(W) + int(rng.integers(0, 4))) & 3]
    y = seen(x, s, c, z); dist = rng.choice(np.array([0, TH - 1, TH, TH + 1]), (N, 8, 1, 1, H)); j0 = rng.integers(0, 4, (N, 8, 1, 1, H))
    m = np.take_along_axis(y, j0 + np.arange(L).reshape(1, 1, 1, L, 1), 3); each = dist // (16 * L)
    d = each + (np.arange(16 * L).reshape(1, 1, 16, L, 1) < dist - 16 * L * each)
    sign = np.where(m < 80, -1, np.where(m > 135, 1, 1 - 2 * (np.arange(16).reshape(1, 1, 16, 1, 1) & 1)))
    planted = (np.arange(8) % 4 != 1).reshape(1, 8, 1, 1, 1)
    return pack(x, s, c, z, np.where(planted, m + sign * d, tm))
def check_inputs(d):
    bad = []
    for k, lo, hi in (("xl", 0, 255), ("s0", 0, W - 1), ("cf", 0, 1023), ("z0", 16, 3000), ("t0", 0, 255)):
        a = np.asarray(d[k]).astype(np.float64)
        if not (np.min(a) >= lo and np.max(a) <= hi): bad.append("range of " + k)
        elif np.any(a != np.floor(a)): bad.append("whole numbers in " + k)
    return bad
def reference(xl, s0, cf, z0, t0):
    x = xl.astype(np.int32).reshape(N, 8, 16, W); s = s0.astype(np.int64).reshape(N, 8, 16, H); c = cf.astype(np.int64).reshape(N, 8, 16, H)
    z = z0.astype(np.int64); tm = t0.astype(np.int32).reshape(N, 8, 16, L, H); ties = np.zeros((N, 8), np.int64)
    row = np.arange(16)[None, :, None]; m = np.arange(Q)[None, :, None]
    for t in range(V):
        for r in range(N):
            q = (r + t) % N
            o = ((5 * np.arange(H)[None, :] + ties[r][:, None]) & (H - 1))[:, None, :]
            so = np.take_along_axis(s[q], o, 2); co = np.take_along_axis(c[q], o, 2)
            k = which(so, z[r])
            y = pick(x[q], place(so, co, k, z[r][:, None, :] + m - B))
            e = np.stack([np.add.reduce(np.abs(y[:, :, j:j + L] - tm[r]), axis=(1, 2)) for j in range(J)])
            best = np.argmin(e, axis=0); tie = np.min(e, axis=0) < TH
            so = so + np.where(tie[:, None, :] & (row >= k[:, None, :]), HALF - best[:, None, :], 0)
            np.put_along_axis(s[q], o, so, 2)
            zz = np.where(tie, z[r], np.maximum(z[r] - Q, 0)); k = np.where(tie, k, which(so, zz))
            v = pick(x[q], place(so, co, k, zz[:, None, :] + m))
            over = (np.add.reduce(np.abs(v[:, :, 1:] - v[:, :, :-1]), axis=1) > TH2)[:, L - 1:]
            n = np.where(np.any(over, axis=1), L + np.argmax(over, axis=1), Q)
            tm[r] = np.take_along_axis(v, n[:, None, None, :] - L + np.arange(L)[None, None, :, None], 2)
            z[r] = zz + n - 1
            ties[r] = np.add.reduce(tie.astype(np.int64), axis=1)
    return {"ys": s.reshape(N, 128, H).astype(np.float32), "yz": z.astype(np.float32), "yt": tm.reshape(N, 128, L * H).astype(np.float32).astype(BF)}

@@ -1,0 +1,589 @@
+import numpy as np
+import comms_topo
+from concourse.bass import DstId, RemoteDMATransfer
+from concourse.mybir import dt, AluOpType, AxisListType, ActivationFunctionType
+
+OP = AluOpType
+AF = ActivationFunctionType
+NV, W, ZC, TH, TH2 = 4, 4096, 1536, 1082, 820
+NC = 128
+SYNCNS = 100
+PE_NS = 0.5
+JA = (8, 4)
+YSPLIT = [[("V", 64), ("A", 64)], [("A", 128)]]
+VSPLIT = [[("V", 32), ("A", 32), ("V", 32), ("A", 32)]] * 2
+TQ = ("V", "A")
+DQ = "V"
+BI = {'M0': -19957, 'S0': 8812, 'Q0': 8916, 'A0': -13949, 'V1': -3468, 'M1': -4459, 'C0': -1044, 'N0': 789, 'D1': -6115, 'V0': -5027, 'C1': -327, 'R0': -3667, 'L1': -1914, 'D0': 5816, 'P': 922, 'A1': 9610, 'R1': 6757, 'Y1': 901}
+CORD = (1, 0)
+RECV = 2500
+GN = 1.56
+
+SCRATCH = {}
+
+
+def _b(name, cols, dtype, where="sbuf", rows=128):
+    SCRATCH[name] = (where, [rows, cols], dtype)
+
+
+for _v in range(4):
+    _b("XL%d" % _v, W, "bfloat16")
+    _b("CF%d" % _v, 256, "float32")
+    _b("SX%d" % _v, 257, "float32")
+    _b("SR%d" % (_v + 1), 257, "float32")
+for _n, _c, _d in (("CFI", 256, "int32"), ("S0I", 256, "int32"), ("TT", 512, "bfloat16"), ("YSO", 256, "float32"),
+                   ("SROT0", 256, "float32"), ("SROT1", 256, "float32"), ("D0", 256, "float32"), ("D1", 256, "float32"),
+                   ("CH0", 256, "float16"), ("CH1", 256, "float16"),
+                   ("BLKf", 128, "float32"), ("SEL", 2048, "bfloat16"), ("IDh", 128, "float16"),
+                   ("MMC1", 128, "float16"), ("MMC2", 128, "float16"),
+                   ("G32", 8, "bfloat16"), ("GM16", 8, "bfloat16"), ("G16", 8, "bfloat16"), ("Gn", 8, "bfloat16"), ("G205", 8, "float32"),
+                   ("RST", 128, "float32"), ("ONE", 128, "bfloat16"), ("ONEh", 128, "float16"), ("CROW", 128, "bfloat16"),
+                   ("KT", 8, "bfloat16"),
+                   ("EXz", 128, "float16"), ("EXn", 128, "float16"), ("EXzn", 128, "float16"), ("EXs", 8, "float16"),
+                   ("AP8", 8, "float32"), ("LO", 16, "uint16"), ("LS", 16, "uint16")):
+    _b(_n, _c, _d)
+VIRT = {}
+for _p, _c, _d, _l in (("PF", 1, "float32", "rg rr r7 q3 rp1 rm8 rpos wz wn wm wzn r16 dA"), ("PI", 1, "int32", "rowI rgI rrI r7I q3I"),
+                       ("PJ", 16, "int32", "c16 i16 n205 o5a o5b LA LB LC LD"), ("PG", 128, "float32", "cg cr colF TRf MA MB RS0 CRW2"),
+                       ("PB", 128, "bfloat16", "BLKb BLKn BM0 BM1 TRI IDb IDn")):
+    for _k, _n in enumerate(_l.split()):
+        VIRT[_n] = (_p, _k * _c, _c)
+    _b(_p, _c * len(_l.split()), _d)
+_b("Z8I", 256, "int32", rows=8)
+_b("Z8", 256, "float16", rows=8)
+_b("YZ", 256, "float32", rows=8)
+for _k in range(2):
+    for _n, _c, _d in (("MASK", NC, "bfloat16"), ("X", NC, "float32"), ("XS", NC, "float32"), ("CS", NC, "float16"),
+                       ("LI", NC, "int32"), ("LJ", NC, "int32"), ("OFF", NC, "uint16"), ("Y", 16 * NC, "bfloat16"),
+                       ("V", 16 * NC, "bfloat16"), ("MX", 30 * NC, "bfloat16"), ("AX", max(1, 2 * max(JA)) * NC, "bfloat16"), ("SC", 128, "float32"), ("KI", 8, "int32"),
+                       ("JJ", 8, "int32"), ("DZ", 8, "float32"), ("ZL", 8, "float32"), ("TD", 8, "float32"),
+                       ("SM", 24, "float16"), ("GE", NC, "float32"), ("AB", 16 * NC, "bfloat16"),
+                       ("OV", NC, "bfloat16"), ("IZ", NC, "bfloat16"), ("TO", 16, "uint16")):
+        _b("%s_%d" % (_n, _k), _c, _d)
+    _b("ST_%d" % _k, NC, "float16", rows=24)
+    for _n in ("K", "T", "E", "V"):
+        _b("p%s%d" % (_n, _k), 512, "float32", where="psum")
+
+SEMAPHORES = ["sV", "sA", "sP", "sG"]
+SEMAPHORES += ["d_" + n for n in ("s0", "cf", "z0", "t00", "t01", "t10", "t11", "xa", "xb", "ys", "yz", "ya0", "ya1", "yb0", "yb1")]
+for _v in range(1, 4):
+    SEMAPHORES += ["%s%d" % (n, _v) for n in ("rca", "rla", "rlb", "lca", "lla", "llb")]
+for _v in range(1, 5):
+    SEMAPHORES += ["%s%d%d" % (n, _v, c) for n in ("rs", "ls") for c in range(2)]
+
+
+class _Plan(dict):
+    pass
+
+
+def plan(g, core, T, topo):
+    rank = T.rank_of(core)
+    n = len(T.cores)
+    ops = []
+    tag = ["c"]
+
+    def B(name):
+        if name in VIRT:
+            p, lo, c = VIRT[name]
+            return (p, lo, lo + c)
+        return (name, 0, SCRATCH[name][1][1])
+
+    def op(q, fns, reads, writes, cost, kind="c", sem=None, cnt=0):
+        ops.append(dict(tag=tag[0], q=q, fns=fns, r=reads, w=writes, cost=cost, kind=kind, sem=sem, cnt=cnt))
+        return len(ops) - 1
+
+    def ap(x):
+        if len(x) == 3:
+            return T[x[0]][:, x[1]:x[2]]
+        if x[3] == "p":
+            return T[x[0]][0:x[4], x[1]:x[2]]
+        return T[x[0]][:, x[1]:x[2]:x[3]]
+
+    def width(x):
+        if len(x) > 3 and x[3] != "p":
+            return -(-(x[2] - x[1]) // x[3])
+        return x[2] - x[1]
+
+    def psum(x):
+        return SCRATCH[x[0]][0] == "psum"
+
+    def reg(x):
+        return (x[0], x[1], x[2])
+
+    def tt(o, a, b, alu):
+        c = width(o) * (1 if psum(a) or psum(b) else 2)
+        op("V", [lambda: g.vector.tensor_tensor(ap(o), ap(a), ap(b), alu)], [reg(a), reg(b)], [reg(o)], max(64, c))
+
+    def sc(x):
+        return ap(x) if isinstance(x, tuple) else x
+
+    def ts(o, a, s1, op0, s2=None, op1=None):
+        rd = [reg(a)] + [reg(s) for s in (s1, s2) if isinstance(s, tuple)]
+        if op1 is None:
+            f = [lambda: g.vector.tensor_scalar(ap(o), ap(a), sc(s1), None, op0)]
+        else:
+            f = [lambda: g.vector.tensor_scalar(ap(o), ap(a), sc(s1), sc(s2), op0, op1)]
+        op("V", f, rd, [reg(o)], max(64, width(o)))
+
+    def cp(o, a):
+        op("V", [lambda: g.vector.tensor_copy(ap(o), ap(a))], [reg(a)], [reg(o)], max(64, width(o)))
+
+    def ms(o, val):
+        op("V", [lambda: g.vector.memset(ap(o), val)], [], [reg(o)], max(64, width(o)))
+
+    def gather(q, o, win, off, scale=1.0, bias=0.0):
+        cost = 60 + GN * width(o)
+        if q == "V":
+            f = lambda: g.vector.tensor_copy(ap(o), ap(win).indirect(ap(off)))
+            if scale != 1.0 or bias != 0.0:
+                f = lambda: g.vector.tensor_scalar(ap(o), ap(win).indirect(ap(off)), scale, bias, OP.mult, OP.add)
+        else:
+            f = lambda: g.scalar.activation(ap(o), ap(win).indirect(ap(off)), AF.Copy)
+            if scale != 1.0 or bias != 0.0:
+                f = lambda: g.scalar.activation(ap(o), ap(win).indirect(ap(off)), AF.Identity, bias=bias, scale=scale)
+        op(q, [f], [reg(win), reg(off)], [reg(o)], cost)
+
+    def mm(o, pairs, start=True, stop=True, wreg=None):
+        fns, rd, cost = [], [], 0
+        for k, (l, r) in enumerate(pairs):
+            fns.append(lambda l=l, r=r, k=k: g.tensor.matmul(ap(o), ap(l), ap(r), start and k == 0, stop and k == len(pairs) - 1))
+            rd += [reg(l), reg(r)]
+            cost += max(min(64, width(l)), width(r)) * (4 if SCRATCH[l[0]][2] == "float32" else 1) * PE_NS
+        op("P", fns, rd, [wreg or reg(o)], cost)
+
+    def dma(q, o, a, rd, wr, sem, cost):
+        eng = g.sync if q == "S" else g.scalar
+        op(q, [lambda: eng.dma_start(o, a)], rd, wr, cost, kind="dma", sem=sem)
+
+    def send(dst, out, src, rs, ls):
+        rid, pid = topo.addr(dst, core)
+        m = topo.mask(core, dst)
+        op("G", [lambda: g.remote_dma(ap(out), ap(src), T.sem[rs], T.sem[ls], pid, rid, m)], [reg(src)], [], 1000,
+           kind="send", sem=ls, cnt=len(topo.engines(core, dst)))
+        return len(ops) - 1
+
+    def recv(o, src, rs, cost, after):
+        op("R", [], [], [reg(o)], cost, kind="recv", sem=rs, cnt=len(topo.engines(src, core)))
+        ops[-1]["after"] = after
+
+    dma("S", ap(B("S0I")), T.s0[:, :], [], [B("S0I")], "d_s0", 2500)
+    dma("A", ap(B("CFI")), T.cf[:, :], [], [B("CFI")], "d_cf", 2500)
+    dma("A", T.Z8I[:, :], T.z0[:, :], [], [B("Z8I")], "d_z0", 2500)
+    dma("S", T.XL0[:, 0:2048], T.xl[:, 0:2048], [], [("XL0", 0, 2048)], "d_xa", 5500)
+    dma("S", T.XL0[:, 2048:4096], T.xl[:, 2048:4096], [], [("XL0", 2048, 4096)], "d_xb", 7500)
+    for c in range(2):
+        for a in range(2):
+            x = ("TT", 256 * c + NC * a, 256 * c + NC * a + NC)
+            dma("A", ap(x), T.t0[:, 256 * a + NC * c:256 * a + NC * c + NC], [], [x], "d_t%d%d" % (c, a), 3500)
+    def iota(o, pat, base, cm):
+        if SCRATCH[o[0]][2] == "int32":
+            f = [lambda: g.iota(ap(o), pat, base, cm)]
+        else:
+            f = [lambda: g.iota(ap(o), pat, base, cm, allow_small_or_imprecise_dtypes=True)]
+        op("G", f, [], [reg(o)], 130 + 2 * width(o))
+
+    def act(o, a, bias, scale):
+        op("A", [lambda: g.scalar.activation(ap(o), ap(a), AF.Identity, bias=bias, scale=scale)], [reg(a)], [reg(o)], max(64, width(o)))
+    iota(B("rowI"), [[0, 1]], 0, 1)
+    iota(B("c16"), [[16, 16]], 0, 0)
+    iota(B("cg"), [[1, 8], [0, 16]], 0, 0)
+    iota(B("cr"), [[0, 8], [1, 16]], 0, 0)
+    iota(B("colF"), [[1, 128]], 0, 0)
+    iota(B("wm"), [[0, 1]], 0, 1)
+    AND, SHR = OP.bitwise_and, OP.arith_shift_right
+    ts(B("rrI"), B("rowI"), 15, AND)
+    cp(B("rr"), B("rrI"))
+    ts(B("i16"), B("c16"), B("rr"), OP.add)
+    ts(B("o5a"), B("i16"), 5, OP.mult)
+    ts(B("o5b"), B("o5a"), 255, AND)
+    cp(B("LO"), B("o5b"))
+    ts(B("rgI"), B("rowI"), 4, SHR)
+    cp(B("rg"), B("rgI"))
+    ts(B("r7I"), B("rowI"), 7, AND)
+    cp(B("r7"), B("r7I"))
+    ts(B("q3I"), B("rowI"), 3, SHR)
+    cp(B("q3"), B("q3I"))
+    ts(B("wz"), B("q3"), 0.0, OP.is_equal)
+    ts(B("EXz"), B("cg"), B("r7"), OP.is_equal, B("wz"), OP.mult)
+    c8 = (B("colF")[0], B("colF")[1], B("colF")[1] + 8)
+    ts(B("EXs"), c8, B("r7"), OP.is_equal, B("wz"), OP.mult)
+    ts(B("BLKb"), B("cg"), B("rg"), OP.is_equal)
+    ts(B("rp1"), B("rr"), 1.0, OP.add)
+    ts(B("rm8"), B("rr"), -8.0, OP.add)
+    ts(("Z8", 0, 256), ("Z8I", 0, 256), -float(ZC), OP.add)
+    cp(B("CF0"), B("CFI"))
+    gather("V", B("SROT0"), B("S0I"), B("LO"), 1.0, -float(ZC))
+
+    def prep_c(v, q):
+        p = v % 2
+        gather(DQ, B("D%d" % p), B("CF%d" % v), B("LO"), 2.0, 1.0)
+        ts(B("CH%d" % p), B("D%d" % p), 0.5, OP.mult, -0.5, OP.add)
+    prep_c(0, "A")
+    for c in range(2):
+        mm(("pK%d" % c, 0, NC), [(("EXz", 0, 128, "p", 8), ("Z8", c * NC, c * NC + NC, "p", 8))])
+        mm(("pE%d" % c, 128, 136), [(("Z8", c * NC, c * NC + NC, "p", 8), ("EXs", 0, 8, "p", 8))])
+    ts(B("BLKf"), B("cg"), B("rg"), OP.is_equal)
+    act(B("MA"), B("cr"), 21.0, 2.0)
+    tt(B("MMC1"), B("MA"), B("BLKf"), OP.mult)
+    ts(B("IDb"), B("colF"), B("wm"), OP.is_equal)
+    for c in range(2):
+        ts(B("BM%d" % c), B("cr"), 14.5 - JA[c], OP.is_lt, -16.0, OP.mult)
+        tt(B("BM%d" % c), B("BM%d" % c), B("BLKb"), OP.mult)
+    ms(B("ONE"), 1.0)
+    ts(B("CRW2"), B("cr"), 15.0, OP.is_equal, 524288.0 - 15.0, OP.mult)
+    tt(B("CROW"), B("CRW2"), B("cr"), OP.add)
+    ts(B("G32"), c8, B("rg"), OP.is_equal, 32.0, OP.mult)
+    act(B("G16"), B("G32"), 0.0, 0.5)
+    act(B("GM16"), B("G32"), 0.0, -0.5)
+    ts(B("RS0"), B("cr"), 0.0, OP.is_equal)
+    act(B("RST"), B("RS0"), -1.0e9, 2.0e9)
+    ts(B("IDh"), B("colF"), B("wm"), OP.is_equal)
+    ts(B("wn"), B("q3"), 1.0, OP.is_equal)
+    ts(B("wzn"), B("q3"), 2.0, OP.is_equal, -7.0, OP.mult)
+    tt(B("wn"), B("wn"), B("wzn"), OP.add)
+    tt(B("wzn"), B("wn"), B("wz"), OP.add)
+    ts(B("EXn"), B("cg"), B("r7"), OP.is_equal, B("wn"), OP.mult)
+    ts(B("EXzn"), B("cg"), B("r7"), OP.is_equal, B("wzn"), OP.mult)
+    act(B("MB"), B("cr"), 37.0, 2.0)
+    tt(B("MMC2"), B("MB"), B("BLKf"), OP.mult)
+    act(B("IDn"), B("IDb"), 0.0, -1.0)
+    ts(B("rpos"), B("rr"), 0.0, OP.is_gt)
+    ts(B("BLKn"), B("cg"), B("rg"), OP.is_equal, B("rpos"), OP.mult)
+    ts(B("Gn"), c8, B("rg"), OP.is_equal, B("rpos"), OP.mult)
+    ts(B("TRf"), B("cr"), B("rr"), OP.is_ge)
+    tt(B("TRI"), B("TRf"), B("BLKf"), OP.mult)
+    ts(B("G205"), c8, B("rg"), OP.is_equal, 205.0, OP.mult)
+    ms(B("ONEh"), 1.0)
+    ts(B("r16"), B("rr"), 16.0, OP.mult)
+    ts(B("KT"), c8, 256.0, OP.mult, B("r16"), OP.add)
+    ts(B("n205"), B("i16"), 205.0, OP.mult)
+    ms(("SX0", 256, 257), 0.0)
+
+    after = {}
+
+    def send_log(v):
+        dst = T.cores[(rank - v) % n]
+        src = T.cores[(rank + v) % n]
+        a = send(dst, B("CF%d" % v), B("CF0"), "rca%d" % v, "lca%d" % v)
+        recv(B("CF%d" % v), src, "rca%d" % v, 4000, a)
+        for h, x in ((0, "a"), (1, "b")):
+            o = ("XL%d" % v, 2048 * h, 2048 * h + 2048)
+            a = send(dst, o, ("XL0", 2048 * h, 2048 * h + 2048), "rl%s%d" % (x, v), "ll%s%d" % (x, v))
+            recv(o, src, "rl%s%d" % (x, v), 9000 * (1 + h), a)
+
+    send_log(1)
+
+    for m in range(16):
+        x = ("SEL", 128 * m, 128 * m + 128)
+        op("G", [lambda x=x, m=m: g.affine_select(ap(x), ap(B("BLKb")), [[0, 8], [1, 16]], OP.is_equal, 0.0, -m, 0)],
+           [B("BLKb")], [x], 430)
+
+    def lists(t, c, zm, zv, mmc, col, lreg, starts=None):
+        K, P = "pK%d" % c, t % 2
+        i0 = c * NC
+        S, D, C = ("SROT%d" % P, i0, i0 + NC), ("D%d" % P, i0, i0 + NC), ("CH%d" % P, i0, i0 + NC)
+        M, X, XS, CS, LI, LJ, OFF = [B("%s_%d" % (x, c)) for x in ("MASK", "X", "XS", "CS", "LI", "LJ", "OFF")]
+        UZ, OH = ("pT%d" % c, 384, 512), ("pT%d" % c, 256, 384)
+        tt(M, S, (K, zm, zm + NC), OP.is_le)
+        if starts is None:
+            tt(UZ, (K, zv, zv + NC), S, OP.subtract)
+            mm((K, 384, 512), [(B("BLKb"), M)])
+        else:
+            mm((K, 384, 512), [(B("BLKb"), M)])
+            starts()
+            tt(UZ, (K, zv, zv + NC), S, OP.subtract)
+        tt(X, UZ, D, OP.mult)
+        ts(OH, (K, 384, 512), 1.0, OP.max, B("rp1"), OP.is_equal)
+        tt(XS, OH, X, OP.mult)
+        tt(CS, OH, C, OP.mult)
+        mm((K, lreg, lreg + NC), [(B("BLKf"), XS), (B(mmc), CS)])
+        ts(LI, (K, lreg, lreg + NC), B(col), OP.add)
+        ts(LJ, LI, W - 1, AND)
+        cp(OFF, LJ)
+
+    def pick(t, c, dst, parts):
+        a = 0
+        for q, k in parts:
+            gather(q, (dst, 16 * a, 16 * (a + k)), B("XL%d" % t), ("OFF_%d" % c, a, a + k))
+            a += k
+
+    for t in range(NV):
+        P = t % 2
+        last = t == NV - 1
+        for c in range(2):
+            E = "pE%d" % c
+            tag[0] = "L%d" % c
+            zs = (E, 128, 136)
+            ts(B("ZL_%d" % c), zs, -16.0, OP.add, -float(ZC), OP.max)
+            tt(B("DZ_%d" % c), zs, B("ZL_%d" % c), OP.subtract)
+            lists(t, c, 0, 0, "MMC1", "rm8", 256)
+        for c in range(2):
+            tag[0] = "Y%d" % c
+            mm(("pT%d" % c, 0, 256), [(B("IDb"), ("TT", 256 * c, 256 * c + 256))])
+            pick(t, c, "Y_%d" % c, YSPLIT[c])
+        for c in range(2):
+            i0 = c * NC
+            E, Y = "pE%d" % c, "Y_%d" % c
+            er = (E, 0, 128)
+            tag[0] = "M%d" % c
+            mm(er, [(("TT", 256 * c, 256 * c + NC), B("BM%d" % c)), (("ONE", 0, 128, "p", 1), ("CROW", 0, 128, "p", 1))], True, False)
+            for j in range(15 - JA[c]):
+                for a in range(2):
+                    s = (2 * j + a) * NC
+                    tt(("MX_%d" % c, s, s + NC), ("pT%d" % c, 128 * a, 128 * a + 128), (Y, j + a, 16 * NC, 16), OP.max)
+                    mm((E, j, 128, 16), [(("MX_%d" % c, s, s + NC), B("G32")), ((Y, j + a, 16 * NC, 16), B("GM16"))], False, False, er)
+            for b in range(0, JA[c], 2):
+                sl = [(j, a) for j in range(15 - JA[c] + b, min(15, 15 - JA[c] + b + 2)) for a in range(2)]
+                pv = "p%s%d" % ("VK"[b // 2 % 2], c)
+                tag[0] = "A%d" % c
+                for k, (j, a) in enumerate(sl):
+                    mm((pv, NC * k, NC * k + NC), [(B("IDb"), (Y, j + a, 16 * NC, 16)), (B("IDn"), ("TT", 256 * c + NC * a, 256 * c + NC * a + NC))])
+                w, x = NC * len(sl), 2 * b * NC
+                op("A", [lambda c=c, pv=pv, w=w, x=x: g.scalar.activation(T["AX_%d" % c][:, x:x + w], T[pv][:, 0:w], AF.Abs)],
+                   [(pv, 0, w)], [("AX_%d" % c, x, x + w)], w)
+                for k, (j, a) in enumerate(sl):
+                    mm((E, j, 128, 16), [(("AX_%d" % c, x + NC * k, x + NC * k + NC), B("G16"))], False, False, er)
+            tag[0] = "C%d" % c
+            mm(er, [(("TT", 256 * c + NC, 256 * c + 2 * NC), B("BM%d" % c))], False, True)
+            SC, KI, JJ, SM = [B("%s_%d" % (x, c)) for x in ("SC", "KI", "JJ", "SM")]
+            op("V", [lambda c=c, E=E: g.vector.tensor_tensor_scan(T["SC_%d" % c][:, :], T.RST[:, :], T[E][:, 0:128], 1.0e9, OP.max, OP.min)],
+               [er, B("RST")], [SC], 128)
+            key = ("SC_%d" % c, 15, 128, 16)
+            tie = ("SM_%d" % c, 16, 24)
+            cp(KI, key)
+            ts(tie, key, float(16 * TH), OP.is_lt)
+            ts(JJ, KI, 15, AND)
+            tt(B("TD_%d" % c), tie, B("DZ_%d" % c), OP.mult)
+            tt(("SM_%d" % c, 8, 16), JJ, tie, OP.mult)
+            tt(("SM_%d" % c, 0, 8), B("TD_%d" % c), B("ZL_%d" % c), OP.add)
+            mm((E, 128, 256, "p", 24), [(SM, B("IDh"))])
+            cp(("ST_%d" % c, 0, NC), (E, 128, 256, "p", 24))
+            K = "pK%d" % c
+            st = B("ST_%d" % c)
+            for r, x in ((0, "EXz"), (128, "EXzn"), (256, "EXn")):
+                mm((K, r, r + 128), [((x, 0, 128, "p", 24), st)])
+            tag[0] = "R%d" % c
+
+            def starts():
+                tag[0] = "S%d" % c
+                ts(B("GE_%d" % c), (K, 384, 512), B("rp1"), OP.is_le)
+                gd = (E, 256, 384)
+                tt(gd, B("GE_%d" % c), (K, 256, 384), OP.mult)
+                tt(("SX%d" % t, i0, i0 + NC), ("SROT%d" % P, i0, i0 + NC), gd, OP.subtract)
+                tag[0] = "Q%d" % c
+            lists(t, c, 0, 128, "MMC2", "rr", 0, starts)
+        for c in CORD:
+            tag[0] = "S%d" % c
+            lo, hi = c * NC, 257 if c else NC
+            s = send(T.cores[(rank - 1) % n], ("SR%d" % (t + 1), lo, hi), ("SX%d" % t, lo, hi), "rs%d%d" % (t + 1, c), "ls%d%d" % (t + 1, c))
+            recv(("SR%d" % (t + 1), lo, hi), T.cores[(rank + 1) % n], "rs%d%d" % (t + 1, c), RECV, s)
+        if t < 2:
+            send_log(t + 2)
+        if not last:
+            tag[0] = "P"
+            an = ("pE1", 160, 168)
+            mm(an, [(B("ONEh"), ("SM_0", 16, 24)), (B("ONEh"), ("SM_1", 16, 24))])
+            tt(B("AP8"), an, B("G205"), OP.mult)
+            acol = ("SX%d" % (t + 1), 256, 257)
+            op("V", [lambda acol=acol: g.vector.tensor_reduce(ap(acol), T.AP8[:, :], AxisListType.X, OP.add)], [B("AP8")], [acol], 64)
+            ts(B("LA"), B("i16"), acol, OP.add, 5.0, OP.mult)
+            ts(B("LB"), B("LA"), 255, AND)
+            cp(B("LO"), B("LB"))
+            prep_c(t + 1, "A")
+            tt(B("dA"), acol, ("SR%d" % (t + 1), 256, 257), OP.subtract)
+            ts(B("LC"), B("i16"), B("dA"), OP.add)
+            ts(B("LD"), B("LC"), 255, AND)
+            cp(B("LS"), B("LD"))
+            gather(DQ, B("SROT%d" % ((t + 1) % 2)), ("SR%d" % (t + 1), 0, 256), B("LS"))
+        for c in range(2):
+            tag[0] = "V%d" % c
+            pick(t, c, "V_%d" % c, VSPLIT[c])
+        for c in range(2):
+            i0 = c * NC
+            E, K, V, AB, st = "pE%d" % c, "pK%d" % c, "V_%d" % c, "AB_%d" % c, B("ST_%d" % c)
+            for b in range(4):
+                a = 512 * b
+                tag[0] = "D%d" % c
+                vd = ("p%s%d" % ("VT"[b % 2], c), 1, 512)
+                mm(vd, [(B("IDb"), (V, a + 1, a + 512)), (B("IDn"), (V, a, a + 511))])
+                op("A", [lambda AB=AB, a=a, vd=vd: g.scalar.activation(T[AB][:, a + 1:a + 512], ap(vd), AF.Abs)],
+                   [vd], [(AB, a + 1, a + 512)], 512)
+                if b % 2:
+                    mm((E, 224 + 32 * b, 288 + 32 * b), [(("SEL", 128 * m, 128 * m + 128), (AB, 512 * b - 512 + m, 512 * b + 512, 16)) for m in range(2, 16)])
+            tag[0] = "N%d" % c
+            OV, IZ = B("OV_%d" % c), B("IZ_%d" % c)
+            ts(OV, (E, 256, 384), float(TH2), OP.is_gt)
+            mm((E, 384, 512), [(B("TRI"), OV)])
+            ts(IZ, (E, 384, 512), 0.0, OP.is_equal)
+            if last:
+                mm((K, 0, NC, "p", 8), [(("EXs", 0, 8, "p", 24), st), (B("Gn"), IZ)])
+            else:
+                mm((K, 0, NC), [(("EXz", 0, 128, "p", 24), st), (B("BLKn"), IZ)])
+            mm((E, 144, 152), [(("SEL", 128 * p, 128 * p + 128), ("IZ_%d" % c, p, NC, 16)) for p in range(16)] + [(B("IDb"), B("KT"))])
+            if not last:
+                mm((E, 128, 136), [(st, ("EXs", 0, 8, "p", 24)), (IZ, B("Gn"))])
+            for a in range(2):
+                ts(("TO_%d" % c, 8 * a, 8 * a + 8), (E, 144, 152), float(a - 2), OP.add)
+            gather(TQ[c], ("TT", 256 * c, 256 * c + 256), B(V), B("TO_%d" % c))
+            if last:
+                ts(("YZ", i0, i0 + NC), (K, 0, NC, "p", 8), float(ZC), OP.add)
+                for a in range(2):
+                    x = ("TT", 256 * c + NC * a, 256 * c + NC * a + NC)
+                    dma("SA"[a], T.yt[:, 256 * a + i0:256 * a + i0 + NC], ap(x), [x], [], "d_y%s%d" % ("ab"[a], c), 2500)
+    dma("S", T.yz[:, :], T.YZ[:, :], [B("YZ")], [], "d_yz", 2000)
+    ts(B("LC"), B("n205"), ("SR4", 256, 257), OP.subtract)
+    ts(B("LD"), B("LC"), 255, AND)
+    cp(B("LS"), B("LD"))
+    gather("V", B("YSO"), ("SR4", 0, 256), B("LS"), 1.0, float(ZC))
+    dma("S", T.ys[:, :], T.YSO[:, :], [B("YSO")], [], "d_ys", 2500)
+    return ops
+
+
+def link(ops):
+    hist = {}
+    for k, o in enumerate(ops):
+        deps = {}
+
+        def add(x, hard):
+            deps[x] = deps.get(x, False) or hard
+        if "after" in o:
+            add(o["after"], False)
+        acc = [(r, False) for r in o["r"]] + [(w, True) for w in o["w"]]
+        for (b, lo, hi), wr in acc:
+            ps = SCRATCH[b][0] == "psum"
+            for (x, l2, h2, w2) in hist.get(b, ()):
+                if x == k:
+                    continue
+                same = ops[x]["q"] == o["q"]
+                if ps and (not same):
+                    add(x, True)
+                elif ps and o["q"] == "P":
+                    add(x, False)
+                elif (wr or w2) and lo < h2 and l2 < hi:
+                    add(x, True)
+        for (b, lo, hi), wr in acc:
+            h = hist.setdefault(b, [])
+            ps = SCRATCH[b][0] == "psum"
+            if wr and not ps:
+                h[:] = [y for y in h if not (lo <= y[1] and y[2] <= hi and y[0] != k)]
+            if ps:
+                h[:] = [y for y in h if ops[y[0]]["q"] != o["q"] or y[0] == k or (o["q"] != "P" and not (wr and lo <= y[1] and y[2] <= hi))] if o["q"] == "P" or wr else h
+            h.append((k, lo, hi, wr))
+        o["deps"] = deps
+
+
+def order(ops):
+    n = len(ops)
+    succ = [[] for _ in range(n)]
+    need = [0] * n
+    for k, o in enumerate(ops):
+        for x in o["deps"]:
+            succ[x].append(k)
+            need[k] += 1
+    way = [0.0] * n
+    for k in range(n - 1, -1, -1):
+        way[k] = ops[k]["cost"] + SYNCNS + max([way[s] for s in succ[k]] + [0.0])
+    for k, o in enumerate(ops):
+        way[k] += BI.get(o["tag"], 0)
+    prev = {}
+    for k, o in enumerate(ops):
+        if o["kind"] in ("dma", "send") or o["q"] == "G":
+            if o["q"] in prev:
+                succ[prev[o["q"]]].append(k)
+                need[k] += 1
+            prev[o["q"]] = k
+    ready_at = [0.0] * n
+    ready = {}
+    free = {}
+    seq = []
+
+    def push(k):
+        ready.setdefault(ops[k]["q"], []).append(k)
+    for k in range(n):
+        if need[k] == 0:
+            push(k)
+    while any(ready.values()):
+        best = None
+        for q, l in ready.items():
+            if not l:
+                continue
+            f = free.get(q, 0.0) if q != "R" else 0.0
+            t0 = max(f, min(ready_at[k] for k in l))
+            k = min((k for k in l if ready_at[k] <= t0 + 1e-6), key=lambda k: (-way[k], k))
+            if best is None or t0 < best[0]:
+                best = (t0, q, k)
+        t0, q, k = best
+        ready[q].remove(k)
+        o = ops[k]
+        busy = {"dma": 60.0, "recv": 0.0, "send": o["cost"]}.get(o["kind"], o["cost"])
+        free[q] = t0 + busy
+        o["t0"] = t0
+        end = t0 + o["cost"] + SYNCNS
+        seq.append(k)
+        for s in succ[k]:
+            e = t0 + busy if (k not in ops[s]["deps"] or ops[s]["q"] == q and not ops[s]["deps"][k]) else end
+            ready_at[s] = max(ready_at[s], e)
+            need[s] -= 1
+            if need[s] == 0:
+                push(s)
+    return seq
+
+
+def emit(g, T, ops, seq):
+    queue = {"V": g.vector, "A": g.scalar, "P": g.tensor, "G": g, "S": g.sync}
+    total = {"V": 0, "A": 0, "P": 0, "G": 0}
+    know = {q: {} for q in queue}
+    waited = {}
+    issued = []
+    for k in seq:
+        o = ops[k]
+        q = o["q"]
+        if o["kind"] == "recv":
+            o["done"] = (o["sem"], o["cnt"])
+            o["clock"] = {}
+            issued.append(o["done"])
+            continue
+        eng = queue[q]
+        for x in sorted(o["deps"], reverse=True):
+            if not o["deps"][x]:
+                continue
+            d = ops[x]
+            s, v = d["done"]
+            if know[q].get(s, 0) >= v:
+                continue
+            eng.wait_ge(T.sem[s], v)
+            waited[s] = max(waited.get(s, 0), v)
+            know[q][s] = v
+            for s2, v2 in d["clock"].items():
+                if know[q].get(s2, 0) < v2:
+                    know[q][s2] = v2
+        if o["kind"] == "c":
+            for f in o["fns"]:
+                f().then_inc(T.sem["s" + q], 1)
+            total[q] += len(o["fns"])
+            o["done"] = ("s" + q, total[q])
+        elif o["kind"] == "dma":
+            for f in o["fns"]:
+                f().then_inc(T.sem[o["sem"]], 16)
+            o["done"] = (o["sem"], 16)
+        else:
+            for f in o["fns"]:
+                f()
+            o["done"] = (o["sem"], o["cnt"])
+        o["clock"] = dict(know[q])
+        if o["kind"] != "c":
+            issued.append(o["done"])
+    for q in total:
+        if total[q]:
+            issued.append(("s" + q, total[q]))
+    for s, v in issued:
+        if know["G"].get(s, 0) < v:
+            g.wait_ge(T.sem[s], v)
+
+
+def rank_program(g, core, T, topo):
+    if T.rank_of(core) is None:
+        return
+    ops = plan(g, core, T, topo)
+    link(ops)
+    emit(g, T, ops, order(ops))

@@ -1,3 +1,4 @@
+import math
 import numpy as np
 import comms_topo
 from concourse.bass import DstId, RemoteDMATransfer
@@ -7,17 +8,20 @@ OP = AluOpType
 AF = ActivationFunctionType
 NV, W, ZC, TH, TH2 = 4, 4096, 1536, 1082, 820
 NC = 128
-SYNCNS = 100
-PE_NS = 0.5
-JA = (8, 4)
-YSPLIT = [[("V", 64), ("A", 64)], [("A", 128)]]
-VSPLIT = [[("V", 32), ("A", 32), ("V", 32), ("A", 32)]] * 2
-TQ = ("V", "A")
-DQ = "V"
-BI = {'M0': -19957, 'S0': 8812, 'Q0': 8916, 'A0': -13949, 'V1': -3468, 'M1': -4459, 'C0': -1044, 'N0': 789, 'D1': -6115, 'V0': -5027, 'C1': -327, 'R0': -3667, 'L1': -1914, 'D0': 5816, 'P': 922, 'A1': 9610, 'R1': 6757, 'Y1': 901}
-CORD = (1, 0)
-RECV = 2500
-GN = 1.56
+WX = W
+SW = 16 + 256
+R16 = 1.5 * 2 ** 27
+R1 = 1.5 * 2 ** 23
+CAP = 32 * (TH - 1) + 32
+PAR = dict(
+    SYNC=100, PE=0.5, GN=1.56, RECV=2500, SEND=1000,
+    YS=["AAAA", "AAAA"],
+    VS=["AAAA", "AAAA"],
+    TQ="AA",
+    FILL=["VVVVVVVVVVGGGGGG", "VVVVVVVVVVGGGGGG"],
+    BI={},
+)
+PAR.update({'YS': ['AAAV', 'AAVA'], 'VS': ['AAAA', 'AVAA'], 'TQ': 'AA', 'FILL': ['VVVVVVVVVAAAAGGG', 'VVVVVVVAAAAGGGGG'], 'BI': {'N1': -6577, 'P': 10849, 'C0': -18109, 'Y0': 29548, 'Q0': 35775, 'L0': 13704, 'B1': 36812, 'Z': 24811, 'Y1': -3215, 'M0': -37336, 'L1': -10511, 'V0': 72407, 'V1': 3110, 'Q1': 34840, 'F1': -67990, 'D1': -9648, 'B0': -34734, 'C1': -90901, 'c': -20085, 'X': 44139, 'F0': -56967, 'S0': -49337, 'E1': -42699, 'S1': 26460, 'T0': 3205, 'M1': -40204, 'D0': -15280, 'N0': 48304, 'E0': -62395, 'T1': -16593}})
 
 SCRATCH = {}
 
@@ -27,53 +31,42 @@ def _b(name, cols, dtype, where="sbuf", rows=128):
 
 
 for _v in range(4):
-    _b("XL%d" % _v, W, "bfloat16")
-    _b("CF%d" % _v, 256, "float32")
-    _b("SX%d" % _v, 257, "float32")
-    _b("SR%d" % (_v + 1), 257, "float32")
-for _n, _c, _d in (("CFI", 256, "int32"), ("S0I", 256, "int32"), ("TT", 512, "bfloat16"), ("YSO", 256, "float32"),
-                   ("SROT0", 256, "float32"), ("SROT1", 256, "float32"), ("D0", 256, "float32"), ("D1", 256, "float32"),
-                   ("CH0", 256, "float16"), ("CH1", 256, "float16"),
-                   ("BLKf", 128, "float32"), ("SEL", 2048, "bfloat16"), ("IDh", 128, "float16"),
-                   ("MMC1", 128, "float16"), ("MMC2", 128, "float16"),
-                   ("G32", 8, "bfloat16"), ("GM16", 8, "bfloat16"), ("G16", 8, "bfloat16"), ("Gn", 8, "bfloat16"), ("G205", 8, "float32"),
-                   ("RST", 128, "float32"), ("ONE", 128, "bfloat16"), ("ONEh", 128, "float16"), ("CROW", 128, "bfloat16"),
-                   ("KT", 8, "bfloat16"),
-                   ("EXz", 128, "float16"), ("EXn", 128, "float16"), ("EXzn", 128, "float16"), ("EXs", 8, "float16"),
-                   ("AP8", 8, "float32"), ("LO", 16, "uint16"), ("LS", 16, "uint16")):
+    _b("XL%d" % _v, WX, "bfloat16")
+    _b("CF%d" % _v, 256, "int32")
+    _b("SX%d" % _v, SW, "float32")
+    _b("SR%d" % (_v + 1), SW, "float32")
+for _n, _c, _d in (("S0I", 256, "int32"), ("TL", 512, "bfloat16"), ("TT", 512, "bfloat16"), ("YSO", 256, "float32"),
+                   ("SROT0", 256, "float32"), ("SROT1", 256, "float32"), ("D0", 256, "float16"), ("D1", 256, "float16"),
+                   ("SEL", 144, "bfloat16"), ("WN", 144, "bfloat16"), ("NCT", 48, "float32"), ("LI", 32, "int32"), ("LJ", 32, "int32"),
+                   ("LOS", 32, "uint16"), ("KT", 8, "bfloat16")):
     _b(_n, _c, _d)
 VIRT = {}
-for _p, _c, _d, _l in (("PF", 1, "float32", "rg rr r7 q3 rp1 rm8 rpos wz wn wm wzn r16 dA"), ("PI", 1, "int32", "rowI rgI rrI r7I q3I"),
-                       ("PJ", 16, "int32", "c16 i16 n205 o5a o5b LA LB LC LD"), ("PG", 128, "float32", "cg cr colF TRf MA MB RS0 CRW2"),
-                       ("PB", 128, "bfloat16", "BLKb BLKn BM0 BM1 TRI IDb IDn")):
+for _p, _c, _d, _l in (("PF", 1, "float32", "rg rr pp rp1 ra rb c17"), ("PI", 1, "int32", "rowI rrI"),
+                       ("PJ", 16, "int32", "c16"), ("PG", 128, "float32", "colF IDn32 BLKs RST EXa EXb EXbn i16"),
+                       ("PB", 128, "bfloat16", "cg cr B64 BM TRI IDb ONE CROW"),
+                       ("PH", 128, "float16", "IDh EXzj EXz EXj EXj64 W1 W9 W0 WM")):
     for _k, _n in enumerate(_l.split()):
         VIRT[_n] = (_p, _k * _c, _c)
     _b(_p, _c * len(_l.split()), _d)
 _b("Z8I", 256, "int32", rows=8)
-_b("Z8", 256, "float16", rows=8)
 _b("YZ", 256, "float32", rows=8)
 for _k in range(2):
-    for _n, _c, _d in (("MASK", NC, "bfloat16"), ("X", NC, "float32"), ("XS", NC, "float32"), ("CS", NC, "float16"),
-                       ("LI", NC, "int32"), ("LJ", NC, "int32"), ("OFF", NC, "uint16"), ("Y", 16 * NC, "bfloat16"),
-                       ("V", 16 * NC, "bfloat16"), ("MX", 30 * NC, "bfloat16"), ("AX", max(1, 2 * max(JA)) * NC, "bfloat16"), ("SC", 128, "float32"), ("KI", 8, "int32"),
-                       ("JJ", 8, "int32"), ("DZ", 8, "float32"), ("ZL", 8, "float32"), ("TD", 8, "float32"),
-                       ("SM", 24, "float16"), ("GE", NC, "float32"), ("AB", 16 * NC, "bfloat16"),
+    for _n, _c, _d in (("MASK", NC, "bfloat16"), ("OHL", NC, "float16"), ("OHQ", NC, "float16"), ("DS", NC, "float16"), ("XS", NC, "float32"),
+                       ("FI", NC, "int32"), ("FJ", NC, "int32"), ("OFL", NC, "uint16"), ("OFQ", NC, "uint16"), ("Z", 32 * NC, "bfloat16"),
+                       ("MX", 32 * NC, "bfloat16"), ("V", 16 * NC, "bfloat16"), ("MV", 16 * NC, "bfloat16"), ("SC", 128, "float32"),
+                       ("RR", 8, "float32"), ("SM", 16, "bfloat16"), ("OHJ", NC, "bfloat16"),
                        ("OV", NC, "bfloat16"), ("IZ", NC, "bfloat16"), ("TO", 16, "uint16")):
         _b("%s_%d" % (_n, _k), _c, _d)
-    _b("ST_%d" % _k, NC, "float16", rows=24)
-    for _n in ("K", "T", "E", "V"):
+    _b("ST_%d" % _k, NC, "float16", rows=16)
+    for _n in ("U", "K", "E", "F"):
         _b("p%s%d" % (_n, _k), 512, "float32", where="psum")
 
 SEMAPHORES = ["sV", "sA", "sP", "sG"]
-SEMAPHORES += ["d_" + n for n in ("s0", "cf", "z0", "t00", "t01", "t10", "t11", "xa", "xb", "ys", "yz", "ya0", "ya1", "yb0", "yb1")]
+SEMAPHORES += ["d_" + n for n in ("s0", "cf", "z0", "t0", "xa", "xb", "ys", "yz", "ya0", "ya1", "yb0", "yb1")]
 for _v in range(1, 4):
     SEMAPHORES += ["%s%d" % (n, _v) for n in ("rca", "rla", "rlb", "lca", "lla", "llb")]
 for _v in range(1, 5):
     SEMAPHORES += ["%s%d%d" % (n, _v, c) for n in ("rs", "ls") for c in range(2)]
-
-
-class _Plan(dict):
-    pass
 
 
 def plan(g, core, T, topo):
@@ -82,57 +75,60 @@ def plan(g, core, T, topo):
     ops = []
     tag = ["c"]
 
-    def B(name):
-        if name in VIRT:
-            p, lo, c = VIRT[name]
-            return (p, lo, lo + c)
-        return (name, 0, SCRATCH[name][1][1])
+    def B(name, lo=0, hi=None, step=1, rows=128):
+        p, o, c = VIRT[name] if name in VIRT else (name, 0, SCRATCH[name][1][1])
+        return (p, o + lo, o + (c if hi is None else hi), step, min(rows, SCRATCH[p][1][0]))
 
-    def op(q, fns, reads, writes, cost, kind="c", sem=None, cnt=0):
-        ops.append(dict(tag=tag[0], q=q, fns=fns, r=reads, w=writes, cost=cost, kind=kind, sem=sem, cnt=cnt))
+    def op(q, fns, reads, writes, cost, kind="c", sem=None, cnt=0, cls=None):
+        ops.append(dict(tag=tag[0], q=q, fns=fns, r=reads, w=writes, cost=cost, kind=kind, sem=sem, cnt=cnt, cls=cls or q))
         return len(ops) - 1
 
     def ap(x):
-        if len(x) == 3:
-            return T[x[0]][:, x[1]:x[2]]
-        if x[3] == "p":
+        if x[3] == 1:
             return T[x[0]][0:x[4], x[1]:x[2]]
-        return T[x[0]][:, x[1]:x[2]:x[3]]
+        return T[x[0]][0:x[4], x[1]:x[2]:x[3]]
 
     def width(x):
-        if len(x) > 3 and x[3] != "p":
-            return -(-(x[2] - x[1]) // x[3])
-        return x[2] - x[1]
+        return -(-(x[2] - x[1]) // x[3])
 
     def psum(x):
         return SCRATCH[x[0]][0] == "psum"
 
-    def reg(x):
-        return (x[0], x[1], x[2])
+    def cyc(*xs):
+        two = all(SCRATCH[x[0]][2] in ("bfloat16", "float16", "uint16") for x in xs)
+        return max(64, width(xs[0]) * (0.5 if two else 1))
 
     def tt(o, a, b, alu):
         c = width(o) * (1 if psum(a) or psum(b) else 2)
-        op("V", [lambda: g.vector.tensor_tensor(ap(o), ap(a), ap(b), alu)], [reg(a), reg(b)], [reg(o)], max(64, c))
+        op("V", [lambda: g.vector.tensor_tensor(ap(o), ap(a), ap(b), alu)], [a, b], [o], max(64, c))
 
     def sc(x):
-        return ap(x) if isinstance(x, tuple) else x
+        return T[x[0]][0:x[4], x[1]:x[2]] if isinstance(x, tuple) else x
 
     def ts(o, a, s1, op0, s2=None, op1=None):
-        rd = [reg(a)] + [reg(s) for s in (s1, s2) if isinstance(s, tuple)]
+        s1, s2 = [s[:4] + (o[4],) if isinstance(s, tuple) else s for s in (s1, s2)]
+        rd = [a] + [s for s in (s1, s2) if isinstance(s, tuple)]
         if op1 is None:
             f = [lambda: g.vector.tensor_scalar(ap(o), ap(a), sc(s1), None, op0)]
         else:
             f = [lambda: g.vector.tensor_scalar(ap(o), ap(a), sc(s1), sc(s2), op0, op1)]
-        op("V", f, rd, [reg(o)], max(64, width(o)))
+        op("V", f, rd, [o], cyc(o, a))
 
-    def cp(o, a):
-        op("V", [lambda: g.vector.tensor_copy(ap(o), ap(a))], [reg(a)], [reg(o)], max(64, width(o)))
+    def cp(o, a, q="V"):
+        if q == "V":
+            op("V", [lambda: g.vector.tensor_copy(ap(o), ap(a))], [a], [o], cyc(o, a))
+        elif q == "A":
+            op("A", [lambda: g.scalar.activation(ap(o), ap(a), AF.Copy)], [a], [o], max(64, width(o)))
+        else:
+            select(o, a, [[0, width(o)]], OP.is_ge, 0, 0)
 
     def ms(o, val):
-        op("V", [lambda: g.vector.memset(ap(o), val)], [], [reg(o)], max(64, width(o)))
+        op("V", [lambda: g.vector.memset(ap(o), val)], [], [o], cyc(o))
+
+    def scan(o, a, b, init, op0, op1):
+        op("V", [lambda: g.vector.tensor_tensor_scan(ap(o), ap(a), ap(b), init, op0, op1)], [a, b], [o], cyc(o, a, b))
 
     def gather(q, o, win, off, scale=1.0, bias=0.0):
-        cost = 60 + GN * width(o)
         if q == "V":
             f = lambda: g.vector.tensor_copy(ap(o), ap(win).indirect(ap(off)))
             if scale != 1.0 or bias != 0.0:
@@ -141,15 +137,16 @@ def plan(g, core, T, topo):
             f = lambda: g.scalar.activation(ap(o), ap(win).indirect(ap(off)), AF.Copy)
             if scale != 1.0 or bias != 0.0:
                 f = lambda: g.scalar.activation(ap(o), ap(win).indirect(ap(off)), AF.Identity, bias=bias, scale=scale)
-        op(q, [f], [reg(win), reg(off)], [reg(o)], cost)
+        op(q, [f], [win, off], [o], 60 + PAR["GN"] * width(o), cls="gather")
 
-    def mm(o, pairs, start=True, stop=True, wreg=None):
-        fns, rd, cost = [], [], 0
-        for k, (l, r) in enumerate(pairs):
-            fns.append(lambda l=l, r=r, k=k: g.tensor.matmul(ap(o), ap(l), ap(r), start and k == 0, stop and k == len(pairs) - 1))
-            rd += [reg(l), reg(r)]
-            cost += max(min(64, width(l)), width(r)) * (4 if SCRATCH[l[0]][2] == "float32" else 1) * PE_NS
-        op("P", fns, rd, [wreg or reg(o)], cost)
+    def mm(items, start=True, stop=True):
+        fns, rd, wr, cost = [], [], [], 0
+        for k, (o, l, r) in enumerate(items):
+            fns.append(lambda o=o, l=l, r=r, k=k: g.tensor.matmul(ap(o), ap(l), ap(r), start and k == 0, stop and k == len(items) - 1))
+            rd += [l, r]
+            wr.append(o)
+            cost += max(min(64, width(l)), width(r)) * (4 if SCRATCH[l[0]][2] == "float32" else 1) * PAR["PE"]
+        op("P", fns, rd, wr, cost)
 
     def dma(q, o, a, rd, wr, sem, cost):
         eng = g.sync if q == "S" else g.scalar
@@ -158,289 +155,254 @@ def plan(g, core, T, topo):
     def send(dst, out, src, rs, ls):
         rid, pid = topo.addr(dst, core)
         m = topo.mask(core, dst)
-        op("G", [lambda: g.remote_dma(ap(out), ap(src), T.sem[rs], T.sem[ls], pid, rid, m)], [reg(src)], [], 1000,
-           kind="send", sem=ls, cnt=len(topo.engines(core, dst)))
-        return len(ops) - 1
+        return op("G", [lambda: g.remote_dma(ap(out), ap(src), T.sem[rs], T.sem[ls], pid, rid, m)], [src], [], PAR["SEND"],
+                  kind="send", sem=ls, cnt=len(topo.engines(core, dst)))
 
     def recv(o, src, rs, cost, after):
-        op("R", [], [], [reg(o)], cost, kind="recv", sem=rs, cnt=len(topo.engines(src, core)))
+        op("R", [], [], [o], cost, kind="recv", sem=rs, cnt=len(topo.engines(src, core)))
         ops[-1]["after"] = after
 
-    dma("S", ap(B("S0I")), T.s0[:, :], [], [B("S0I")], "d_s0", 2500)
-    dma("A", ap(B("CFI")), T.cf[:, :], [], [B("CFI")], "d_cf", 2500)
-    dma("A", T.Z8I[:, :], T.z0[:, :], [], [B("Z8I")], "d_z0", 2500)
-    dma("S", T.XL0[:, 0:2048], T.xl[:, 0:2048], [], [("XL0", 0, 2048)], "d_xa", 5500)
-    dma("S", T.XL0[:, 2048:4096], T.xl[:, 2048:4096], [], [("XL0", 2048, 4096)], "d_xb", 7500)
-    for c in range(2):
-        for a in range(2):
-            x = ("TT", 256 * c + NC * a, 256 * c + NC * a + NC)
-            dma("A", ap(x), T.t0[:, 256 * a + NC * c:256 * a + NC * c + NC], [], [x], "d_t%d%d" % (c, a), 3500)
     def iota(o, pat, base, cm):
         if SCRATCH[o[0]][2] == "int32":
             f = [lambda: g.iota(ap(o), pat, base, cm)]
         else:
             f = [lambda: g.iota(ap(o), pat, base, cm, allow_small_or_imprecise_dtypes=True)]
-        op("G", f, [], [reg(o)], 130 + 2 * width(o))
+        op("G", f, [], [o], 150 + 2 * width(o))
+
+    def select(o, a, pat, cmp, base, cm):
+        op("G", [lambda: g.affine_select(ap(o), ap(a), pat, cmp, 0.0, base, cm)], [a], [o], 190 + 2 * width(o))
 
     def act(o, a, bias, scale):
-        op("A", [lambda: g.scalar.activation(ap(o), ap(a), AF.Identity, bias=bias, scale=scale)], [reg(a)], [reg(o)], max(64, width(o)))
+        op("A", [lambda: g.scalar.activation(ap(o), ap(a), AF.Identity, bias=sc(bias), scale=scale)],
+           [a] + ([bias] if isinstance(bias, tuple) else []), [o], max(64, width(o)))
+
+    H = W // 2
+    dma("S", ap(B("S0I")), T.s0[:, :], [], [B("S0I")], "d_s0", 2500)
+    dma("A", ap(B("CF0")), T.cf[:, :], [], [B("CF0")], "d_cf", 2500)
+    dma("A", ap(B("Z8I")), T.z0[:, :], [], [B("Z8I")], "d_z0", 2500)
+    dma("S", ap(B("XL0", 0, H)), T.xl[:, 0:H], [], [B("XL0", 0, H)], "d_xa", 5500)
+    dma("S", ap(B("XL0", H, W)), T.xl[:, H:W], [], [B("XL0", H, W)], "d_xb", 7500)
+    dma("A", ap(B("TL")), T.t0[:, :], [], [B("TL")], "d_t0", 3500)
+    AND = OP.bitwise_and
     iota(B("rowI"), [[0, 1]], 0, 1)
     iota(B("c16"), [[16, 16]], 0, 0)
+    iota(B("pp"), [[0, 1]], 0, 1)
     iota(B("cg"), [[1, 8], [0, 16]], 0, 0)
-    iota(B("cr"), [[0, 8], [1, 16]], 0, 0)
     iota(B("colF"), [[1, 128]], 0, 0)
-    iota(B("wm"), [[0, 1]], 0, 1)
-    AND, SHR = OP.bitwise_and, OP.arith_shift_right
+    iota(B("cr"), [[0, 8], [1, 16]], 0, 0)
     ts(B("rrI"), B("rowI"), 15, AND)
     cp(B("rr"), B("rrI"))
-    ts(B("i16"), B("c16"), B("rr"), OP.add)
-    ts(B("o5a"), B("i16"), 5, OP.mult)
-    ts(B("o5b"), B("o5a"), 255, AND)
-    cp(B("LO"), B("o5b"))
-    ts(B("rgI"), B("rowI"), 4, SHR)
-    cp(B("rg"), B("rgI"))
-    ts(B("r7I"), B("rowI"), 7, AND)
-    cp(B("r7"), B("r7I"))
-    ts(B("q3I"), B("rowI"), 3, SHR)
-    cp(B("q3"), B("q3I"))
-    ts(B("wz"), B("q3"), 0.0, OP.is_equal)
-    ts(B("EXz"), B("cg"), B("r7"), OP.is_equal, B("wz"), OP.mult)
-    c8 = (B("colF")[0], B("colF")[1], B("colF")[1] + 8)
-    ts(B("EXs"), c8, B("r7"), OP.is_equal, B("wz"), OP.mult)
-    ts(B("BLKb"), B("cg"), B("rg"), OP.is_equal)
-    ts(B("rp1"), B("rr"), 1.0, OP.add)
-    ts(B("rm8"), B("rr"), -8.0, OP.add)
-    ts(("Z8", 0, 256), ("Z8I", 0, 256), -float(ZC), OP.add)
-    cp(B("CF0"), B("CFI"))
-    gather("V", B("SROT0"), B("S0I"), B("LO"), 1.0, -float(ZC))
-
-    def prep_c(v, q):
-        p = v % 2
-        gather(DQ, B("D%d" % p), B("CF%d" % v), B("LO"), 2.0, 1.0)
-        ts(B("CH%d" % p), B("D%d" % p), 0.5, OP.mult, -0.5, OP.add)
-    prep_c(0, "A")
+    ts(B("LI", 0, 16), B("c16"), B("rr"), OP.add, 5.0, OP.mult)
+    ts(B("LJ", 0, 16), B("LI", 0, 16), 255, AND)
+    cp(B("LOS", 0, 16), B("LJ", 0, 16))
+    ts(B("rg"), B("pp"), B("rr"), OP.subtract, 1.0 / 16, OP.mult)
+    ts(B("B64"), B("cg"), B("rg"), OP.is_equal, 64.0, OP.mult)
+    ts(B("IDn32"), B("colF"), B("pp"), OP.is_equal, -1.0, OP.mult)
+    ts(B("EXz"), B("cg"), B("pp"), OP.is_equal)
     for c in range(2):
-        mm(("pK%d" % c, 0, NC), [(("EXz", 0, 128, "p", 8), ("Z8", c * NC, c * NC + NC, "p", 8))])
-        mm(("pE%d" % c, 128, 136), [(("Z8", c * NC, c * NC + NC, "p", 8), ("EXs", 0, 8, "p", 8))])
-    ts(B("BLKf"), B("cg"), B("rg"), OP.is_equal)
-    act(B("MA"), B("cr"), 21.0, 2.0)
-    tt(B("MMC1"), B("MA"), B("BLKf"), OP.mult)
-    ts(B("IDb"), B("colF"), B("wm"), OP.is_equal)
-    for c in range(2):
-        ts(B("BM%d" % c), B("cr"), 14.5 - JA[c], OP.is_lt, -16.0, OP.mult)
-        tt(B("BM%d" % c), B("BM%d" % c), B("BLKb"), OP.mult)
+        ms(B("IZ_%d" % c), 1.0 / 64)
+        ts(B("ST_%d" % c, rows=8), B("Z8I", c * NC, c * NC + NC), -float(ZC + 15), OP.add)
+    gather("V", B("SROT0"), B("S0I"), B("LOS", 0, 16), 1.0, -float(ZC))
+    gather("V", B("D0"), B("CF0"), B("LOS", 0, 16), -2.0, -1.0)
+    act(B("rp1"), B("rr"), 64.0, 64.0)
+    act(B("WM"), B("cr"), -9.5 / 64, -1.0 / 64)
+    tt(B("W1"), B("WM"), B("B64"), OP.mult)
+    act(B("W0"), B("B64"), 0.0, -18.5 / 64)
+    act(B("BLKs"), B("B64"), 0.0, -1.0 / 64)
+    act(B("IDh", 0, 16), B("IDn32", 0, 16), 0.0, -1.0)
+    act(B("BM"), B("B64"), 0.0, -0.5)
+    act(B("IDb"), B("IDn32"), 0.0, -1.0)
+    act(B("W9"), B("B64"), 0.0, -9.0 / 64)
+    iota(B("CROW", rows=1), [[0, 8], [1, 16]], 9, 0)
     ms(B("ONE"), 1.0)
-    ts(B("CRW2"), B("cr"), 15.0, OP.is_equal, 524288.0 - 15.0, OP.mult)
-    tt(B("CROW"), B("CRW2"), B("cr"), OP.add)
-    ts(B("G32"), c8, B("rg"), OP.is_equal, 32.0, OP.mult)
-    act(B("G16"), B("G32"), 0.0, 0.5)
-    act(B("GM16"), B("G32"), 0.0, -0.5)
-    ts(B("RS0"), B("cr"), 0.0, OP.is_equal)
-    act(B("RST"), B("RS0"), -1.0e9, 2.0e9)
-    ts(B("IDh"), B("colF"), B("wm"), OP.is_equal)
-    ts(B("wn"), B("q3"), 1.0, OP.is_equal)
-    ts(B("wzn"), B("q3"), 2.0, OP.is_equal, -7.0, OP.mult)
-    tt(B("wn"), B("wn"), B("wzn"), OP.add)
-    tt(B("wzn"), B("wn"), B("wz"), OP.add)
-    ts(B("EXn"), B("cg"), B("r7"), OP.is_equal, B("wn"), OP.mult)
-    ts(B("EXzn"), B("cg"), B("r7"), OP.is_equal, B("wzn"), OP.mult)
-    act(B("MB"), B("cr"), 37.0, 2.0)
-    tt(B("MMC2"), B("MB"), B("BLKf"), OP.mult)
-    act(B("IDn"), B("IDb"), 0.0, -1.0)
-    ts(B("rpos"), B("rr"), 0.0, OP.is_gt)
-    ts(B("BLKn"), B("cg"), B("rg"), OP.is_equal, B("rpos"), OP.mult)
-    ts(B("Gn"), c8, B("rg"), OP.is_equal, B("rpos"), OP.mult)
-    ts(B("TRf"), B("cr"), B("rr"), OP.is_ge)
-    tt(B("TRI"), B("TRf"), B("BLKf"), OP.mult)
-    ts(B("G205"), c8, B("rg"), OP.is_equal, 205.0, OP.mult)
-    ms(B("ONEh"), 1.0)
-    ts(B("r16"), B("rr"), 16.0, OP.mult)
-    ts(B("KT"), c8, 256.0, OP.mult, B("r16"), OP.add)
-    ts(B("n205"), B("i16"), 205.0, OP.mult)
-    ms(("SX0", 256, 257), 0.0)
-
-    after = {}
+    ts(B("RST"), B("cr"), 0.0, OP.is_equal, float(CAP), OP.mult)
+    ts(B("c17"), B("pp"), 8.0, OP.is_lt, -17.0, OP.mult)
+    ts(B("EXj"), B("cg"), 8.0, OP.add, B("pp"), OP.is_equal)
+    act(B("EXj64"), B("EXj"), 0.0, 1.0 / 64)
+    tt(B("EXzj", rows=16), B("EXz", rows=16), B("EXj", rows=16), OP.add)
+    act(B("EXa"), B("EXz"), 0.0, 1.0 / 16)
+    act(B("EXb"), B("EXz"), 0.0, 205.0 / 16)
+    act(B("EXbn"), B("EXz"), 0.0, -205.0 / 16)
+    act(B("ra"), B("rr"), -2.0, 16.0)
+    act(B("rb"), B("rr"), -1.0, 16.0)
+    ts(B("i16", 0, 16), B("c16"), B("rr"), OP.add)
+    for k, f in enumerate((5.0, 1.0, 205.0)):
+        act(B("NCT", 16 * k, 16 * k + 16), B("i16", 0, 16), 0.0, -f)
+    for v in range(NV):
+        iota(B("SX%d" % v, 0, 16), [[0, 16]], 0, 0)
 
     def send_log(v):
         dst = T.cores[(rank - v) % n]
         src = T.cores[(rank + v) % n]
         a = send(dst, B("CF%d" % v), B("CF0"), "rca%d" % v, "lca%d" % v)
         recv(B("CF%d" % v), src, "rca%d" % v, 4000, a)
-        for h, x in ((0, "a"), (1, "b")):
-            o = ("XL%d" % v, 2048 * h, 2048 * h + 2048)
-            a = send(dst, o, ("XL0", 2048 * h, 2048 * h + 2048), "rl%s%d" % (x, v), "ll%s%d" % (x, v))
-            recv(o, src, "rl%s%d" % (x, v), 9000 * (1 + h), a)
+        for lo, hi, x in ((0, H, "a"), (H, WX, "b")):
+            a = send(dst, B("XL%d" % v, lo, hi), B("XL0", lo, hi), "rl%s%d" % (x, v), "ll%s%d" % (x, v))
+            recv(B("XL%d" % v, lo, hi), src, "rl%s%d" % (x, v), 9000 * (1 + lo // H), a)
 
     send_log(1)
+    select(B("TRI"), B("B64"), [[1, 128]], OP.is_ge, 0, -1)
+    for x, src, top in (("SEL", "B64", 0), ("WN", "BM", 1)):
+        iota(B(x, 0, 16), [[0, 16]], 0, 0)
+        select(B(x, 16, 144), B(src), [[0, 8], [-1, 16]], OP.is_ge, top, 0)
+    iota(B("KT", rows=1), [[256, 8]], 0, 0)
 
-    for m in range(16):
-        x = ("SEL", 128 * m, 128 * m + 128)
-        op("G", [lambda x=x, m=m: g.affine_select(ap(x), ap(B("BLKb")), [[0, 8], [1, 16]], OP.is_equal, 0.0, -m, 0)],
-           [B("BLKb")], [x], 430)
-
-    def lists(t, c, zm, zv, mmc, col, lreg, starts=None):
-        K, P = "pK%d" % c, t % 2
-        i0 = c * NC
-        S, D, C = ("SROT%d" % P, i0, i0 + NC), ("D%d" % P, i0, i0 + NC), ("CH%d" % P, i0, i0 + NC)
-        M, X, XS, CS, LI, LJ, OFF = [B("%s_%d" % (x, c)) for x in ("MASK", "X", "XS", "CS", "LI", "LJ", "OFF")]
-        UZ, OH = ("pT%d" % c, 384, 512), ("pT%d" % c, 256, 384)
-        tt(M, S, (K, zm, zm + NC), OP.is_le)
-        if starts is None:
-            tt(UZ, (K, zv, zv + NC), S, OP.subtract)
-            mm((K, 384, 512), [(B("BLKb"), M)])
+    def lists(t, c, u, zz, kreg, oh, ws, off, between=None):
+        D = B("D%d" % (t % 2), c * NC, c * NC + NC)
+        M, DS, XS, FI, FJ = [B("%s_%d" % (x, c)) for x in ("MASK", "DS", "XS", "FI", "FJ")]
+        cnt, f = B("pK%d" % c, kreg, kreg + NC), B("pF%d" % c, kreg, kreg + NC)
+        if zz is None:
+            ts(M, u, 1.0, OP.is_ge)
         else:
-            mm((K, 384, 512), [(B("BLKb"), M)])
-            starts()
-            tt(UZ, (K, zv, zv + NC), S, OP.subtract)
-        tt(X, UZ, D, OP.mult)
-        ts(OH, (K, 384, 512), 1.0, OP.max, B("rp1"), OP.is_equal)
-        tt(XS, OH, X, OP.mult)
-        tt(CS, OH, C, OP.mult)
-        mm((K, lreg, lreg + NC), [(B("BLKf"), XS), (B(mmc), CS)])
-        ts(LI, (K, lreg, lreg + NC), B(col), OP.add)
-        ts(LJ, LI, W - 1, AND)
-        cp(OFF, LJ)
-
-    def pick(t, c, dst, parts):
-        a = 0
-        for q, k in parts:
-            gather(q, (dst, 16 * a, 16 * (a + k)), B("XL%d" % t), ("OFF_%d" % c, a, a + k))
-            a += k
+            tt(M, B("SROT%d" % (t % 2), c * NC, c * NC + NC), zz, OP.is_le)
+        mm([(cnt, B("B64"), M)])
+        if between:
+            between()
+        ts(oh, cnt, 64.0, OP.max, B("rp1"), OP.is_equal)
+        scan(DS, oh, D, 0.0, OP.max, OP.mult)
+        tt(XS, u, DS, OP.mult)
+        mm([(f, B(x), DS) for x in ws] + [(f, B("W0"), oh)], True, False)
+        mm([(f, B("BLKs"), XS)], False, True)
+        cp(FI, f)
+        ts(FJ, FI, W - 1, AND)
+        cp(off, FJ)
 
     for t in range(NV):
         P = t % 2
         last = t == NV - 1
+
+        def tm(c, a):
+            return B("TL", 256 * a + NC * c, 256 * a + NC * c + NC) if t == 0 else B("TT", 256 * c + NC * a, 256 * c + NC * a + NC)
         for c in range(2):
-            E = "pE%d" % c
             tag[0] = "L%d" % c
-            zs = (E, 128, 136)
-            ts(B("ZL_%d" % c), zs, -16.0, OP.add, -float(ZC), OP.max)
-            tt(B("DZ_%d" % c), zs, B("ZL_%d" % c), OP.subtract)
-            lists(t, c, 0, 0, "MMC1", "rm8", 256)
+            S, st, iz = B("SROT%d" % P, c * NC, c * NC + NC), B("ST_%d" % c, rows=8), B("IZ_%d" % c)
+            ua, ub = B("pU%d" % c, 0, NC), B("pU%d" % c, NC, 2 * NC)
+            mm([(ua, B("IDn32"), S)], True, False)
+            mm([(ua, B("EXz", rows=8), st)], False, False)
+            mm([(ua, B("B64"), iz)], False, True)
+            lists(t, c, ua, None, 0, B("OHL_%d" % c), ["W1"], B("OFL_%d" % c))
+            tag[0] = "B%d" % c
+            mm([(B("pK%d" % c, 256, 384, rows=16), B("IDh", 0, 16, rows=8), st), (B("pK%d" % c, 256, 384, rows=8), B("B64", 0, 128, 16), iz)], True, False)
+            mm([(ub, B("IDn32"), S)], True, False)
+            tag[0] = "F%d" % c
+            for m in range(16):
+                cp(B("Z_%d" % c, 2 * m, 32 * NC, 32), tm(c, m % 2), "V" if t == 0 else PAR["FILL"][c][m])
+            er = B("pE%d" % c, 0, 128)
+            mm([(er, tm(c, 0), B("BM")), (er, B("ONE", rows=1), B("CROW", rows=1)), (er, tm(c, 1), B("BM"))], True, False)
         for c in range(2):
-            tag[0] = "Y%d" % c
-            mm(("pT%d" % c, 0, 256), [(B("IDb"), ("TT", 256 * c, 256 * c + 256))])
-            pick(t, c, "Y_%d" % c, YSPLIT[c])
+            Z, MX = "Z_%d" % c, "MX_%d" % c
+            for k in range(4):
+                tag[0] = "Y%d" % c
+                gather(PAR["YS"][c][k], B(Z, 1024 * k + 1, 1024 * k + 1024, 2), B("XL%d" % t), B("OFL_%d" % c, 32 * k, 32 * k + 32))
+                tag[0] = "M%d" % c
+                scan(B(MX, 1024 * k + 1, 1024 * k + 1024), B(Z, 1024 * k, 1024 * k + 1023), B(Z, 1024 * k + 1, 1024 * k + 1024), 256.0, OP.min, OP.max)
         for c in range(2):
             i0 = c * NC
-            E, Y = "pE%d" % c, "Y_%d" % c
-            er = (E, 0, 128)
-            tag[0] = "M%d" % c
-            mm(er, [(("TT", 256 * c, 256 * c + NC), B("BM%d" % c)), (("ONE", 0, 128, "p", 1), ("CROW", 0, 128, "p", 1))], True, False)
-            for j in range(15 - JA[c]):
-                for a in range(2):
-                    s = (2 * j + a) * NC
-                    tt(("MX_%d" % c, s, s + NC), ("pT%d" % c, 128 * a, 128 * a + 128), (Y, j + a, 16 * NC, 16), OP.max)
-                    mm((E, j, 128, 16), [(("MX_%d" % c, s, s + NC), B("G32")), ((Y, j + a, 16 * NC, 16), B("GM16"))], False, False, er)
-            for b in range(0, JA[c], 2):
-                sl = [(j, a) for j in range(15 - JA[c] + b, min(15, 15 - JA[c] + b + 2)) for a in range(2)]
-                pv = "p%s%d" % ("VK"[b // 2 % 2], c)
-                tag[0] = "A%d" % c
-                for k, (j, a) in enumerate(sl):
-                    mm((pv, NC * k, NC * k + NC), [(B("IDb"), (Y, j + a, 16 * NC, 16)), (B("IDn"), ("TT", 256 * c + NC * a, 256 * c + NC * a + NC))])
-                w, x = NC * len(sl), 2 * b * NC
-                op("A", [lambda c=c, pv=pv, w=w, x=x: g.scalar.activation(T["AX_%d" % c][:, x:x + w], T[pv][:, 0:w], AF.Abs)],
-                   [(pv, 0, w)], [("AX_%d" % c, x, x + w)], w)
-                for k, (j, a) in enumerate(sl):
-                    mm((E, j, 128, 16), [(("AX_%d" % c, x + NC * k, x + NC * k + NC), B("G16"))], False, False, er)
+            E, K, Z, MX = "pE%d" % c, "pK%d" % c, "Z_%d" % c, "MX_%d" % c
+            tag[0] = "E%d" % c
+            for j0 in range(0, 15, 3):
+                mm([(B(E, j, 128, 16), B(Z, 2 * (j + a) + 1, 32 * NC, 32), B("BM", 0, 128, 16)) for j in range(j0, j0 + 3) for a in range(2)], False, False)
+            for j0 in range(0, 15, 3):
+                mm([(B(E, j, 128, 16), B(MX, 2 * (j + a) + 1 + j % 2, 32 * NC, 32), B("B64", 0, 128, 16)) for j in range(j0, j0 + 3) for a in range(2)], False, j0 == 12)
             tag[0] = "C%d" % c
-            mm(er, [(("TT", 256 * c + NC, 256 * c + 2 * NC), B("BM%d" % c))], False, True)
-            SC, KI, JJ, SM = [B("%s_%d" % (x, c)) for x in ("SC", "KI", "JJ", "SM")]
-            op("V", [lambda c=c, E=E: g.vector.tensor_tensor_scan(T["SC_%d" % c][:, :], T.RST[:, :], T[E][:, 0:128], 1.0e9, OP.max, OP.min)],
-               [er, B("RST")], [SC], 128)
-            key = ("SC_%d" % c, 15, 128, 16)
-            tie = ("SM_%d" % c, 16, 24)
-            cp(KI, key)
-            ts(tie, key, float(16 * TH), OP.is_lt)
-            ts(JJ, KI, 15, AND)
-            tt(B("TD_%d" % c), tie, B("DZ_%d" % c), OP.mult)
-            tt(("SM_%d" % c, 8, 16), JJ, tie, OP.mult)
-            tt(("SM_%d" % c, 0, 8), B("TD_%d" % c), B("ZL_%d" % c), OP.add)
-            mm((E, 128, 256, "p", 24), [(SM, B("IDh"))])
-            cp(("ST_%d" % c, 0, NC), (E, 128, 256, "p", 24))
-            K = "pK%d" % c
-            st = B("ST_%d" % c)
-            for r, x in ((0, "EXz"), (128, "EXzn"), (256, "EXn")):
-                mm((K, r, r + 128), [((x, 0, 128, "p", 24), st)])
-            tag[0] = "R%d" % c
+            st, sm = B("ST_%d" % c), "SM_%d" % c
+            rows, ub = B(K, 256, 384, rows=16), B("pU%d" % c, NC, 2 * NC)
+            scan(B("SC_%d" % c), B("RST"), B(E, 0, 128), float(CAP), OP.max, OP.min)
+            key = B("SC_%d" % c, 14, 128, 16)
+            ts(B("RR_%d" % c), key, R16, OP.add, R16, OP.subtract)
+            ts(B(sm, 0, 8), key, float(CAP - 4), OP.is_lt, 16.0, OP.mult)
+            tt(B(sm, 8, 16), key, B("RR_%d" % c), OP.subtract)
+            mm([(rows, B(sm), B("IDb"))], False, True)
+            ts(st, rows, B("c17"), OP.add, -float(ZC), OP.max)
+            zz, dl, gd = B(E, 0, 128), B(E, 384, 512), B(E, 256, 384)
+            mm([(zz, B("EXz", rows=8), B("ST_%d" % c, rows=8))])
+            mm([(dl, B("EXj64", rows=16), st)])
+            tag[0] = "Q%d" % c
+            mm([(ub, B("EXzj", rows=16), st)], False, True)
 
             def starts():
                 tag[0] = "S%d" % c
-                ts(B("GE_%d" % c), (K, 384, 512), B("rp1"), OP.is_le)
-                gd = (E, 256, 384)
-                tt(gd, B("GE_%d" % c), (K, 256, 384), OP.mult)
-                tt(("SX%d" % t, i0, i0 + NC), ("SROT%d" % P, i0, i0 + NC), gd, OP.subtract)
+                tt(B("OHJ_%d" % c), dl, B("OHL_%d" % c), OP.mult)
+                mm([(gd, B("TRI"), B("OHJ_%d" % c))])
+                tt(B("SX%d" % t, 16 + i0, 16 + i0 + NC), B("SROT%d" % P, i0, i0 + NC), gd, OP.subtract)
+                lo, hi = (0, 16 + NC) if c == 0 else (16 + NC, SW)
+                sr = B("SR%d" % (t + 1), lo, hi)
+                s = send(T.cores[(rank - 1) % n], sr, B("SX%d" % t, lo, hi), "rs%d%d" % (t + 1, c), "ls%d%d" % (t + 1, c))
+                recv(sr, T.cores[(rank + 1) % n], "rs%d%d" % (t + 1, c), PAR["RECV"], s)
                 tag[0] = "Q%d" % c
-            lists(t, c, 0, 128, "MMC2", "rr", 0, starts)
-        for c in CORD:
-            tag[0] = "S%d" % c
-            lo, hi = c * NC, 257 if c else NC
-            s = send(T.cores[(rank - 1) % n], ("SR%d" % (t + 1), lo, hi), ("SX%d" % t, lo, hi), "rs%d%d" % (t + 1, c), "ls%d%d" % (t + 1, c))
-            recv(("SR%d" % (t + 1), lo, hi), T.cores[(rank + 1) % n], "rs%d%d" % (t + 1, c), RECV, s)
+            lists(t, c, ub, zz, NC, B("OHQ_%d" % c), ["W1", "W9"], B("OFQ_%d" % c), starts)
+        tag[0] = "X"
         if t < 2:
             send_log(t + 2)
         if not last:
             tag[0] = "P"
-            an = ("pE1", 160, 168)
-            mm(an, [(B("ONEh"), ("SM_0", 16, 24)), (B("ONEh"), ("SM_1", 16, 24))])
-            tt(B("AP8"), an, B("G205"), OP.mult)
-            acol = ("SX%d" % (t + 1), 256, 257)
-            op("V", [lambda acol=acol: g.vector.tensor_reduce(ap(acol), T.AP8[:, :], AxisListType.X, OP.add)], [B("AP8")], [acol], 64)
-            ts(B("LA"), B("i16"), acol, OP.add, 5.0, OP.mult)
-            ts(B("LB"), B("LA"), 255, AND)
-            cp(B("LO"), B("LB"))
-            prep_c(t + 1, "A")
-            tt(B("dA"), acol, ("SR%d" % (t + 1), 256, 257), OP.subtract)
-            ts(B("LC"), B("i16"), B("dA"), OP.add)
-            ts(B("LD"), B("LC"), 255, AND)
-            cp(B("LS"), B("LD"))
-            gather(DQ, B("SROT%d" % ((t + 1) % 2)), ("SR%d" % (t + 1), 0, 256), B("LS"))
+            an, own, far = B("pU0", 256, 272, rows=8), B("SX%d" % (t + 1), 0, 16, rows=8), B("SR%d" % (t + 1), 0, 16, rows=8)
+            mm([(an, B("SM_%d" % c, 0, 8), B("ONE", 0, 16)) for c in range(2)])
+            cp(own, an)
+            mm([(B("pU0", 272, 304), B("IDn32"), B("NCT", 0, 32)), (B("pU0", 288, 304), B("EXbn", rows=8), far)], True, False)
+            mm([(B("pU0", 272, 288), B("EXa", rows=8), own), (B("pU0", 288, 304), B("EXb", rows=8), own)], False, True)
+            cp(B("LI"), B("pU0", 272, 304))
+            ts(B("LJ"), B("LI"), 255, AND)
+            cp(B("LOS"), B("LJ"))
+            gather("V", B("D%d" % (1 - P)), B("CF%d" % (t + 1)), B("LOS", 0, 16), -2.0, -1.0)
+            gather("V", B("SROT%d" % (1 - P)), B("SR%d" % (t + 1), 16, SW), B("LOS", 16, 32))
         for c in range(2):
-            tag[0] = "V%d" % c
-            pick(t, c, "V_%d" % c, VSPLIT[c])
+            V, MV = "V_%d" % c, "MV_%d" % c
+            for k in range(4):
+                tag[0] = "V%d" % c
+                gather(PAR["VS"][c][k], B(V, 512 * k, 512 * k + 512), B("XL%d" % t), B("OFQ_%d" % c, 32 * k, 32 * k + 32))
+                tag[0] = "D%d" % c
+                scan(B(MV, 512 * k + 1, 512 * k + 512), B(V, 512 * k, 512 * k + 511), B(V, 512 * k + 1, 512 * k + 512), 256.0, OP.min, OP.max)
         for c in range(2):
             i0 = c * NC
-            E, K, V, AB, st = "pE%d" % c, "pK%d" % c, "V_%d" % c, "AB_%d" % c, B("ST_%d" % c)
-            for b in range(4):
-                a = 512 * b
+            E, K, F, V, MV, st = "pE%d" % c, "pK%d" % c, "pF%d" % c, "V_%d" % c, "MV_%d" % c, B("ST_%d" % c, rows=8)
+            OV, iz = "OV_%d" % c, B("IZ_%d" % c)
+            for h in range(2):
                 tag[0] = "D%d" % c
-                vd = ("p%s%d" % ("VT"[b % 2], c), 1, 512)
-                mm(vd, [(B("IDb"), (V, a + 1, a + 512)), (B("IDn"), (V, a, a + 511))])
-                op("A", [lambda AB=AB, a=a, vd=vd: g.scalar.activation(T[AB][:, a + 1:a + 512], ap(vd), AF.Abs)],
-                   [vd], [(AB, a + 1, a + 512)], 512)
-                if b % 2:
-                    mm((E, 224 + 32 * b, 288 + 32 * b), [(("SEL", 128 * m, 128 * m + 128), (AB, 512 * b - 512 + m, 512 * b + 512, 16)) for m in range(2, 16)])
-            tag[0] = "N%d" % c
-            OV, IZ = B("OV_%d" % c), B("IZ_%d" % c)
-            ts(OV, (E, 256, 384), float(TH2), OP.is_gt)
-            mm((E, 384, 512), [(B("TRI"), OV)])
-            ts(IZ, (E, 384, 512), 0.0, OP.is_equal)
-            if last:
-                mm((K, 0, NC, "p", 8), [(("EXs", 0, 8, "p", 24), st), (B("Gn"), IZ)])
-            else:
-                mm((K, 0, NC), [(("EXz", 0, 128, "p", 24), st), (B("BLKn"), IZ)])
-            mm((E, 144, 152), [(("SEL", 128 * p, 128 * p + 128), ("IZ_%d" % c, p, NC, 16)) for p in range(16)] + [(B("IDb"), B("KT"))])
-            if not last:
-                mm((E, 128, 136), [(st, ("EXs", 0, 8, "p", 24)), (IZ, B("Gn"))])
+                r = B((E, K)[h], 0, 64)
+                for m0 in (1, 6, 11):
+                    mm([(r, B("WN", 16 - m, 144 - m), B(V, 1024 * h + m, 1024 * h + 1024, 16)) for m in range(m0, m0 + 5)], m0 == 1, False)
+                for m0 in (2, 9):
+                    mm([(r, B("SEL", 16 - m, 144 - m), B(MV, 1024 * h + m, 1024 * h + 1024, 16)) for m in range(m0, m0 + 7)], False, m0 == 9)
+                tag[0] = "N%d" % c
+                ts(B(OV, 64 * h, 64 * h + 64), r, float(32 * TH2), OP.is_gt)
+            mm([(B(F, 256, 384), B("TRI"), B(OV))])
+            ts(iz, B(F, 256, 384), 0.0, OP.is_equal, 1.0 / 64, OP.mult)
+            tag[0] = "T%d" % c
+            tl = B(E, 128, 136)
+            mm([(tl, B("ONE", rows=1), B("KT", rows=1))] + [(tl, B("SEL", 16 - p, 144 - p), B("IZ_%d" % c, p, NC, 16)) for p in range(16)])
             for a in range(2):
-                ts(("TO_%d" % c, 8 * a, 8 * a + 8), (E, 144, 152), float(a - 2), OP.add)
-            gather(TQ[c], ("TT", 256 * c, 256 * c + 256), B(V), B("TO_%d" % c))
+                ts(B("TO_%d" % c, 8 * a, 8 * a + 8), tl, B(("ra", "rb")[a]), OP.add)
+            gather(PAR["TQ"][c], B("TT", 256 * c, 256 * c + 256), B(V), B("TO_%d" % c))
             if last:
-                ts(("YZ", i0, i0 + NC), (K, 0, NC, "p", 8), float(ZC), OP.add)
+                r8 = B(K, 256, 384, rows=8)
+                mm([(r8, B("IDh", 0, 8, rows=8), st), (r8, B("B64", 0, 128, 16), iz)])
+                ts(B("YZ", i0, i0 + NC), r8, float(ZC - 1), OP.add)
                 for a in range(2):
-                    x = ("TT", 256 * c + NC * a, 256 * c + NC * a + NC)
+                    x = B("TT", 256 * c + NC * a, 256 * c + NC * a + NC)
                     dma("SA"[a], T.yt[:, 256 * a + i0:256 * a + i0 + NC], ap(x), [x], [], "d_y%s%d" % ("ab"[a], c), 2500)
-    dma("S", T.yz[:, :], T.YZ[:, :], [B("YZ")], [], "d_yz", 2000)
-    ts(B("LC"), B("n205"), ("SR4", 256, 257), OP.subtract)
-    ts(B("LD"), B("LC"), 255, AND)
-    cp(B("LS"), B("LD"))
-    gather("V", B("YSO"), ("SR4", 0, 256), B("LS"), 1.0, float(ZC))
-    dma("S", T.ys[:, :], T.YSO[:, :], [B("YSO")], [], "d_ys", 2500)
+    tag[0] = "Z"
+    dma("S", T.yz[:, :], ap(B("YZ")), [B("YZ")], [], "d_yz", 2000)
+    fin = B("pU0", 272, 288)
+    mm([(fin, B("IDn32"), B("NCT", 32, 48)), (fin, B("EXbn", rows=8), B("SR4", 0, 16, rows=8))])
+    cp(B("LI", 0, 16), fin)
+    ts(B("LJ", 0, 16), B("LI", 0, 16), 255, AND)
+    cp(B("LOS", 0, 16), B("LJ", 0, 16))
+    gather("V", B("YSO"), B("SR4", 16, SW), B("LOS", 0, 16), 1.0, float(ZC))
+    dma("S", T.ys[:, :], ap(B("YSO")), [B("YSO")], [], "d_ys", 2500)
     return ops
 
 
+def meet(a, b):
+    return a[1] < b[2] and b[1] < a[2] and (a[1] - b[1]) % math.gcd(a[3], b[3]) == 0
+
+
+def covers(a, b):
+    return a[1] <= b[1] and b[2] <= a[2] and b[3] % a[3] == 0 and (b[1] - a[1]) % a[3] == 0 and b[4] <= a[4]
+
+
 def link(ops):
-    hist = {}
+    hist, turns = {}, {}
     for k, o in enumerate(ops):
         deps = {}
 
@@ -449,31 +411,30 @@ def link(ops):
         if "after" in o:
             add(o["after"], False)
         acc = [(r, False) for r in o["r"]] + [(w, True) for w in o["w"]]
-        for (b, lo, hi), wr in acc:
-            ps = SCRATCH[b][0] == "psum"
-            for (x, l2, h2, w2) in hist.get(b, ()):
-                if x == k:
-                    continue
-                same = ops[x]["q"] == o["q"]
-                if ps and (not same):
-                    add(x, True)
-                elif ps and o["q"] == "P":
-                    add(x, False)
-                elif (wr or w2) and lo < h2 and l2 < hi:
-                    add(x, True)
-        for (b, lo, hi), wr in acc:
-            h = hist.setdefault(b, [])
-            ps = SCRATCH[b][0] == "psum"
-            if wr and not ps:
-                h[:] = [y for y in h if not (lo <= y[1] and y[2] <= hi and y[0] != k)]
-            if ps:
-                h[:] = [y for y in h if ops[y[0]]["q"] != o["q"] or y[0] == k or (o["q"] != "P" and not (wr and lo <= y[1] and y[2] <= hi))] if o["q"] == "P" or wr else h
-            h.append((k, lo, hi, wr))
+        for b in set(r[0] for r, wr in acc if SCRATCH[r[0]][0] == "psum"):
+            was, now = turns.get(b, ([], []))
+            if now and ops[now[0]]["q"] != o["q"]:
+                was, now = now, []
+            for x in was:
+                add(x, True)
+            if now and o["q"] == "P":
+                add(now[-1], False)
+            turns[b] = (was, now + [k])
+        for r, wr in acc:
+            for (x, r2, w2) in hist.get(r[0], ()):
+                if (wr or w2) and meet(r, r2):
+                    add(x, not (o["q"] == "P" and ops[x]["q"] == "P"))
+        for r, wr in acc:
+            h = hist.setdefault(r[0], [])
+            if wr:
+                h[:] = [y for y in h if y[0] == k or not covers(r, y[1])]
+            h.append((k, r, wr))
         o["deps"] = deps
 
 
 def order(ops):
     n = len(ops)
+    sync = PAR["SYNC"]
     succ = [[] for _ in range(n)]
     need = [0] * n
     for k, o in enumerate(ops):
@@ -482,12 +443,12 @@ def order(ops):
             need[k] += 1
     way = [0.0] * n
     for k in range(n - 1, -1, -1):
-        way[k] = ops[k]["cost"] + SYNCNS + max([way[s] for s in succ[k]] + [0.0])
+        way[k] = ops[k]["cost"] + sync + max([way[s] for s in succ[k]] + [0.0])
     for k, o in enumerate(ops):
-        way[k] += BI.get(o["tag"], 0)
+        way[k] += PAR["BI"].get(o["tag"], 0)
     prev = {}
     for k, o in enumerate(ops):
-        if o["kind"] in ("dma", "send") or o["q"] == "G":
+        if o["kind"] in ("dma", "send"):
             if o["q"] in prev:
                 succ[prev[o["q"]]].append(k)
                 need[k] += 1
@@ -518,7 +479,7 @@ def order(ops):
         busy = {"dma": 60.0, "recv": 0.0, "send": o["cost"]}.get(o["kind"], o["cost"])
         free[q] = t0 + busy
         o["t0"] = t0
-        end = t0 + o["cost"] + SYNCNS
+        end = t0 + o["cost"] + sync
         seq.append(k)
         for s in succ[k]:
             e = t0 + busy if (k not in ops[s]["deps"] or ops[s]["q"] == q and not ops[s]["deps"][k]) else end
@@ -533,7 +494,6 @@ def emit(g, T, ops, seq):
     queue = {"V": g.vector, "A": g.scalar, "P": g.tensor, "G": g, "S": g.sync}
     total = {"V": 0, "A": 0, "P": 0, "G": 0}
     know = {q: {} for q in queue}
-    waited = {}
     issued = []
     for k in seq:
         o = ops[k]
@@ -552,7 +512,6 @@ def emit(g, T, ops, seq):
             if know[q].get(s, 0) >= v:
                 continue
             eng.wait_ge(T.sem[s], v)
-            waited[s] = max(waited.get(s, 0), v)
             know[q][s] = v
             for s2, v2 in d["clock"].items():
                 if know[q].get(s2, 0) < v2:

@@ -19,11 +19,13 @@ PAR = dict(
     VS=["AAAA", "AAAA"],
     TQ="AA",
     FILL=["VVVVVVVVVVGGGGGG", "VVVVVVVVVVGGGGGG"],
-    BI={},
+    BI={}, TURNS=3000, TAIL=64, SEED=1, HEAT=500, LOG=(20000, 34000, 48000), EC="",
 )
+PAR.update(SYNC=290, SEND=1200, RECV=1800, LOG=(22000, 40000, 58000), TURNS=2500, HEAT=600)
 PAR.update({'YS': ['AAAV', 'AAVA'], 'VS': ['AAAA', 'AVAA'], 'TQ': 'AA', 'FILL': ['VVVVVVVVVAAAAGGG', 'VVVVVVVAAAAGGGGG'], 'BI': {'N1': -6577, 'P': 10849, 'C0': -18109, 'Y0': 29548, 'Q0': 35775, 'L0': 13704, 'B1': 36812, 'Z': 24811, 'Y1': -3215, 'M0': -37336, 'L1': -10511, 'V0': 72407, 'V1': 3110, 'Q1': 34840, 'F1': -67990, 'D1': -9648, 'B0': -34734, 'C1': -90901, 'c': -20085, 'X': 44139, 'F0': -56967, 'S0': -49337, 'E1': -42699, 'S1': 26460, 'T0': 3205, 'M1': -40204, 'D0': -15280, 'N0': 48304, 'E0': -62395, 'T1': -16593}})
 
 SCRATCH = {}
+DONE = {}
 
 
 def _b(name, cols, dtype, where="sbuf", rows=128):
@@ -53,7 +55,7 @@ _b("YZ", 256, "float32", rows=8)
 for _k in range(2):
     for _n, _c, _d in (("MASK", NC, "bfloat16"), ("OHL", NC, "float16"), ("OHQ", NC, "float16"), ("DS", NC, "float16"), ("XS", NC, "float32"),
                        ("FI", NC, "int32"), ("FJ", NC, "int32"), ("OFL", NC, "uint16"), ("OFQ", NC, "uint16"), ("Z", 32 * NC, "bfloat16"),
-                       ("MX", 32 * NC, "bfloat16"), ("V", 16 * NC, "bfloat16"), ("MV", 16 * NC, "bfloat16"), ("SC", 128, "float32"),
+                       ("MX", 32 * NC, "bfloat16"), ("V", 16 * NC, "bfloat16"), ("MV", 16 * NC, "bfloat16"), ("SC", 128, "float32"), ("EC", 128, "float32"),
                        ("RR", 8, "float32"), ("SM", 16, "bfloat16"), ("OHJ", NC, "bfloat16"),
                        ("OV", NC, "bfloat16"), ("IZ", NC, "bfloat16"), ("TO", 16, "uint16")):
         _b("%s_%d" % (_n, _k), _c, _d)
@@ -61,26 +63,55 @@ for _k in range(2):
     for _n in ("U", "K", "E", "F"):
         _b("p%s%d" % (_n, _k), 512, "float32", where="psum")
 
-SEMAPHORES = ["sV", "sA", "sP", "sG"]
+SEMAPHORES = ["sV", "sA", "sP", "sG", "h0", "h1", "lh0", "lh1"]
 SEMAPHORES += ["d_" + n for n in ("s0", "cf", "z0", "t0", "xa", "xb", "ys", "yz", "ya0", "ya1", "yb0", "yb1")]
 for _v in range(1, 4):
-    SEMAPHORES += ["%s%d" % (n, _v) for n in ("rca", "rla", "rlb", "lca", "lla", "llb")]
+    SEMAPHORES += ["%s%d" % (n, _v) for n in ("rca", "rla", "rlb", "lca", "lla", "llb", "lcf", "llf")]
 for _v in range(1, 5):
     SEMAPHORES += ["%s%d%d" % (n, _v, c) for n in ("rs", "ls") for c in range(2)]
+
+
+def engines(topo, src, dst, upper=0):
+    e = topo.engines(src, dst)
+    if dst in topo.cores_of(src):
+        return e[len(e) // 2:] if upper else e[:len(e) // 2]
+    return e
+
+
+def way_of(T, topo, rank, v):
+    n = len(T.cores)
+    far = [x for x in range(1, NV) if T.cores[(rank - x) % n] not in topo.cores_of(T.cores[rank])]
+    return "near" if v not in far else "far" if v == far[0] else "on"
+
+
+def helper(T, topo, rank):
+    c = T.cores[rank]
+    return [x for x in topo.cores_of(c) if x not in T.cores and topo.die(x) != topo.die(c)][0]
+
+
+def hand_on(g, core, T, topo, rank):
+    v = [x for x in range(1, NV) if way_of(T, topo, rank, x) == "far"][0]
+    dst = T.cores[(rank - v) % len(T.cores)]
+    rid, pid = topo.addr(dst, core)
+    for k in range(2):
+        g.wait_ge(T.sem["h%d" % k], len(engines(topo, T.cores[rank], core, 1)))
+        lo, hi = k * W // 4, (k + 1) * W // 4
+        g.remote_dma(T["XL%d" % v][:, lo:hi], T.XL0[:, lo:hi], T.sem["rla%d" % v], T.sem["lh0"], pid, rid, topo.mask(core, dst))
+    g.wait_ge(T.sem["lh0"], 2 * len(topo.engines(core, dst)))
 
 
 def plan(g, core, T, topo):
     rank = T.rank_of(core)
     n = len(T.cores)
     ops = []
-    tag = ["c"]
+    tag = ["c", 0]
 
     def B(name, lo=0, hi=None, step=1, rows=128):
         p, o, c = VIRT[name] if name in VIRT else (name, 0, SCRATCH[name][1][1])
         return (p, o + lo, o + (c if hi is None else hi), step, min(rows, SCRATCH[p][1][0]))
 
     def op(q, fns, reads, writes, cost, kind="c", sem=None, cnt=0, cls=None):
-        ops.append(dict(tag=tag[0], q=q, fns=fns, r=reads, w=writes, cost=cost, kind=kind, sem=sem, cnt=cnt, cls=cls or q))
+        ops.append(dict(tag=tag[0], blk=(tag[0], tag[1]), q=q, fns=fns, r=reads, w=writes, cost=cost, kind=kind, sem=sem, cnt=cnt, cls=cls or q))
         return len(ops) - 1
 
     def ap(x):
@@ -139,6 +170,15 @@ def plan(g, core, T, topo):
                 f = lambda: g.scalar.activation(ap(o), ap(win).indirect(ap(off)), AF.Identity, bias=bias, scale=scale)
         op(q, [f], [win, off], [o], 60 + PAR["GN"] * width(o), cls="gather")
 
+    def either(first, qs, make):
+        alt = {}
+        for q in [x for x in qs if x != first] + [first]:
+            make(q)
+            alt[q] = (ops[-1]["fns"], ops[-1]["cost"])
+            if q != first:
+                ops.pop()
+        ops[-1]["alt"] = alt
+
     def mm(items, start=True, stop=True):
         fns, rd, wr, cost = [], [], [], 0
         for k, (o, l, r) in enumerate(items):
@@ -152,15 +192,16 @@ def plan(g, core, T, topo):
         eng = g.sync if q == "S" else g.scalar
         op(q, [lambda: eng.dma_start(o, a)], rd, wr, cost, kind="dma", sem=sem)
 
-    def send(dst, out, src, rs, ls):
+    def send(dst, out, src, rs, ls, upper=0):
         rid, pid = topo.addr(dst, core)
-        m = topo.mask(core, dst)
-        return op("G", [lambda: g.remote_dma(ap(out), ap(src), T.sem[rs], T.sem[ls], pid, rid, m)], [src], [], PAR["SEND"],
-                  kind="send", sem=ls, cnt=len(topo.engines(core, dst)))
+        e = engines(topo, core, dst, upper)
+        return op("G", [lambda: g.remote_dma(ap(out), ap(src), T.sem[rs], T.sem[ls], pid, rid, sum(1 << x for x in e))], [src], [], PAR["SEND"],
+                  kind="send", sem=ls, cnt=len(e))
 
-    def recv(o, src, rs, cost, after):
-        op("R", [], [], [o], cost, kind="recv", sem=rs, cnt=len(topo.engines(src, core)))
-        ops[-1]["after"] = after
+    def recv(o, e, rs, cost, after=None):
+        op("R", [], [], [o], cost, kind="recv", sem=rs, cnt=len(e))
+        if after is not None:
+            ops[-1]["after"] = after
 
     def iota(o, pat, base, cm):
         if SCRATCH[o[0]][2] == "int32":
@@ -231,16 +272,36 @@ def plan(g, core, T, topo):
     for v in range(NV):
         iota(B("SX%d" % v, 0, 16), [[0, 16]], 0, 0)
 
-    def send_log(v):
-        dst = T.cores[(rank - v) % n]
-        src = T.cores[(rank + v) % n]
-        a = send(dst, B("CF%d" % v), B("CF0"), "rca%d" % v, "lca%d" % v)
-        recv(B("CF%d" % v), src, "rca%d" % v, 4000, a)
-        for lo, hi, x in ((0, H, "a"), (H, WX, "b")):
-            a = send(dst, B("XL%d" % v, lo, hi), B("XL0", lo, hi), "rl%s%d" % (x, v), "ll%s%d" % (x, v))
-            recv(B("XL%d" % v, lo, hi), src, "rl%s%d" % (x, v), 9000 * (1 + lo // H), a)
+    def send_logs(t):
+        for v in range(1, NV):
+            dst = T.cores[(rank - v) % n]
+            how = way_of(T, topo, rank, v)
+            if how == "near" and t == min(v - 1, 1):
+                send(dst, B("CF%d" % v), B("CF0"), "rca%d" % v, "lca%d" % v, 1)
+                send(dst, B("XL%d" % v), B("XL0"), "rla%d" % v, "lla%d" % v, 1)
+            if how == "far" and t == v - 1:
+                send(dst, B("CF%d" % v), B("CF0"), "rca%d" % v, "lca%d" % v)
+                for k in range(2):
+                    x = B("XL0", k * H // 2, (k + 1) * H // 2)
+                    send(helper(T, topo, rank), x, x, "h%d" % k, "lh%d" % k, 1)
+                send(dst, B("XL%d" % v, H, W), B("XL0", H, W), "rlb%d" % v, "llb%d" % v)
+        if 0 < t < NV - 1 and way_of(T, topo, (rank + t) % n, t + 1) == "on":
+            dst = T.cores[(rank - 1) % n]
+            send(dst, B("CF%d" % (t + 1)), B("CF%d" % t), "rca%d" % (t + 1), "lcf%d" % t, 1)
+            send(dst, B("XL%d" % (t + 1)), B("XL%d" % t), "rla%d" % (t + 1), "llf%d" % t, 1)
 
-    send_log(1)
+    for v in range(1, NV):
+        own = (rank + v) % n
+        at = PAR["LOG"][v - 1]
+        if way_of(T, topo, own, v) == "far":
+            recv(B("CF%d" % v), engines(topo, T.cores[own], core), "rca%d" % v, at - 4000)
+            recv(B("XL%d" % v, 0, H), 2 * engines(topo, helper(T, topo, own), core), "rla%d" % v, at)
+            recv(B("XL%d" % v, H, W), engines(topo, T.cores[own], core), "rlb%d" % v, at)
+        else:
+            e = engines(topo, T.cores[(rank + 1) % n if way_of(T, topo, own, v) == "on" else own], core, 1)
+            recv(B("CF%d" % v), e, "rca%d" % v, at - 4000)
+            recv(B("XL%d" % v), e, "rla%d" % v, at)
+    send_logs(0)
     select(B("TRI"), B("B64"), [[1, 128]], OP.is_ge, 0, -1)
     for x, src, top in (("SEL", "B64", 0), ("WN", "BM", 1)):
         iota(B(x, 0, 16), [[0, 16]], 0, 0)
@@ -251,10 +312,7 @@ def plan(g, core, T, topo):
         D = B("D%d" % (t % 2), c * NC, c * NC + NC)
         M, DS, XS, FI, FJ = [B("%s_%d" % (x, c)) for x in ("MASK", "DS", "XS", "FI", "FJ")]
         cnt, f = B("pK%d" % c, kreg, kreg + NC), B("pF%d" % c, kreg, kreg + NC)
-        if zz is None:
-            ts(M, u, 1.0, OP.is_ge)
-        else:
-            tt(M, B("SROT%d" % (t % 2), c * NC, c * NC + NC), zz, OP.is_le)
+        tt(M, B("SROT%d" % (t % 2), c * NC, c * NC + NC), zz, OP.is_le if between else OP.is_lt)
         mm([(cnt, B("B64"), M)])
         if between:
             between()
@@ -263,13 +321,18 @@ def plan(g, core, T, topo):
         tt(XS, u, DS, OP.mult)
         mm([(f, B(x), DS) for x in ws] + [(f, B("W0"), oh)], True, False)
         mm([(f, B("BLKs"), XS)], False, True)
-        cp(FI, f)
-        ts(FJ, FI, W - 1, AND)
-        cp(off, FJ)
+        w = PAR["TAIL"]
+        parts = [[(x[0], x[1] + a, x[1] + a + w) + x[3:] for x in (f, FI, FJ, off)] for a in range(0, NC, w)]
+        for x in parts:
+            cp(x[1], x[0])
+        for x in parts:
+            ts(x[2], x[1], W - 1, AND)
+            cp(x[3], x[2])
 
     for t in range(NV):
         P = t % 2
         last = t == NV - 1
+        tag[1] = t
 
         def tm(c, a):
             return B("TL", 256 * a + NC * c, 256 * a + NC * c + NC) if t == 0 else B("TT", 256 * c + NC * a, 256 * c + NC * a + NC)
@@ -280,20 +343,22 @@ def plan(g, core, T, topo):
             mm([(ua, B("IDn32"), S)], True, False)
             mm([(ua, B("EXz", rows=8), st)], False, False)
             mm([(ua, B("B64"), iz)], False, True)
-            lists(t, c, ua, None, 0, B("OHL_%d" % c), ["W1"], B("OFL_%d" % c))
+            z1 = B("pK%d" % c, 384, 512)
+            mm([(z1, B("EXz", rows=8), st), (z1, B("B64"), iz)])
+            lists(t, c, ua, z1, 0, B("OHL_%d" % c), ["W1"], B("OFL_%d" % c))
             tag[0] = "B%d" % c
             mm([(B("pK%d" % c, 256, 384, rows=16), B("IDh", 0, 16, rows=8), st), (B("pK%d" % c, 256, 384, rows=8), B("B64", 0, 128, 16), iz)], True, False)
             mm([(ub, B("IDn32"), S)], True, False)
             tag[0] = "F%d" % c
             for m in range(16):
-                cp(B("Z_%d" % c, 2 * m, 32 * NC, 32), tm(c, m % 2), "V" if t == 0 else PAR["FILL"][c][m])
+                either("V" if m < 12 or t == 0 else "G", "VAG", lambda q: cp(B("Z_%d" % c, 2 * m, 32 * NC, 32), tm(c, m % 2), q))
             er = B("pE%d" % c, 0, 128)
             mm([(er, tm(c, 0), B("BM")), (er, B("ONE", rows=1), B("CROW", rows=1)), (er, tm(c, 1), B("BM"))], True, False)
         for c in range(2):
             Z, MX = "Z_%d" % c, "MX_%d" % c
             for k in range(4):
                 tag[0] = "Y%d" % c
-                gather(PAR["YS"][c][k], B(Z, 1024 * k + 1, 1024 * k + 1024, 2), B("XL%d" % t), B("OFL_%d" % c, 32 * k, 32 * k + 32))
+                either("A", "AV", lambda q: gather(q, B(Z, 1024 * k + 1, 1024 * k + 1024, 2), B("XL%d" % t), B("OFL_%d" % c, 32 * k, 32 * k + 32)))
                 tag[0] = "M%d" % c
                 scan(B(MX, 1024 * k + 1, 1024 * k + 1024), B(Z, 1024 * k, 1024 * k + 1023), B(Z, 1024 * k + 1, 1024 * k + 1024), 256.0, OP.min, OP.max)
         for c in range(2):
@@ -328,12 +393,11 @@ def plan(g, core, T, topo):
                 lo, hi = (0, 16 + NC) if c == 0 else (16 + NC, SW)
                 sr = B("SR%d" % (t + 1), lo, hi)
                 s = send(T.cores[(rank - 1) % n], sr, B("SX%d" % t, lo, hi), "rs%d%d" % (t + 1, c), "ls%d%d" % (t + 1, c))
-                recv(sr, T.cores[(rank + 1) % n], "rs%d%d" % (t + 1, c), PAR["RECV"], s)
+                recv(sr, engines(topo, T.cores[(rank + 1) % n], core), "rs%d%d" % (t + 1, c), PAR["RECV"], s)
                 tag[0] = "Q%d" % c
             lists(t, c, ub, zz, NC, B("OHQ_%d" % c), ["W1", "W9"], B("OFQ_%d" % c), starts)
         tag[0] = "X"
-        if t < 2:
-            send_log(t + 2)
+        send_logs(t + 1)
         if not last:
             tag[0] = "P"
             an, own, far = B("pU0", 256, 272, rows=8), B("SX%d" % (t + 1), 0, 16, rows=8), B("SR%d" % (t + 1), 0, 16, rows=8)
@@ -345,12 +409,13 @@ def plan(g, core, T, topo):
             ts(B("LJ"), B("LI"), 255, AND)
             cp(B("LOS"), B("LJ"))
             gather("V", B("D%d" % (1 - P)), B("CF%d" % (t + 1)), B("LOS", 0, 16), -2.0, -1.0)
-            gather("V", B("SROT%d" % (1 - P)), B("SR%d" % (t + 1), 16, SW), B("LOS", 16, 32))
+            for c in range(2):
+                either("V", "AV", lambda q: gather(q, B("SROT%d" % (1 - P), NC * c, NC * c + NC), B("SR%d" % (t + 1), 16, SW), B("LOS", 16 + 8 * c, 24 + 8 * c)))
         for c in range(2):
             V, MV = "V_%d" % c, "MV_%d" % c
             for k in range(4):
                 tag[0] = "V%d" % c
-                gather(PAR["VS"][c][k], B(V, 512 * k, 512 * k + 512), B("XL%d" % t), B("OFQ_%d" % c, 32 * k, 32 * k + 32))
+                either("A", "AV", lambda q: gather(q, B(V, 512 * k, 512 * k + 512), B("XL%d" % t), B("OFQ_%d" % c, 32 * k, 32 * k + 32)))
                 tag[0] = "D%d" % c
                 scan(B(MV, 512 * k + 1, 512 * k + 512), B(V, 512 * k, 512 * k + 511), B(V, 512 * k + 1, 512 * k + 512), 256.0, OP.min, OP.max)
         for c in range(2):
@@ -373,7 +438,7 @@ def plan(g, core, T, topo):
             mm([(tl, B("ONE", rows=1), B("KT", rows=1))] + [(tl, B("SEL", 16 - p, 144 - p), B("IZ_%d" % c, p, NC, 16)) for p in range(16)])
             for a in range(2):
                 ts(B("TO_%d" % c, 8 * a, 8 * a + 8), tl, B(("ra", "rb")[a]), OP.add)
-            gather(PAR["TQ"][c], B("TT", 256 * c, 256 * c + 256), B(V), B("TO_%d" % c))
+            either("A", "AV", lambda q: gather(q, B("TT", 256 * c, 256 * c + 256), B(V), B("TO_%d" % c)))
             if last:
                 r8 = B(K, 256, 384, rows=8)
                 mm([(r8, B("IDh", 0, 8, rows=8), st), (r8, B("B64", 0, 128, 16), iz)])
@@ -402,7 +467,7 @@ def covers(a, b):
 
 
 def link(ops):
-    hist, turns = {}, {}
+    hist, turns, prev = {}, {}, {}
     for k, o in enumerate(ops):
         deps = {}
 
@@ -410,6 +475,10 @@ def link(ops):
             deps[x] = deps.get(x, False) or hard
         if "after" in o:
             add(o["after"], False)
+        if o["kind"] in ("dma", "send"):
+            if o["q"] in prev:
+                add(prev[o["q"]], False)
+            prev[o["q"]] = k
         acc = [(r, False) for r in o["r"]] + [(w, True) for w in o["w"]]
         for b in set(r[0] for r, wr in acc if SCRATCH[r[0]][0] == "psum"):
             was, now = turns.get(b, ([], []))
@@ -435,59 +504,94 @@ def link(ops):
 def order(ops):
     n = len(ops)
     sync = PAR["SYNC"]
-    succ = [[] for _ in range(n)]
-    need = [0] * n
-    for k, o in enumerate(ops):
-        for x in o["deps"]:
-            succ[x].append(k)
-            need[k] += 1
+    busy = [{"dma": 60.0, "recv": 0.0}.get(o["kind"], o["cost"]) for o in ops]
+    lag = [{x: (ops[x]["cost"] + sync if h else busy[x]) for x, h in o["deps"].items()} for o in ops]
+    succ = [{} for _ in range(n)]
+    for k in range(n):
+        for x, l in lag[k].items():
+            succ[x][k] = l
+
+    def place(key, back):
+        need = [len(succ[k] if back else lag[k]) for k in range(n)]
+        at = [ops[k]["cost"] - busy[k] if back else 0.0 for k in range(n)]
+        ready = sorted((key[k], k) for k in range(n) if need[k] == 0)
+        slots, t0 = {}, [0.0] * n
+        while ready:
+            k = ready.pop(0)[1]
+            t, w = at[k], busy[k]
+            if w:
+                l = slots.setdefault(ops[k]["q"], [])
+                i = len(l)
+                while i and l[i - 1][1] > t:
+                    i -= 1
+                while i < len(l) and l[i][0] < t + w:
+                    t = max(t, l[i][1])
+                    i += 1
+                l.insert(i, (t, t + w))
+            t0[k] = t
+            for s, d in (lag[k] if back else succ[k]).items():
+                at[s] = max(at[s], t + (d + w - busy[s] if back else d))
+                need[s] -= 1
+                if need[s] == 0:
+                    e, i = (key[s], s), len(ready)
+                    while i and ready[i - 1] > e:
+                        i -= 1
+                    ready.insert(i, e)
+        if back:
+            return [-(t0[k] + busy[k]) for k in range(n)], max(t0[k] + busy[k] for k in range(n))
+        return t0, max(t0[k] + ops[k]["cost"] for k in range(n))
     way = [0.0] * n
     for k in range(n - 1, -1, -1):
-        way[k] = ops[k]["cost"] + sync + max([way[s] for s in succ[k]] + [0.0])
-    for k, o in enumerate(ops):
-        way[k] += PAR["BI"].get(o["tag"], 0)
-    prev = {}
-    for k, o in enumerate(ops):
-        if o["kind"] in ("dma", "send"):
-            if o["q"] in prev:
-                succ[prev[o["q"]]].append(k)
-                need[k] += 1
-            prev[o["q"]] = k
-    ready_at = [0.0] * n
-    ready = {}
-    free = {}
-    seq = []
+        way[k] = max([ops[k]["cost"]] + [way[s] + d for s, d in succ[k].items()])
+    seed = [PAR["SEED"]]
 
-    def push(k):
-        ready.setdefault(ops[k]["q"], []).append(k)
-    for k in range(n):
-        if need[k] == 0:
-            push(k)
-    while any(ready.values()):
-        best = None
-        for q, l in ready.items():
-            if not l:
-                continue
-            f = free.get(q, 0.0) if q != "R" else 0.0
-            t0 = max(f, min(ready_at[k] for k in l))
-            k = min((k for k in l if ready_at[k] <= t0 + 1e-6), key=lambda k: (-way[k], k))
-            if best is None or t0 < best[0]:
-                best = (t0, q, k)
-        t0, q, k = best
-        ready[q].remove(k)
-        o = ops[k]
-        busy = {"dma": 60.0, "recv": 0.0, "send": o["cost"]}.get(o["kind"], o["cost"])
-        free[q] = t0 + busy
-        o["t0"] = t0
-        end = t0 + o["cost"] + sync
-        seq.append(k)
+    def rnd():
+        seed[0] = (seed[0] * 1103515245 + 12345) % 2 ** 31
+        return seed[0] / 2 ** 31
+
+    def assign(k, q):
+        ops[k]["q"], ops[k]["fns"], ops[k]["cost"] = q, ops[k]["alt"][q][0], ops[k]["alt"][q][1]
+        busy[k] = ops[k]["cost"]
         for s in succ[k]:
-            e = t0 + busy if (k not in ops[s]["deps"] or ops[s]["q"] == q and not ops[s]["deps"][k]) else end
-            ready_at[s] = max(ready_at[s], e)
-            need[s] -= 1
-            if need[s] == 0:
-                push(s)
-    return seq
+            succ[k][s] = lag[s][k] = busy[k] + sync
+
+    def packed(key):
+        t0, end = place(key, False)
+        t1, e1 = place(place([-(t0[k] + busy[k]) for k in range(n)], True)[0], False)
+        return (e1, t1) if e1 < end else (end, t0)
+    free = [k for k in range(n) if "alt" in ops[k]]
+    blocks = {}
+    for k in range(n):
+        blocks.setdefault(ops[k]["blk"], []).append(k)
+    blocks = list(blocks.values())
+    sig = tuple((o["blk"], o["kind"], o["sem"]) for o in ops)
+    cur = best = DONE.get(sig) or packed([-w for w in way]) + ([ops[k]["q"] for k in free],)
+    for it in range(0 if sig in DONE else PAR["TURNS"]):
+        key = list(cur[1])
+        if rnd() < 0.5:
+            for _ in range(1 + int(2 * rnd())):
+                k = free[int(rnd() * len(free))]
+                qs = sorted(ops[k]["alt"])
+                assign(k, qs[int(rnd() * len(qs))])
+        else:
+            for _ in range(1 + int(3 * rnd())):
+                d = (rnd() - 0.5) * (600, 2000, 6000)[int(3 * rnd())]
+                for k in blocks[int(rnd() * len(blocks))]:
+                    key[k] += d
+        new = packed(key) + ([ops[k]["q"] for k in free],)
+        if new[0] <= cur[0] + PAR["HEAT"] * rnd() * (1 - it / PAR["TURNS"]):
+            cur = new
+            if new[0] < best[0]:
+                best = new
+        else:
+            for k, q in zip(free, cur[2]):
+                assign(k, q)
+    DONE[sig] = best
+    for k, q in zip(free, best[2]):
+        assign(k, q)
+    for k in range(n):
+        ops[k]["t0"] = best[1][k]
+    return sorted(range(n), key=lambda k: (best[1][k], k))
 
 
 def emit(g, T, ops, seq):
@@ -542,6 +646,9 @@ def emit(g, T, ops, seq):
 
 def rank_program(g, core, T, topo):
     if T.rank_of(core) is None:
+        for r in range(len(T.cores)):
+            if core == helper(T, topo, r):
+                hand_on(g, core, T, topo, r)
         return
     ops = plan(g, core, T, topo)
     link(ops)

@@ -19,9 +19,9 @@ PAR = dict(
     VS=["AAAA", "AAAA"],
     TQ="AA",
     FILL=["VVVVVVVVVVGGGGGG", "VVVVVVVVVVGGGGGG"],
-    BI={}, TURNS=3000, TAIL=64, SEED=1, HEAT=500, LOG=(20000, 34000, 48000), EC="",
+    BI={}, TURNS=3000, TAIL=64, SEED=1, HEAT=500, LOG=(20000, 34000, 48000), XP=1, MOVE=(0.5, 0.7),
 )
-PAR.update(SYNC=290, SEND=1200, RECV=1800, LOG=(22000, 40000, 58000), TURNS=2500, HEAT=600)
+PAR.update(SYNC=290, SEND=1200, RECV=1800, LOG=(19000, 33000, 47000), TURNS=2500, HEAT=400, MOVE=(0.7, 0.85))
 PAR.update({'YS': ['AAAV', 'AAVA'], 'VS': ['AAAA', 'AVAA'], 'TQ': 'AA', 'FILL': ['VVVVVVVVVAAAAGGG', 'VVVVVVVAAAAGGGGG'], 'BI': {'N1': -6577, 'P': 10849, 'C0': -18109, 'Y0': 29548, 'Q0': 35775, 'L0': 13704, 'B1': 36812, 'Z': 24811, 'Y1': -3215, 'M0': -37336, 'L1': -10511, 'V0': 72407, 'V1': 3110, 'Q1': 34840, 'F1': -67990, 'D1': -9648, 'B0': -34734, 'C1': -90901, 'c': -20085, 'X': 44139, 'F0': -56967, 'S0': -49337, 'E1': -42699, 'S1': 26460, 'T0': 3205, 'M1': -40204, 'D0': -15280, 'N0': 48304, 'E0': -62395, 'T1': -16593}})
 
 SCRATCH = {}
@@ -40,26 +40,30 @@ for _v in range(4):
 for _n, _c, _d in (("S0I", 256, "int32"), ("TL", 512, "bfloat16"), ("TT", 512, "bfloat16"), ("YSO", 256, "float32"),
                    ("SROT0", 256, "float32"), ("SROT1", 256, "float32"), ("D0", 256, "float16"), ("D1", 256, "float16"),
                    ("SEL", 144, "bfloat16"), ("WN", 144, "bfloat16"), ("NCT", 48, "float32"), ("LI", 32, "int32"), ("LJ", 32, "int32"),
-                   ("LOS", 32, "uint16"), ("KT", 8, "bfloat16")):
+                   ("LOS", 32, "uint16"), ("KT", 8, "bfloat16"), ("WJ4", 512, "bfloat16"), ("WF4", 512, "float32"), ("P4", 4, "float32")):
     _b(_n, _c, _d)
 VIRT = {}
-for _p, _c, _d, _l in (("PF", 1, "float32", "rg rr pp rp1 ra rb c17"), ("PI", 1, "int32", "rowI rrI"),
-                       ("PJ", 16, "int32", "c16"), ("PG", 128, "float32", "colF IDn32 BLKs RST EXa EXb EXbn i16"),
-                       ("PB", 128, "bfloat16", "cg cr B64 BM TRI IDb ONE CROW"),
-                       ("PH", 128, "float16", "IDh EXzj EXz EXj EXj64 W1 W9 W0 WM")):
+for _p, _c, _d, _l in (("PF", 1, "float32", "rg rr pp rp1 ra rb p8 p32 pb wa wb wc"), ("PI", 1, "int32", "rowI rrI p8I p32I"),
+                       ("PJ", 16, "int32", "c16"), ("PG", 128, "float32", "colF IDn32 BLKs RST EXa EXb EXbn i16 WF GP"),
+                       ("PB", 128, "bfloat16", "cg cr B64 BM TRI ID16 ONE CROW WJ WC WE"),
+                       ("PH", 128, "float16", "IDh EXz W1 W9 W0 WM"), ("PA", 24, "float16", "GA")):
     for _k, _n in enumerate(_l.split()):
         VIRT[_n] = (_p, _k * _c, _c)
     _b(_p, _c * len(_l.split()), _d)
 _b("Z8I", 256, "int32", rows=8)
 _b("YZ", 256, "float32", rows=8)
 for _k in range(2):
-    for _n, _c, _d in (("MASK", NC, "bfloat16"), ("OHL", NC, "float16"), ("OHQ", NC, "float16"), ("DS", NC, "float16"), ("XS", NC, "float32"),
+    for _n, _c, _d in (("MASK", NC, "bfloat16"), ("OH0", NC, "float16"), ("OH1", NC, "float16"), ("DS0", NC, "float16"), ("XS0", NC, "float32"),
+                       ("DS1", NC, "float16"), ("XS1", NC, "float32"), ("GE", NC, "bfloat16"),
                        ("FI", NC, "int32"), ("FJ", NC, "int32"), ("OFL", NC, "uint16"), ("OFQ", NC, "uint16"), ("Z", 32 * NC, "bfloat16"),
-                       ("MX", 32 * NC, "bfloat16"), ("V", 16 * NC, "bfloat16"), ("MV", 16 * NC, "bfloat16"), ("SC", 128, "float32"), ("EC", 128, "float32"),
-                       ("RR", 8, "float32"), ("SM", 16, "bfloat16"), ("OHJ", NC, "bfloat16"),
+                       ("MX", 32 * NC, "bfloat16"), ("V", 16 * NC, "bfloat16"), ("MV", 16 * NC, "bfloat16"), ("SC", 128, "float32"),
+                       ("RR", 8, "float32"), ("SM", 32, "bfloat16"), ("PR", 32, "float32"),
                        ("OV", NC, "bfloat16"), ("IZ", NC, "bfloat16"), ("TO", 16, "uint16")):
         _b("%s_%d" % (_n, _k), _c, _d)
-    _b("ST_%d" % _k, NC, "float16", rows=16)
+    _b("ST_%d" % _k, NC, "float16", rows=8)
+    _b("SN_%d" % _k, NC, "float16", rows=8)
+    _b("SM_%dT" % _k, 32, "bfloat16")
+    _b("PR_%dT" % _k, 32, "float32")
     for _n in ("U", "K", "E", "F"):
         _b("p%s%d" % (_n, _k), 512, "float32", where="psum")
 
@@ -115,9 +119,10 @@ def plan(g, core, T, topo):
         return len(ops) - 1
 
     def ap(x):
+        p = x[5] if len(x) > 5 else 0
         if x[3] == 1:
-            return T[x[0]][0:x[4], x[1]:x[2]]
-        return T[x[0]][0:x[4], x[1]:x[2]:x[3]]
+            return T[x[0]][p:x[4], x[1]:x[2]]
+        return T[x[0]][p:x[4], x[1]:x[2]:x[3]]
 
     def width(x):
         return -(-(x[2] - x[1]) // x[3])
@@ -179,10 +184,10 @@ def plan(g, core, T, topo):
                 ops.pop()
         ops[-1]["alt"] = alt
 
-    def mm(items, start=True, stop=True):
+    def mm(items, start=True, stop=True, each=False):
         fns, rd, wr, cost = [], [], [], 0
         for k, (o, l, r) in enumerate(items):
-            fns.append(lambda o=o, l=l, r=r, k=k: g.tensor.matmul(ap(o), ap(l), ap(r), start and k == 0, stop and k == len(items) - 1))
+            fns.append(lambda o=o, l=l, r=r, k=k: g.tensor.matmul(ap(o), ap(l), ap(r), each or start and k == 0, each or stop and k == len(items) - 1))
             rd += [l, r]
             wr.append(o)
             cost += max(min(64, width(l)), width(r)) * (4 if SCRATCH[l[0]][2] == "float32" else 1) * PAR["PE"]
@@ -214,8 +219,8 @@ def plan(g, core, T, topo):
         op("G", [lambda: g.affine_select(ap(o), ap(a), pat, cmp, 0.0, base, cm)], [a], [o], 190 + 2 * width(o))
 
     def act(o, a, bias, scale):
-        op("A", [lambda: g.scalar.activation(ap(o), ap(a), AF.Identity, bias=sc(bias), scale=scale)],
-           [a] + ([bias] if isinstance(bias, tuple) else []), [o], max(64, width(o)))
+        op("A", [lambda: g.scalar.activation(ap(o), ap(a), AF.Identity, bias=sc(bias), scale=sc(scale))],
+           [a] + [x for x in (bias, scale) if isinstance(x, tuple)], [o], max(64, width(o)))
 
     H = W // 2
     dma("S", ap(B("S0I")), T.s0[:, :], [], [B("S0I")], "d_s0", 2500)
@@ -252,18 +257,35 @@ def plan(g, core, T, topo):
     act(B("BLKs"), B("B64"), 0.0, -1.0 / 64)
     act(B("IDh", 0, 16), B("IDn32", 0, 16), 0.0, -1.0)
     act(B("BM"), B("B64"), 0.0, -0.5)
-    act(B("IDb"), B("IDn32"), 0.0, -1.0)
+    act(B("ID16"), B("IDn32"), 0.0, -16.0)
     act(B("W9"), B("B64"), 0.0, -9.0 / 64)
     iota(B("CROW", rows=1), [[0, 8], [1, 16]], 9, 0)
     ms(B("ONE"), 1.0)
     ts(B("RST"), B("cr"), 0.0, OP.is_equal, float(CAP), OP.mult)
-    ts(B("c17"), B("pp"), 8.0, OP.is_lt, -17.0, OP.mult)
-    ts(B("EXj"), B("cg"), 8.0, OP.add, B("pp"), OP.is_equal)
-    act(B("EXj64"), B("EXj"), 0.0, 1.0 / 64)
-    tt(B("EXzj", rows=16), B("EXz", rows=16), B("EXj", rows=16), OP.add)
-    act(B("EXa"), B("EXz"), 0.0, 1.0 / 16)
-    act(B("EXb"), B("EXz"), 0.0, 205.0 / 16)
-    act(B("EXbn"), B("EXz"), 0.0, -205.0 / 16)
+    for x, bits in (("p8", 7), ("p32", 31)):
+        ts(B(x + "I"), B("rowI"), bits, AND)
+        cp(B(x), B(x + "I"))
+    ts(B("WJ"), B("cg"), B("p32"), OP.is_equal)
+    ts(B("wb"), B("p32"), B("p8"), OP.subtract, 16.0, OP.is_equal)
+    ts(B("wa"), B("p32"), 16.0, OP.is_lt)
+    ts(B("wc"), B("wb"), 18.5, OP.mult, B("wa"), OP.add)
+    ts(B("WC"), B("cr"), B("wb"), OP.mult, B("wc"), OP.add)
+    ts(B("WE"), B("cg"), B("p8"), OP.is_equal)
+    tt(B("WF"), B("WC"), B("WE"), OP.mult)
+    ts(B("pb"), B("pp"), B("p32"), OP.subtract)
+    ts(B("P4"), B("colF", 0, 128, 32), B("pb"), OP.is_equal)
+    for x in ("WJ", "WF"):
+        for a in range(4):
+            act(B(x + "4", 128 * a, 128 * a + 128), B(x), 0.0, B("P4", a, a + 1))
+    for k, f in enumerate((-1.0, 1.0, -1.0)):
+        act(B("GA", 8 * k, 8 * k + 8), B("B64", 0, 128, 16), 0.0, f / 64)
+    act(B("GP", 0, 8), B("B64", 0, 128, 16), 0.0, 1.0 / 64)
+    for c in range(2):
+        iota(B("SM_%d" % c, 24, 32), [[0, 8]], 0, 0)
+        iota(B("PR_%d" % c, 24, 32), [[0, 8]], 0, 0)
+    act(B("EXa"), B("EXz"), 0.0, 1.0)
+    act(B("EXb"), B("EXz"), 0.0, 205.0)
+    act(B("EXbn"), B("EXz"), 0.0, -205.0)
     act(B("ra"), B("rr"), -2.0, 16.0)
     act(B("rb"), B("rr"), -1.0, 16.0)
     ts(B("i16", 0, 16), B("c16"), B("rr"), OP.add)
@@ -308,19 +330,28 @@ def plan(g, core, T, topo):
         select(B(x, 16, 144), B(src), [[0, 8], [-1, 16]], OP.is_ge, top, 0)
     iota(B("KT", rows=1), [[256, 8]], 0, 0)
 
-    def lists(t, c, u, zz, kreg, oh, ws, off, between=None):
+    def lists(t, c, u, zz, new):
         D = B("D%d" % (t % 2), c * NC, c * NC + NC)
-        M, DS, XS, FI, FJ = [B("%s_%d" % (x, c)) for x in ("MASK", "DS", "XS", "FI", "FJ")]
-        cnt, f = B("pK%d" % c, kreg, kreg + NC), B("pF%d" % c, kreg, kreg + NC)
-        tt(M, B("SROT%d" % (t % 2), c * NC, c * NC + NC), zz, OP.is_le if between else OP.is_lt)
+        M, oh, DS, XS = [B(x + "_%d" % c) for x in ("MASK", "OH%d" % new, "DS%d" % new, "XS%d" % new)]
+        cnt, f, xp = B("pK%d" % c, new * NC, new * NC + NC), B("pF%d" % c, new * NC, new * NC + NC), B("pU%d" % c, 256, 384)
+        tt(M, B("SROT%d" % (t % 2), c * NC, c * NC + NC), zz, OP.is_le if new else OP.is_lt)
         mm([(cnt, B("B64"), M)])
-        if between:
-            between()
+        pre = PAR["XP"] and not new
+        if pre:
+            tt(xp, u, D, OP.mult)
         ts(oh, cnt, 64.0, OP.max, B("rp1"), OP.is_equal)
         scan(DS, oh, D, 0.0, OP.max, OP.mult)
-        tt(XS, u, DS, OP.mult)
-        mm([(f, B(x), DS) for x in ws] + [(f, B("W0"), oh)], True, False)
-        mm([(f, B("BLKs"), XS)], False, True)
+        if pre:
+            tt(XS, xp, oh, OP.mult)
+        else:
+            tt(XS, u, DS, OP.mult)
+        if not new:
+            ts(B("GE_%d" % c), cnt, B("rp1"), OP.is_le)
+        mm([(f, B(x), DS) for x in ["W1", "W9"][:1 + new]] + [(f, B("W0"), oh)], True, False)
+        mm([(f, B("BLKs"), XS)], False, not new)
+
+    def offsets(c, f, off):
+        FI, FJ = B("FI_%d" % c), B("FJ_%d" % c)
         w = PAR["TAIL"]
         parts = [[(x[0], x[1] + a, x[1] + a + w) + x[3:] for x in (f, FI, FJ, off)] for a in range(0, NC, w)]
         for x in parts:
@@ -345,10 +376,18 @@ def plan(g, core, T, topo):
             mm([(ua, B("B64"), iz)], False, True)
             z1 = B("pK%d" % c, 384, 512)
             mm([(z1, B("EXz", rows=8), st), (z1, B("B64"), iz)])
-            lists(t, c, ua, z1, 0, B("OHL_%d" % c), ["W1"], B("OFL_%d" % c))
-            tag[0] = "B%d" % c
-            mm([(B("pK%d" % c, 256, 384, rows=16), B("IDh", 0, 16, rows=8), st), (B("pK%d" % c, 256, 384, rows=8), B("B64", 0, 128, 16), iz)], True, False)
-            mm([(ub, B("IDn32"), S)], True, False)
+            lists(t, c, ua, z1, 0)
+            offsets(c, B("pF%d" % c, 0, NC), B("OFL_%d" % c))
+            tag[0] = "H%d" % c
+            rows, sn = B("pK%d" % c, 256, 384, rows=8), B("SN_%d" % c)
+            mm([(rows, B("IDh", 0, 8, rows=8), st), (rows, B("B64", 0, 128, 16), iz)])
+            ts(sn, rows, -17.0, OP.add, -float(ZC), OP.max)
+            mm([(z1, B("EXz", rows=8), sn)])
+            mm([(ub, B("IDn32"), S), (ub, B("EXz", rows=8), sn)])
+            lists(t, c, ub, z1, 1)
+            x = "pK%d" % c
+            mm([(B(x, 256, 280), B("DS0_%d" % c), B("GA")), (B(x, 272, 280), B("DS1_%d" % c), B("GA", 8, 16)),
+                (B(x, 264, 272), B("XS0_%d" % c), B("BLKs", 0, 128, 16)), (B(x, 264, 272), B("XS1_%d" % c), B("GP", 0, 8))])
             tag[0] = "F%d" % c
             for m in range(16):
                 either("V" if m < 12 or t == 0 else "G", "VAG", lambda q: cp(B("Z_%d" % c, 2 * m, 32 * NC, 32), tm(c, m % 2), q))
@@ -370,38 +409,40 @@ def plan(g, core, T, topo):
             for j0 in range(0, 15, 3):
                 mm([(B(E, j, 128, 16), B(MX, 2 * (j + a) + 1 + j % 2, 32 * NC, 32), B("B64", 0, 128, 16)) for j in range(j0, j0 + 3) for a in range(2)], False, j0 == 12)
             tag[0] = "C%d" % c
-            st, sm = B("ST_%d" % c), "SM_%d" % c
-            rows, ub = B(K, 256, 384, rows=16), B("pU%d" % c, NC, 2 * NC)
+            st, sm, pr = B("ST_%d" % c), "SM_%d" % c, "PR_%d" % c
             scan(B("SC_%d" % c), B("RST"), B(E, 0, 128), float(CAP), OP.max, OP.min)
             key = B("SC_%d" % c, 14, 128, 16)
             ts(B("RR_%d" % c), key, R16, OP.add, R16, OP.subtract)
-            ts(B(sm, 0, 8), key, float(CAP - 4), OP.is_lt, 16.0, OP.mult)
-            tt(B(sm, 8, 16), key, B("RR_%d" % c), OP.subtract)
-            mm([(rows, B(sm), B("IDb"))], False, True)
-            ts(st, rows, B("c17"), OP.add, -float(ZC), OP.max)
-            zz, dl, gd = B(E, 0, 128), B(E, 384, 512), B(E, 256, 384)
-            mm([(zz, B("EXz", rows=8), B("ST_%d" % c, rows=8))])
-            mm([(dl, B("EXj64", rows=16), st)])
-            tag[0] = "Q%d" % c
-            mm([(ub, B("EXzj", rows=16), st)], False, True)
+            for a in (8, 16):
+                ts(B(sm, a, a + 8), key, float(CAP - 4), OP.is_lt)
+            tt(B(sm, 0, 8), key, B("RR_%d" % c), OP.subtract)
 
-            def starts():
-                tag[0] = "S%d" % c
-                tt(B("OHJ_%d" % c), dl, B("OHL_%d" % c), OP.mult)
-                mm([(gd, B("TRI"), B("OHJ_%d" % c))])
-                tt(B("SX%d" % t, 16 + i0, 16 + i0 + NC), B("SROT%d" % P, i0, i0 + NC), gd, OP.subtract)
-                lo, hi = (0, 16 + NC) if c == 0 else (16 + NC, SW)
-                sr = B("SR%d" % (t + 1), lo, hi)
-                s = send(T.cores[(rank - 1) % n], sr, B("SX%d" % t, lo, hi), "rs%d%d" % (t + 1, c), "ls%d%d" % (t + 1, c))
-                recv(sr, engines(topo, T.cores[(rank + 1) % n], core), "rs%d%d" % (t + 1, c), PAR["RECV"], s)
-                tag[0] = "Q%d" % c
-            lists(t, c, ub, zz, NC, B("OHQ_%d" % c), ["W1", "W9"], B("OFQ_%d" % c), starts)
+            def spread(o, w, x, start):
+                op("V", [lambda: g.vector.transpose(ap(B(x + "T")), ap(B(x)))], [B(x)], [B(x + "T")], 64)
+                mm([((o[0], o[1] + a, o[1] + a + 32) + o[3:], B(w + "4", 4 * a, 4 * a + 128), B(x + "T")) for a in range(0, NC, 32)], start, True, start)
+            tag[0] = "S%d" % c
+            dl, gd = B(E, 384, 512), B(E, 256, 384)
+            spread(dl, "WJ", sm, True)
+            tt(gd, dl, B("GE_%d" % c), OP.mult)
+            tt(B("SX%d" % t, 16 + i0, 16 + i0 + NC), B("SROT%d" % P, i0, i0 + NC), gd, OP.subtract)
+            lo, hi = (0, 16 + NC) if c == 0 else (16 + NC, SW)
+            sr = B("SR%d" % (t + 1), lo, hi)
+            s = send(T.cores[(rank - 1) % n], sr, B("SX%d" % t, lo, hi), "rs%d%d" % (t + 1, c), "ls%d%d" % (t + 1, c))
+            recv(sr, engines(topo, T.cores[(rank + 1) % n], core), "rs%d%d" % (t + 1, c), PAR["RECV"], s)
+            tag[0] = "Q%d" % c
+            tt(B(pr, 0, 24), B(sm, 0, 24), B(K, 256, 280), OP.mult)
+            spread(B("pF%d" % c, NC, 2 * NC), "WF", pr, False)
+            offsets(c, B("pF%d" % c, NC, 2 * NC), B("OFQ_%d" % c))
+            tag[0] = "R%d" % c
+            rows = B(K, 384, 512, rows=8)
+            mm([(rows, B("IDh", 0, 8, rows=8), st), (rows, B("B64", 0, 128, 16), B("IZ_%d" % c)), (rows, B(sm, 8, 16), B("ID16"))])
+            ts(st, rows, -17.0, OP.add, -float(ZC), OP.max)
         tag[0] = "X"
         send_logs(t + 1)
         if not last:
             tag[0] = "P"
             an, own, far = B("pU0", 256, 272, rows=8), B("SX%d" % (t + 1), 0, 16, rows=8), B("SR%d" % (t + 1), 0, 16, rows=8)
-            mm([(an, B("SM_%d" % c, 0, 8), B("ONE", 0, 16)) for c in range(2)])
+            mm([(an, B("SM_%d" % c, 8, 16), B("ONE", 0, 16)) for c in range(2)])
             cp(own, an)
             mm([(B("pU0", 272, 304), B("IDn32"), B("NCT", 0, 32)), (B("pU0", 288, 304), B("EXbn", rows=8), far)], True, False)
             mm([(B("pU0", 272, 288), B("EXa", rows=8), own), (B("pU0", 288, 304), B("EXb", rows=8), own)], False, True)
@@ -563,21 +604,55 @@ def order(ops):
     blocks = {}
     for k in range(n):
         blocks.setdefault(ops[k]["blk"], []).append(k)
+    same = {}
+    for b, l in blocks.items():
+        for i, k in enumerate(l):
+            same.setdefault((b[0], i, len(l)), []).append(k)
+    like = {k: l for l in same.values() for k in l}
     blocks = list(blocks.values())
+
+    def chain(t0):
+        before = {(ops[k]["q"], round(t0[k] + busy[k], 3)): k for k in range(n) if busy[k]}
+        k, held = max(range(n), key=lambda k: t0[k] + ops[k]["cost"]), []
+        while t0[k] > 0:
+            x = [x for x, d in lag[k].items() if t0[x] + d > t0[k] - 1e-3]
+            if x:
+                k = x[0]
+            else:
+                held.append((k, before[(ops[k]["q"], round(t0[k], 3))]))
+                k = held[-1][1]
+        return held
     sig = tuple((o["blk"], o["kind"], o["sem"]) for o in ops)
     cur = best = DONE.get(sig) or packed([-w for w in way]) + ([ops[k]["q"] for k in free],)
     for it in range(0 if sig in DONE else PAR["TURNS"]):
         key = list(cur[1])
-        if rnd() < 0.5:
+        r = rnd()
+        if r < PAR["MOVE"][0]:
+            held = chain(cur[1])
+            for _ in range(1 + int(2 * rnd())):
+                k, p = held[int(rnd() * len(held))]
+                k = p if "alt" in ops[p] and rnd() < 0.5 else k
+                if "alt" in ops[k] and rnd() < 0.7:
+                    qs = [q for q in sorted(ops[k]["alt"]) if q != ops[k]["q"]]
+                    assign(k, qs[int(rnd() * len(qs))])
+                elif rnd() < 0.5:
+                    key[k] = key[p] - 1 - 300 * rnd()
+                else:
+                    key[p] = key[k] + 1 + 1000 * rnd()
+        elif r < PAR["MOVE"][1]:
             for _ in range(1 + int(2 * rnd())):
                 k = free[int(rnd() * len(free))]
                 qs = sorted(ops[k]["alt"])
-                assign(k, qs[int(rnd() * len(qs))])
+                q = qs[int(rnd() * len(qs))]
+                for x in (like[k] if rnd() < 0.5 else [k]):
+                    assign(x, q)
         else:
             for _ in range(1 + int(3 * rnd())):
                 d = (rnd() - 0.5) * (600, 2000, 6000)[int(3 * rnd())]
-                for k in blocks[int(rnd() * len(blocks))]:
-                    key[k] += d
+                b = blocks[int(rnd() * len(blocks))]
+                for k in b:
+                    for x in (like[k] if it % 2 else [k]):
+                        key[x] += d
         new = packed(key) + ([ops[k]["q"] for k in free],)
         if new[0] <= cur[0] + PAR["HEAT"] * rnd() * (1 - it / PAR["TURNS"]):
             cur = new

@@ -7,21 +7,23 @@ from concourse.mybir import dt, AluOpType, AxisListType, ActivationFunctionType
 OP = AluOpType
 AF = ActivationFunctionType
 NV, W, ZC, TH, TH2 = 4, 4096, 1536, 1082, 820
+NB = 144
 NC = 128
-WX = W
+WX = W + 16
 SW = 16 + 256
 R16 = 1.5 * 2 ** 27
-R1 = 1.5 * 2 ** 23
-CAP = 32 * (TH - 1) + 32
+R4096 = 1.5 * 2 ** 35
+CAP = 32 * (TH - 1) + 224
 PAR = dict(
     SYNC=100, PE=0.5, GN=1.56, RECV=2500, SEND=1000,
     YS=["AAAA", "AAAA"],
     VS=["AAAA", "AAAA"],
     TQ="AA",
     FILL=["VVVVVVVVVVGGGGGG", "VVVVVVVVVVGGGGGG"],
-    BI={}, TURNS=3000, TAIL=64, SEED=1, HEAT=500, LOG=(20000, 34000, 48000), XP=1, MOVE=(0.5, 0.7),
+    BI={}, TURNS=3000, TAIL=64, SEED=1, HEAT=500, LOG=(20000, 34000, 48000), XP=1, MW=512, BAR=2500, GF=12, SL=(1, 0), LOAD=(2000, 4000, 5800), PICK=[["AAAA"] * 4] * 4, FINE=12, WARM=600, FAR=24, COPY=0.05, TIED=0.3, RND=(1, 1), OFFQ="AV", DQ="AV", EM=((0, 96), (96, 128)), MOVE=(0.5, 0.7),
 )
-PAR.update(SYNC=290, SEND=1200, RECV=1800, LOG=(19000, 33000, 47000), TURNS=2500, HEAT=400, MOVE=(0.7, 0.85))
+PAR.update(SYNC=290, SEND=1200, RECV=1800, LOG=(19000, 33000, 47000), TURNS=9000, HEAT=1000, MOVE=(0.6, 0.75), EM=[((0, 128),)] * 2, RND=(1, 0), FINE=1, WARM=300,
+           SEED=5, TIED=0.6, COPY=0.07, BAR=1000)
 PAR.update({'YS': ['AAAV', 'AAVA'], 'VS': ['AAAA', 'AVAA'], 'TQ': 'AA', 'FILL': ['VVVVVVVVVAAAAGGG', 'VVVVVVVAAAAGGGGG'], 'BI': {'N1': -6577, 'P': 10849, 'C0': -18109, 'Y0': 29548, 'Q0': 35775, 'L0': 13704, 'B1': 36812, 'Z': 24811, 'Y1': -3215, 'M0': -37336, 'L1': -10511, 'V0': 72407, 'V1': 3110, 'Q1': 34840, 'F1': -67990, 'D1': -9648, 'B0': -34734, 'C1': -90901, 'c': -20085, 'X': 44139, 'F0': -56967, 'S0': -49337, 'E1': -42699, 'S1': 26460, 'T0': 3205, 'M1': -40204, 'D0': -15280, 'N0': 48304, 'E0': -62395, 'T1': -16593}})
 
 SCRATCH = {}
@@ -39,14 +41,14 @@ for _v in range(4):
     _b("SR%d" % (_v + 1), SW, "float32")
 for _n, _c, _d in (("S0I", 256, "int32"), ("TL", 512, "bfloat16"), ("TT", 512, "bfloat16"), ("YSO", 256, "float32"),
                    ("SROT0", 256, "float32"), ("SROT1", 256, "float32"), ("D0", 256, "float16"), ("D1", 256, "float16"),
-                   ("SEL", 144, "bfloat16"), ("WN", 144, "bfloat16"), ("NCT", 48, "float32"), ("LI", 32, "int32"), ("LJ", 32, "int32"),
-                   ("LOS", 32, "uint16"), ("KT", 8, "bfloat16"), ("WJ4", 512, "bfloat16"), ("WF4", 512, "float32"), ("P4", 4, "float32")):
+                   ("WN4", 512, "bfloat16"), ("NCT", 48, "float32"), ("LI", 32, "int32"), ("LJ", 32, "int32"),
+                   ("LOS", 32, "uint16"), ("KT", 8, "bfloat16"), ("WJ4", 512, "bfloat16"), ("WF4", 512, "float32"), ("WF4n", 512, "float32"), ("P4", 4, "float32")):
     _b(_n, _c, _d)
 VIRT = {}
-for _p, _c, _d, _l in (("PF", 1, "float32", "rg rr pp rp1 ra rb p8 p32 pb wa wb wc"), ("PI", 1, "int32", "rowI rrI p8I p32I"),
-                       ("PJ", 16, "int32", "c16"), ("PG", 128, "float32", "colF IDn32 BLKs RST EXa EXb EXbn i16 WF GP"),
-                       ("PB", 128, "bfloat16", "cg cr B64 BM TRI ID16 ONE CROW WJ WC WE"),
-                       ("PH", 128, "float16", "IDh EXz W1 W9 W0 WM"), ("PA", 24, "float16", "GA")):
+for _p, _c, _d, _l in (("PF", 1, "float32", "rg rr pp rp1 rp2 rp4 ra rb p8 p32 pb wa wb wc"), ("PI", 1, "int32", "rowI rrI p8I p32I"),
+                       ("PJ", 16, "int32", "c16"), ("PG", 128, "float32", "colF IDn32 BLKs BLKsn EXa EXb EXbn i16 WF GP"),
+                       ("PB", 128, "bfloat16", "cg cr B64 BM MROW DROW IDbn ID16 ONE CROW WJ WC WE BE RM"),
+                       ("PH", 128, "float16", "IDh EXz W1 W9 W0 WM WM2 W1n W9n W0n"), ("PA", 24, "float16", "GA")):
     for _k, _n in enumerate(_l.split()):
         VIRT[_n] = (_p, _k * _c, _c)
     _b(_p, _c * len(_l.split()), _d)
@@ -58,14 +60,17 @@ for _k in range(2):
                        ("FI", NC, "int32"), ("FJ", NC, "int32"), ("OFL", NC, "uint16"), ("OFQ", NC, "uint16"), ("Z", 32 * NC, "bfloat16"),
                        ("MX", 32 * NC, "bfloat16"), ("V", 16 * NC, "bfloat16"), ("MV", 16 * NC, "bfloat16"), ("SC", 128, "float32"),
                        ("RR", 8, "float32"), ("SM", 32, "bfloat16"), ("PR", 32, "float32"),
-                       ("OV", NC, "bfloat16"), ("IZ", NC, "bfloat16"), ("TO", 16, "uint16")):
+                       ("NS", 32, "bfloat16"), ("NZ", 144, "bfloat16"), ("TO", 16, "uint16")):
         _b("%s_%d" % (_n, _k), _c, _d)
     _b("ST_%d" % _k, NC, "float16", rows=8)
     _b("SN_%d" % _k, NC, "float16", rows=8)
     _b("SM_%dT" % _k, 32, "bfloat16")
     _b("PR_%dT" % _k, 32, "float32")
+    _b("NS_%dT" % _k, 32, "bfloat16")
+    SCRATCH["OV_%d" % _k] = ("sbuf", [128, 8, 16], "bfloat16")
     for _n in ("U", "K", "E", "F"):
         _b("p%s%d" % (_n, _k), 512, "float32", where="psum")
+    SCRATCH["pE%d" % _k] = ("psum", [128, 32, 16], "float32")
 
 SEMAPHORES = ["sV", "sA", "sP", "sG", "h0", "h1", "lh0", "lh1"]
 SEMAPHORES += ["d_" + n for n in ("s0", "cf", "z0", "t0", "xa", "xb", "ys", "yz", "ya0", "ya1", "yb0", "yb1")]
@@ -73,6 +78,14 @@ for _v in range(1, 4):
     SEMAPHORES += ["%s%d" % (n, _v) for n in ("rca", "rla", "rlb", "lca", "lla", "llb", "lcf", "llf")]
 for _v in range(1, 5):
     SEMAPHORES += ["%s%d%d" % (n, _v, c) for n in ("rs", "ls") for c in range(2)]
+
+
+def pieces(s):
+    out, lo = [], 0
+    for x in s:
+        out.append((x.upper(), lo, lo + (32 if x.isupper() else 16)))
+        lo = out[-1][2]
+    return out
 
 
 def engines(topo, src, dst, upper=0):
@@ -120,6 +133,14 @@ def plan(g, core, T, topo):
 
     def ap(x):
         p = x[5] if len(x) > 5 else 0
+        if len(SCRATCH[x[0]][1]) == 3:
+            if len(x) > 6:
+                return T[x[0]][p:x[4], x[1] // 16:x[2] // 16, x[6]:x[6] + 2]
+            if x[3] == 16:
+                return T[x[0]][p:x[4], x[1] // 16:x[2] // 16, x[1] % 16]
+            if x[2] - x[1] < 16:
+                return T[x[0]][p:x[4], x[1] // 16, x[1] % 16:x[1] % 16 + x[2] - x[1]]
+            return T[x[0]][p:x[4], x[1] // 16:x[2] // 16, :]
         if x[3] == 1:
             return T[x[0]][p:x[4], x[1]:x[2]]
         return T[x[0]][p:x[4], x[1]:x[2]:x[3]]
@@ -175,6 +196,11 @@ def plan(g, core, T, topo):
                 f = lambda: g.scalar.activation(ap(o), ap(win).indirect(ap(off)), AF.Identity, bias=bias, scale=scale)
         op(q, [f], [win, off], [o], 60 + PAR["GN"] * width(o), cls="gather")
 
+    def join(k):
+        for o in [ops.pop() for _ in range(k - 1)]:
+            for x in ("fns", "r", "w", "cost"):
+                ops[-1][x] += o[x]
+
     def either(first, qs, make):
         alt = {}
         for q in [x for x in qs if x != first] + [first]:
@@ -215,20 +241,21 @@ def plan(g, core, T, topo):
             f = [lambda: g.iota(ap(o), pat, base, cm, allow_small_or_imprecise_dtypes=True)]
         op("G", f, [], [o], 150 + 2 * width(o))
 
-    def select(o, a, pat, cmp, base, cm):
-        op("G", [lambda: g.affine_select(ap(o), ap(a), pat, cmp, 0.0, base, cm)], [a], [o], 190 + 2 * width(o))
+    def select(o, a, pat, cmp, base, cm, fill=0.0):
+        op("G", [lambda: g.affine_select(ap(o), ap(a), pat, cmp, fill, base, cm)], [a], [o], 190 + 2 * width(o))
 
-    def act(o, a, bias, scale):
-        op("A", [lambda: g.scalar.activation(ap(o), ap(a), AF.Identity, bias=sc(bias), scale=sc(scale))],
+    def act(o, a, bias, scale, fn=AF.Identity):
+        op("A", [lambda: g.scalar.activation(ap(o), ap(a), fn, bias=sc(bias), scale=sc(scale))],
            [a] + [x for x in (bias, scale) if isinstance(x, tuple)], [o], max(64, width(o)))
 
     H = W // 2
-    dma("S", ap(B("S0I")), T.s0[:, :], [], [B("S0I")], "d_s0", 2500)
-    dma("A", ap(B("CF0")), T.cf[:, :], [], [B("CF0")], "d_cf", 2500)
-    dma("A", ap(B("Z8I")), T.z0[:, :], [], [B("Z8I")], "d_z0", 2500)
-    dma("S", ap(B("XL0", 0, H)), T.xl[:, 0:H], [], [B("XL0", 0, H)], "d_xa", 5500)
-    dma("S", ap(B("XL0", H, W)), T.xl[:, H:W], [], [B("XL0", H, W)], "d_xb", 7500)
-    dma("A", ap(B("TL")), T.t0[:, :], [], [B("TL")], "d_t0", 3500)
+    ld = PAR["LOAD"]
+    dma("S", ap(B("S0I")), T.s0[:, :], [], [B("S0I")], "d_s0", ld[0])
+    dma("A", ap(B("Z8I")), T.z0[:, :], [], [B("Z8I")], "d_z0", ld[0])
+    dma("A", ap(B("CF0")), T.cf[:, :], [], [B("CF0")], "d_cf", ld[0])
+    dma("S", ap(B("XL0", 0, H)), T.xl[:, H:W], [], [B("XL0", 0, H)], "d_xa", ld[1])
+    dma("S", ap(B("XL0", H, WX)), T.xl[:, 0:WX - H], [], [B("XL0", H, WX)], "d_xb", ld[2])
+    dma("A", ap(B("TL")), T.t0[:, :], [], [B("TL")], "d_t0", ld[1])
     AND = OP.bitwise_and
     iota(B("rowI"), [[0, 1]], 0, 1)
     iota(B("c16"), [[16, 16]], 0, 0)
@@ -246,22 +273,30 @@ def plan(g, core, T, topo):
     ts(B("IDn32"), B("colF"), B("pp"), OP.is_equal, -1.0, OP.mult)
     ts(B("EXz"), B("cg"), B("pp"), OP.is_equal)
     for c in range(2):
-        ms(B("IZ_%d" % c), 1.0 / 64)
-        ts(B("ST_%d" % c, rows=8), B("Z8I", c * NC, c * NC + NC), -float(ZC + 15), OP.add)
+        ts(B("ST_%d" % c, rows=8), B("Z8I", c * NC, c * NC + NC), 1.0 - ZC, OP.add)
     gather("V", B("SROT0"), B("S0I"), B("LOS", 0, 16), 1.0, -float(ZC))
     gather("V", B("D0"), B("CF0"), B("LOS", 0, 16), -2.0, -1.0)
     act(B("rp1"), B("rr"), 64.0, 64.0)
+    act(B("rp2"), B("rr"), -14.0 * 64, 128.0)
+    act(B("rp4"), B("rr"), 4.0 * 96, 256.0)
+    for k in range(2):
+        ms(B("RM", 64 * k, 64 * k + 64, rows=1), (1 - 2 * k) * R4096)
     act(B("WM"), B("cr"), -9.5 / 64, -1.0 / 64)
-    tt(B("W1"), B("WM"), B("B64"), OP.mult)
+    scan(B("W1"), B("B64"), B("WM"), 0.0, OP.max, OP.mult)
     act(B("W0"), B("B64"), 0.0, -18.5 / 64)
     act(B("BLKs"), B("B64"), 0.0, -1.0 / 64)
+    if max(PAR["RND"]):
+        for x in ("W1", "W0", "BLKs"):
+            act(B(x + "n"), B(x), 0.0, -1.0)
     act(B("IDh", 0, 16), B("IDn32", 0, 16), 0.0, -1.0)
     act(B("BM"), B("B64"), 0.0, -0.5)
     act(B("ID16"), B("IDn32"), 0.0, -16.0)
-    act(B("W9"), B("B64"), 0.0, -9.0 / 64)
-    iota(B("CROW", rows=1), [[0, 8], [1, 16]], 9, 0)
+    act(B("WM2"), B("cr"), -18.5 / 64, -1.0 / 64)
+    scan(B("W9"), B("B64"), B("WM2"), 0.0, OP.max, OP.mult)
+    iota(B("CROW", rows=1), [[0, 8], [1, 16]], 201, 0)
+    select(B("CROW", rows=1), B("CROW", rows=1), [[0, 8], [-1, 16]], OP.is_ge, 14, 0, float(CAP))
+    select(B("BE"), B("BM"), [[0, 8], [-1, 16]], OP.is_ge, 14, 0)
     ms(B("ONE"), 1.0)
-    ts(B("RST"), B("cr"), 0.0, OP.is_equal, float(CAP), OP.mult)
     for x, bits in (("p8", 7), ("p32", 31)):
         ts(B(x + "I"), B("rowI"), bits, AND)
         cp(B(x), B(x + "I"))
@@ -277,6 +312,9 @@ def plan(g, core, T, topo):
     for x in ("WJ", "WF"):
         for a in range(4):
             act(B(x + "4", 128 * a, 128 * a + 128), B(x), 0.0, B("P4", a, a + 1))
+    if PAR["RND"][1]:
+        act(B("W9n"), B("W9"), 0.0, -1.0)
+        act(B("WF4n"), B("WF4"), 0.0, -1.0)
     for k, f in enumerate((-1.0, 1.0, -1.0)):
         act(B("GA", 8 * k, 8 * k + 8), B("B64", 0, 128, 16), 0.0, f / 64)
     act(B("GP", 0, 8), B("B64", 0, 128, 16), 0.0, 1.0 / 64)
@@ -286,8 +324,8 @@ def plan(g, core, T, topo):
     act(B("EXa"), B("EXz"), 0.0, 1.0)
     act(B("EXb"), B("EXz"), 0.0, 205.0)
     act(B("EXbn"), B("EXz"), 0.0, -205.0)
-    act(B("ra"), B("rr"), -2.0, 16.0)
-    act(B("rb"), B("rr"), -1.0, 16.0)
+    act(B("ra"), B("rr"), NB - 2.0, 16.0)
+    act(B("rb"), B("rr"), NB - 1.0, 16.0)
     ts(B("i16", 0, 16), B("c16"), B("rr"), OP.add)
     for k, f in enumerate((5.0, 1.0, 205.0)):
         act(B("NCT", 16 * k, 16 * k + 16), B("i16", 0, 16), 0.0, -f)
@@ -306,7 +344,7 @@ def plan(g, core, T, topo):
                 for k in range(2):
                     x = B("XL0", k * H // 2, (k + 1) * H // 2)
                     send(helper(T, topo, rank), x, x, "h%d" % k, "lh%d" % k, 1)
-                send(dst, B("XL%d" % v, H, W), B("XL0", H, W), "rlb%d" % v, "llb%d" % v)
+                send(dst, B("XL%d" % v, H, WX), B("XL0", H, WX), "rlb%d" % v, "llb%d" % v)
         if 0 < t < NV - 1 and way_of(T, topo, (rank + t) % n, t + 1) == "on":
             dst = T.cores[(rank - 1) % n]
             send(dst, B("CF%d" % (t + 1)), B("CF%d" % t), "rca%d" % (t + 1), "lcf%d" % t, 1)
@@ -318,44 +356,78 @@ def plan(g, core, T, topo):
         if way_of(T, topo, own, v) == "far":
             recv(B("CF%d" % v), engines(topo, T.cores[own], core), "rca%d" % v, at - 4000)
             recv(B("XL%d" % v, 0, H), 2 * engines(topo, helper(T, topo, own), core), "rla%d" % v, at)
-            recv(B("XL%d" % v, H, W), engines(topo, T.cores[own], core), "rlb%d" % v, at)
+            recv(B("XL%d" % v, H, WX), engines(topo, T.cores[own], core), "rlb%d" % v, at)
         else:
             e = engines(topo, T.cores[(rank + 1) % n if way_of(T, topo, own, v) == "on" else own], core, 1)
             recv(B("CF%d" % v), e, "rca%d" % v, at - 4000)
             recv(B("XL%d" % v), e, "rla%d" % v, at)
     send_logs(0)
-    select(B("TRI"), B("B64"), [[1, 128]], OP.is_ge, 0, -1)
-    for x, src, top in (("SEL", "B64", 0), ("WN", "BM", 1)):
-        iota(B(x, 0, 16), [[0, 16]], 0, 0)
-        select(B(x, 16, 144), B(src), [[0, 8], [-1, 16]], OP.is_ge, top, 0)
+    iota(B("MROW"), [[0, 8], [-1, 16]], NB, 0)
+    iota(B("DROW", rows=1), [[0, 128]], NB - 16 - 32 * TH2, 0)
+    select(B("DROW", rows=1), B("DROW", rows=1), [[0, 8], [1, 16]], OP.is_gt, 0, 0, NB - 16.0)
+    for c in range(2):
+        iota(B("NS_%d" % c, 8, 32), [[0, 24]], 0, 0)
+        iota(B("NZ_%d" % c), [[0, 144]], 0, 0)
+    act(B("WN4"), B("WJ4"), 0.0, -1.0)
+    act(B("IDbn"), B("IDn32"), 0.0, 1.0)
     iota(B("KT", rows=1), [[256, 8]], 0, 0)
 
     def lists(t, c, u, zz, new):
         D = B("D%d" % (t % 2), c * NC, c * NC + NC)
         M, oh, DS, XS = [B(x + "_%d" % c) for x in ("MASK", "OH%d" % new, "DS%d" % new, "XS%d" % new)]
         cnt, f, xp = B("pK%d" % c, new * NC, new * NC + NC), B("pF%d" % c, new * NC, new * NC + NC), B("pU%d" % c, 256, 384)
-        tt(M, B("SROT%d" % (t % 2), c * NC, c * NC + NC), zz, OP.is_le if new else OP.is_lt)
+        if new:
+            act(M, u, 0.5, 1.0, AF.Sign)
+        else:
+            tt(M, B("SROT%d" % (t % 2), c * NC, c * NC + NC), zz, OP.is_lt)
         mm([(cnt, B("B64"), M)])
         pre = PAR["XP"] and not new
         if pre:
             tt(xp, u, D, OP.mult)
-        ts(oh, cnt, 64.0, OP.max, B("rp1"), OP.is_equal)
+        if new:
+            ts(oh, cnt, -14.0 * 64, OP.max, B("rp2"), OP.is_equal)
+        else:
+            ts(oh, cnt, 64.0, OP.max, B("rp1"), OP.is_equal)
         scan(DS, oh, D, 0.0, OP.max, OP.mult)
         if pre:
             tt(XS, xp, oh, OP.mult)
         else:
             tt(XS, u, DS, OP.mult)
         if not new:
-            ts(B("GE_%d" % c), cnt, B("rp1"), OP.is_le)
-        mm([(f, B(x), DS) for x in ["W1", "W9"][:1 + new]] + [(f, B("W0"), oh)], True, False)
-        mm([(f, B("BLKs"), XS)], False, not new)
+            ge = B("GE_%d" % c)
+            either("A", "AV", lambda q: ts(ge, cnt, B("rp1"), OP.is_le) if q == "V" else act(ge, cnt, B("rp4"), -4.0, AF.Sigmoid))
+        if not PAR["RND"][new]:
+            mm([(f, B(("W1", "W9")[new]), DS), (f, B("W0"), oh)], True, False)
+            mm([(f, B("BLKs"), XS)], False, not new)
+            return
+        for h in range(2):
+            mm(terms(c, new, h, "n")[:2], True, False)
+        for h in range(2):
+            if new:
+                mm(terms(c, new, h, "n")[2:], False, False)
+            else:
+                mm(terms(c, new, h, "n")[2:] + rounded(c, h) + terms(c, new, h, "")[::-1], False, True)
+
+    def half(c, h):
+        return B(("pF%d", "pU%d")[h] % c, 256 * h, 256 * h + 64)
+
+    def terms(c, new, h, s):
+        return [(half(c, h), B(w + s), B(x % (new, c), 64 * h, 64 * h + 64)) for w, x in ((("W1", "W9")[new], "DS%d_%d"), ("W0", "OH%d_%d"), ("BLKs", "XS%d_%d"))]
+
+    def rounded(c, h):
+        return [(half(c, h), B("ONE", rows=1), B("RM", 64 * k, 64 * k + 64, rows=1)) for k in range(2)]
+
+    def rest(c, off):
+        for h in range(2):
+            o, r = (off[0], 64 * h, 64 * h + 64) + off[3:], half(c, h)
+            either("V", PAR["OFFQ"], lambda q: ts(o, r, float(H), OP.add) if q == "V" else act(o, r, float(H), 1.0))
 
     def offsets(c, f, off):
         FI, FJ = B("FI_%d" % c), B("FJ_%d" % c)
         w = PAR["TAIL"]
         parts = [[(x[0], x[1] + a, x[1] + a + w) + x[3:] for x in (f, FI, FJ, off)] for a in range(0, NC, w)]
         for x in parts:
-            cp(x[1], x[0])
+            ts(x[1], x[0], float(H), OP.add)
         for x in parts:
             ts(x[2], x[1], W - 1, AND)
             cp(x[3], x[2])
@@ -369,49 +441,65 @@ def plan(g, core, T, topo):
             return B("TL", 256 * a + NC * c, 256 * a + NC * c + NC) if t == 0 else B("TT", 256 * c + NC * a, 256 * c + NC * a + NC)
         for c in range(2):
             tag[0] = "L%d" % c
-            S, st, iz = B("SROT%d" % P, c * NC, c * NC + NC), B("ST_%d" % c, rows=8), B("IZ_%d" % c)
+            S, st = B("SROT%d" % P, c * NC, c * NC + NC), B("ST_%d" % c, rows=8)
             ua, ub = B("pU%d" % c, 0, NC), B("pU%d" % c, NC, 2 * NC)
-            mm([(ua, B("IDn32"), S)], True, False)
-            mm([(ua, B("EXz", rows=8), st)], False, False)
-            mm([(ua, B("B64"), iz)], False, True)
             z1 = B("pK%d" % c, 384, 512)
-            mm([(z1, B("EXz", rows=8), st), (z1, B("B64"), iz)])
+            for o in (z1, ua):
+                x = [[(o, B("EXz", rows=8), st)]]
+                if t:
+                    x.append([((o[0], o[1] + a, o[1] + a + 32) + o[3:], B("WN4", 4 * a, 4 * a + 128), B("NS_%dT" % c)) for a in range(0, NC, 32)])
+                if o == ua:
+                    x.insert(len(x) if PAR["SL"][c] else 0, [(ua, B("IDn32"), S)])
+                for k, y in enumerate(x):
+                    mm(y, k == 0, k == len(x) - 1)
             lists(t, c, ua, z1, 0)
-            offsets(c, B("pF%d" % c, 0, NC), B("OFL_%d" % c))
+            if PAR["RND"][0]:
+                rest(c, B("OFL_%d" % c))
+            else:
+                offsets(c, B("pF%d" % c, 0, NC), B("OFL_%d" % c))
             tag[0] = "H%d" % c
             rows, sn = B("pK%d" % c, 256, 384, rows=8), B("SN_%d" % c)
-            mm([(rows, B("IDh", 0, 8, rows=8), st), (rows, B("B64", 0, 128, 16), iz)])
+            mm([(rows, B("IDh", 0, 8, rows=8), st), (rows, B("NS_%d" % c, 0, 8), B("IDbn"))][:1 + (t > 0)])
             ts(sn, rows, -17.0, OP.add, -float(ZC), OP.max)
-            mm([(z1, B("EXz", rows=8), sn)])
             mm([(ub, B("IDn32"), S), (ub, B("EXz", rows=8), sn)])
             lists(t, c, ub, z1, 1)
             x = "pK%d" % c
             mm([(B(x, 256, 280), B("DS0_%d" % c), B("GA")), (B(x, 272, 280), B("DS1_%d" % c), B("GA", 8, 16)),
                 (B(x, 264, 272), B("XS0_%d" % c), B("BLKs", 0, 128, 16)), (B(x, 264, 272), B("XS1_%d" % c), B("GP", 0, 8))])
             tag[0] = "F%d" % c
-            for m in range(16):
-                either("V" if m < 12 or t == 0 else "G", "VAG", lambda q: cp(B("Z_%d" % c, 2 * m, 32 * NC, 32), tm(c, m % 2), q))
+            def fill(q, ms):
+                for m in ms:
+                    cp(B("Z_%d" % c, 2 * m, 32 * NC, 32), tm(c, m % 2), q)
+                join(len(ms))
+            for m in range(0, 16, 2):
+                either("V" if m < 8 or t == 0 else "A", "VAG" if m >= PAR["GF"] else "VA", lambda q: fill(q, [m, m + 1]))
             er = B("pE%d" % c, 0, 128)
-            mm([(er, tm(c, 0), B("BM")), (er, B("ONE", rows=1), B("CROW", rows=1)), (er, tm(c, 1), B("BM"))], True, False)
+            mm([(er, tm(c, 0), B("BE")), (er, B("ONE", rows=1), B("CROW", rows=1)), (er, tm(c, 1), B("BE"))], True, False)
         for c in range(2):
             Z, MX = "Z_%d" % c, "MX_%d" % c
-            for k in range(4):
+            for q, lo, hi in pieces(PAR["PICK"][t][c]):
                 tag[0] = "Y%d" % c
-                either("A", "AV", lambda q: gather(q, B(Z, 1024 * k + 1, 1024 * k + 1024, 2), B("XL%d" % t), B("OFL_%d" % c, 32 * k, 32 * k + 32)))
+                either(q, "AV", lambda q: gather(q, B(Z, 32 * lo + 1, 32 * hi, 2), B("XL%d" % t), B("OFL_%d" % c, lo, hi)))
+                ops[-1]["row"] = (c, 0)
                 tag[0] = "M%d" % c
-                scan(B(MX, 1024 * k + 1, 1024 * k + 1024), B(Z, 1024 * k, 1024 * k + 1023), B(Z, 1024 * k + 1, 1024 * k + 1024), 256.0, OP.min, OP.max)
+                w = PAR["MW"]
+                for a in range(32 * lo, 32 * hi, w):
+                    scan(B(MX, a + 1, a + w), B(Z, a, a + w - 1), B(Z, a + 1, a + w), 256.0, OP.min, OP.max)
         for c in range(2):
             i0 = c * NC
             E, K, Z, MX = "pE%d" % c, "pK%d" % c, "Z_%d" % c, "MX_%d" % c
             tag[0] = "E%d" % c
-            for j0 in range(0, 15, 3):
-                mm([(B(E, j, 128, 16), B(Z, 2 * (j + a) + 1, 32 * NC, 32), B("BM", 0, 128, 16)) for j in range(j0, j0 + 3) for a in range(2)], False, False)
-            for j0 in range(0, 15, 3):
-                mm([(B(E, j, 128, 16), B(MX, 2 * (j + a) + 1 + j % 2, 32 * NC, 32), B("B64", 0, 128, 16)) for j in range(j0, j0 + 3) for a in range(2)], False, j0 == 12)
+            for lo, hi in PAR["EM"][c]:
+                for m0 in range(0, 16 * (hi == NC), 4):
+                    mm([(B(E, 0, 128) + (0, m - 1) if m % 15 else B(E, m * 14 // 15, 128, 16), B(Z, 2 * m + 1, 32 * NC, 32), B("BM", 0, 128, 8 if m % 15 else 16))
+                        for m in range(m0, m0 + 4)], False, False)
+                for j0 in range(0, 15, 5):
+                    mm([(B(E, j, 128, 16, rows=hi) + (lo,), B(MX, 32 * lo + 2 * (j + a) + 1 + j % 2, 32 * hi, 32), B("B64", 0, 128, 16))
+                        for j in range(j0, j0 + 5) for a in range(2)], False, j0 == 10 and hi == NC)
             tag[0] = "C%d" % c
             st, sm, pr = B("ST_%d" % c), "SM_%d" % c, "PR_%d" % c
-            scan(B("SC_%d" % c), B("RST"), B(E, 0, 128), float(CAP), OP.max, OP.min)
-            key = B("SC_%d" % c, 14, 128, 16)
+            key = B("SC_%d" % c, 0, 8)
+            op("V", [lambda key=key, E=E: g.vector.tensor_reduce(ap(key), ap(B(E, 0, 128)), AxisListType.X, OP.min)], [B(E, 0, 128)], [key], 128)
             ts(B("RR_%d" % c), key, R16, OP.add, R16, OP.subtract)
             for a in (8, 16):
                 ts(B(sm, a, a + 8), key, float(CAP - 4), OP.is_lt)
@@ -431,58 +519,82 @@ def plan(g, core, T, topo):
             recv(sr, engines(topo, T.cores[(rank + 1) % n], core), "rs%d%d" % (t + 1, c), PAR["RECV"], s)
             tag[0] = "Q%d" % c
             tt(B(pr, 0, 24), B(sm, 0, 24), B(K, 256, 280), OP.mult)
-            spread(B("pF%d" % c, NC, 2 * NC), "WF", pr, False)
-            offsets(c, B("pF%d" % c, NC, 2 * NC), B("OFQ_%d" % c))
+            if PAR["RND"][1]:
+                op("V", [lambda pr=pr: g.vector.transpose(ap(B(pr + "T")), ap(B(pr)))], [B(pr)], [B(pr + "T")], 64)
+                for h in range(2):
+                    o = half(c, h)
+                    late = [[((o[0], o[1] + a, o[1] + a + 32) + o[3:], B(w, 256 * h + 4 * a, 256 * h + 4 * a + 128), B(pr + "T")) for a in (0, 32)]
+                            for w in ("WF4n", "WF4")]
+                    x = terms(c, 1, h, "")
+                    mm(late[0] + rounded(c, h) + x[2:] + late[1] + x[:2], False, True)
+                rest(c, B("OFQ_%d" % c))
+            else:
+                spread(B("pF%d" % c, NC, 2 * NC), "WF", pr, False)
+                offsets(c, B("pF%d" % c, NC, 2 * NC), B("OFQ_%d" % c))
             tag[0] = "R%d" % c
             rows = B(K, 384, 512, rows=8)
-            mm([(rows, B("IDh", 0, 8, rows=8), st), (rows, B("B64", 0, 128, 16), B("IZ_%d" % c)), (rows, B(sm, 8, 16), B("ID16"))])
-            ts(st, rows, -17.0, OP.add, -float(ZC), OP.max)
+            mm([(rows, B("IDh", 0, 8, rows=8), st), (rows, B(sm, 8, 16), B("ID16")), (rows, B("NS_%d" % c, 0, 8), B("IDbn"))][:2 + (t > 0)])
+            ts(st, rows, NB - 17.0, OP.add, NB - ZC, OP.max)
         tag[0] = "X"
         send_logs(t + 1)
         if not last:
             tag[0] = "P"
             an, own, far = B("pU0", 256, 272, rows=8), B("SX%d" % (t + 1), 0, 16, rows=8), B("SR%d" % (t + 1), 0, 16, rows=8)
             mm([(an, B("SM_%d" % c, 8, 16), B("ONE", 0, 16)) for c in range(2)])
-            cp(own, an)
+            either("V", "AV", lambda q: cp(own, an, q))
             mm([(B("pU0", 272, 304), B("IDn32"), B("NCT", 0, 32)), (B("pU0", 288, 304), B("EXbn", rows=8), far)], True, False)
             mm([(B("pU0", 272, 288), B("EXa", rows=8), own), (B("pU0", 288, 304), B("EXb", rows=8), own)], False, True)
             cp(B("LI"), B("pU0", 272, 304))
             ts(B("LJ"), B("LI"), 255, AND)
             cp(B("LOS"), B("LJ"))
-            gather("V", B("D%d" % (1 - P)), B("CF%d" % (t + 1)), B("LOS", 0, 16), -2.0, -1.0)
+            either("V", PAR["DQ"], lambda q: gather(q, B("D%d" % (1 - P)), B("CF%d" % (t + 1)), B("LOS", 0, 16), -2.0, -1.0))
             for c in range(2):
                 either("V", "AV", lambda q: gather(q, B("SROT%d" % (1 - P), NC * c, NC * c + NC), B("SR%d" % (t + 1), 16, SW), B("LOS", 16 + 8 * c, 24 + 8 * c)))
         for c in range(2):
             V, MV = "V_%d" % c, "MV_%d" % c
-            for k in range(4):
+            for q, lo, hi in pieces(PAR["PICK"][t][2 + c]):
                 tag[0] = "V%d" % c
-                either("A", "AV", lambda q: gather(q, B(V, 512 * k, 512 * k + 512), B("XL%d" % t), B("OFQ_%d" % c, 32 * k, 32 * k + 32)))
+                either(q, "AV", lambda q: gather(q, B(V, 16 * lo, 16 * hi), B("XL%d" % t), B("OFQ_%d" % c, lo, hi)))
+                ops[-1]["row"] = (c, 1)
                 tag[0] = "D%d" % c
-                scan(B(MV, 512 * k + 1, 512 * k + 512), B(V, 512 * k, 512 * k + 511), B(V, 512 * k + 1, 512 * k + 512), 256.0, OP.min, OP.max)
+                scan(B(MV, 16 * lo + 1, 16 * hi), B(V, 16 * lo, 16 * hi - 1), B(V, 16 * lo + 1, 16 * hi), 256.0, OP.min, OP.max)
         for c in range(2):
             i0 = c * NC
             E, K, F, V, MV, st = "pE%d" % c, "pK%d" % c, "pF%d" % c, "V_%d" % c, "MV_%d" % c, B("ST_%d" % c, rows=8)
-            OV, iz = "OV_%d" % c, B("IZ_%d" % c)
-            for h in range(2):
-                tag[0] = "D%d" % c
-                r = B((E, K)[h], 0, 64)
-                for m0 in (1, 6, 11):
-                    mm([(r, B("WN", 16 - m, 144 - m), B(V, 1024 * h + m, 1024 * h + 1024, 16)) for m in range(m0, m0 + 5)], m0 == 1, False)
-                for m0 in (2, 9):
-                    mm([(r, B("SEL", 16 - m, 144 - m), B(MV, 1024 * h + m, 1024 * h + 1024, 16)) for m in range(m0, m0 + 7)], False, m0 == 9)
-                tag[0] = "N%d" % c
-                ts(B(OV, 64 * h, 64 * h + 64), r, float(32 * TH2), OP.is_gt)
-            mm([(B(F, 256, 384), B("TRI"), B(OV))])
-            ts(iz, B(F, 256, 384), 0.0, OP.is_equal, 1.0 / 64, OP.mult)
+            tag[0] = "D%d" % c
+            er, ns, ov = B(E, 0, 128), "NS_%d" % c, B("OV_%d" % c, 0, 128)
+            mm([(er, B("ONE", rows=1), B("DROW", rows=1))], True, False)
+            for m0 in (1, 6, 11):
+                mm([(er + (0, m) if m < 15 else B(E, 15, 128, 16), B(V, m, 16 * NC, 16), B("BM", 0, 128, 8 if m < 15 else 16))
+                    for m in range(m0, m0 + 5)], False, False)
+            for m0 in (2, 9):
+                mm([(B(E, m, 128, 16), B(MV, m, 16 * NC, 16), B("B64", 0, 128, 16)) for m in range(m0, m0 + 7)], False, m0 == 9)
+            tag[0] = "N%d" % c
+            tt(ov, er, B("MROW"), OP.min)
+            nz = B("NZ_%d" % c, 16, 144, 16)
+            x = nz if last else B(ns, 0, 8)
+            op("V", [lambda x=x, ov=ov: g.vector.tensor_reduce(ap(x), ap(ov), AxisListType.X, OP.max)], [ov], [x], 128)
+            if not last:
+                op("V", [lambda ns=ns: g.vector.transpose(ap(B(ns + "T")), ap(B(ns)))], [B(ns)], [B(ns + "T")], 64)
             tag[0] = "T%d" % c
+            if not last:
+                either("A", "AV", lambda q: cp(nz, B(ns, 0, 8), q))
             tl = B(E, 128, 136)
-            mm([(tl, B("ONE", rows=1), B("KT", rows=1))] + [(tl, B("SEL", 16 - p, 144 - p), B("IZ_%d" % c, p, NC, 16)) for p in range(16)])
-            for a in range(2):
-                ts(B("TO_%d" % c, 8 * a, 8 * a + 8), tl, B(("ra", "rb")[a]), OP.add)
+            mm([(tl, B("ONE", rows=1), B("KT", rows=1))] + [(tl, B("NZ_%d" % c, 16 - p, 144 - p), B("IDbn", p, 128, 16)) for p in range(16)])
+
+            def both(q):
+                for a in range(2):
+                    x, r = B("TO_%d" % c, 8 * a, 8 * a + 8), B(("ra", "rb")[a])
+                    if q == "V":
+                        ts(x, tl, r, OP.add)
+                    else:
+                        act(x, tl, r, 1.0)
+                join(2)
+            either("V", PAR["OFFQ"], both)
             either("A", "AV", lambda q: gather(q, B("TT", 256 * c, 256 * c + 256), B(V), B("TO_%d" % c)))
             if last:
                 r8 = B(K, 256, 384, rows=8)
-                mm([(r8, B("IDh", 0, 8, rows=8), st), (r8, B("B64", 0, 128, 16), iz)])
+                mm([(r8, B("IDh", 0, 8, rows=8), st), (r8, nz, B("IDbn"))])
                 ts(B("YZ", i0, i0 + NC), r8, float(ZC - 1), OP.add)
                 for a in range(2):
                     x = B("TT", 256 * c + NC * a, 256 * c + NC * a + NC)
@@ -516,14 +628,14 @@ def link(ops):
             deps[x] = deps.get(x, False) or hard
         if "after" in o:
             add(o["after"], False)
-        if o["kind"] in ("dma", "send"):
-            if o["q"] in prev:
-                add(prev[o["q"]], False)
-            prev[o["q"]] = k
+        if o["kind"] == "send" or o["kind"] == "dma" and o["w"]:
+            if (o["q"], o["kind"]) in prev:
+                add(prev[o["q"], o["kind"]], False)
+            prev[o["q"], o["kind"]] = k
         acc = [(r, False) for r in o["r"]] + [(w, True) for w in o["w"]]
         for b in set(r[0] for r, wr in acc if SCRATCH[r[0]][0] == "psum"):
             was, now = turns.get(b, ([], []))
-            if now and ops[now[0]]["q"] != o["q"]:
+            if now and (ops[now[0]]["q"] != o["q"] or "alt" in o or "alt" in ops[now[0]]):
                 was, now = now, []
             for x in was:
                 add(x, True)
@@ -553,34 +665,43 @@ def order(ops):
             succ[x][k] = l
 
     def place(key, back):
-        need = [len(succ[k] if back else lag[k]) for k in range(n)]
-        at = [ops[k]["cost"] - busy[k] if back else 0.0 for k in range(n)]
-        ready = sorted((key[k], k) for k in range(n) if need[k] == 0)
-        slots, t0 = {}, [0.0] * n
-        while ready:
-            k = ready.pop(0)[1]
-            t, w = at[k], busy[k]
+        first = succ if back else lag
+        for k in (range(n - 1, -1, -1) if back else range(n)):
+            a = key[k]
+            for x in first[k]:
+                if key[x] >= a:
+                    a = key[x] + 1e-3
+            key[k] = a
+        slots, t0 = {q: [] for q in "VAPGSR"}, [0.0] * n
+        for a, k in sorted(zip(key, range(n))):
+            w = busy[k]
+            if back:
+                t = ops[k]["cost"]
+                for x, d in first[k].items():
+                    d += t0[x] + busy[x]
+                    if d > t:
+                        t = d
+                t -= w
+            else:
+                t = 0.0
+                for x, d in first[k].items():
+                    d += t0[x]
+                    if d > t:
+                        t = d
             if w:
-                l = slots.setdefault(ops[k]["q"], [])
-                i = len(l)
+                l = slots[ops[k]["q"]]
+                i = m = len(l)
                 while i and l[i - 1][1] > t:
                     i -= 1
-                while i < len(l) and l[i][0] < t + w:
-                    t = max(t, l[i][1])
+                while i < m and l[i][0] < t + w:
+                    if l[i][1] > t:
+                        t = l[i][1]
                     i += 1
                 l.insert(i, (t, t + w))
             t0[k] = t
-            for s, d in (lag[k] if back else succ[k]).items():
-                at[s] = max(at[s], t + (d + w - busy[s] if back else d))
-                need[s] -= 1
-                if need[s] == 0:
-                    e, i = (key[s], s), len(ready)
-                    while i and ready[i - 1] > e:
-                        i -= 1
-                    ready.insert(i, e)
         if back:
-            return [-(t0[k] + busy[k]) for k in range(n)], max(t0[k] + busy[k] for k in range(n))
-        return t0, max(t0[k] + ops[k]["cost"] for k in range(n))
+            return [-a - b for a, b in zip(t0, busy)], 0
+        return t0, max(t0[k] + ops[k]["cost"] for k in range(n - 40, n))
     way = [0.0] * n
     for k in range(n - 1, -1, -1):
         way[k] = max([ops[k]["cost"]] + [way[s] + d for s, d in succ[k].items()])
@@ -596,8 +717,10 @@ def order(ops):
         for s in succ[k]:
             succ[k][s] = lag[s][k] = busy[k] + sync
 
-    def packed(key):
+    def packed(key, bar=1e9):
         t0, end = place(key, False)
+        if end > bar:
+            return end, t0
         t1, e1 = place(place([-(t0[k] + busy[k]) for k in range(n)], True)[0], False)
         return (e1, t1) if e1 < end else (end, t0)
     free = [k for k in range(n) if "alt" in ops[k]]
@@ -609,6 +732,7 @@ def order(ops):
         for i, k in enumerate(l):
             same.setdefault((b[0], i, len(l)), []).append(k)
     like = {k: l for l in same.values() for k in l}
+    mark = [blocks[("C0", t)][0] for t in range(NV)]
     blocks = list(blocks.values())
 
     def chain(t0):
@@ -623,22 +747,42 @@ def order(ops):
                 k = held[-1][1]
         return held
     sig = tuple((o["blk"], o["kind"], o["sem"]) for o in ops)
-    cur = best = DONE.get(sig) or packed([-w for w in way]) + ([ops[k]["q"] for k in free],)
-    for it in range(0 if sig in DONE else PAR["TURNS"]):
+    own = [k for k in range(n) if ops[k]["kind"] in ("c", "dma")]
+    key, turns = [-w for w in way], PAR["TURNS"]
+    if "first" in DONE:
+        key, turns = [0.0] * n, turns // 8
+        for k, t in zip(own, DONE["first"][0]):
+            key[k] = t
+        for k, q in zip(free, DONE["first"][1]):
+            assign(k, q)
+    cur = best = DONE.get(sig) or packed(key) + ([ops[k]["q"] for k in free],)
+    for it in range(0 if sig in DONE else turns):
         key = list(cur[1])
         r = rnd()
-        if r < PAR["MOVE"][0]:
+        if rnd() < PAR["COPY"]:
+            a, b = int(rnd() * NV), int(rnd() * NV)
+            d = key[mark[b]] - key[mark[a]]
+            for l in same.values():
+                x = {ops[k]["blk"][1]: k for k in l}
+                if a in x and b in x:
+                    key[x[b]] = key[x[a]] + d
+                    if ops[x[a]]["q"] in ops[x[b]].get("alt", ""):
+                        assign(x[b], ops[x[a]]["q"])
+        elif r < PAR["MOVE"][0]:
             held = chain(cur[1])
             for _ in range(1 + int(2 * rnd())):
                 k, p = held[int(rnd() * len(held))]
-                k = p if "alt" in ops[p] and rnd() < 0.5 else k
-                if "alt" in ops[k] and rnd() < 0.7:
-                    qs = [q for q in sorted(ops[k]["alt"]) if q != ops[k]["q"]]
-                    assign(k, qs[int(rnd() * len(qs))])
-                elif rnd() < 0.5:
-                    key[k] = key[p] - 1 - 300 * rnd()
+                a = p if "alt" in ops[p] and rnd() < 0.5 else k
+                tied = rnd() < PAR["TIED"]
+                if "alt" in ops[a] and rnd() < 0.6:
+                    qs = [q for q in sorted(ops[a]["alt"]) if q != ops[a]["q"]]
+                    q = qs[int(rnd() * len(qs))]
+                    for x in (like[a] if tied else [a]):
+                        assign(x, q)
                 else:
-                    key[p] = key[k] + 1 + 1000 * rnd()
+                    a, d = (k, key[p] - key[k] - 300 * rnd()) if rnd() < 0.5 else (p, key[k] - key[p] + 1000 * rnd())
+                    for x in (like[a] if tied else [a]):
+                        key[x] += d
         elif r < PAR["MOVE"][1]:
             for _ in range(1 + int(2 * rnd())):
                 k = free[int(rnd() * len(free))]
@@ -653,20 +797,103 @@ def order(ops):
                 for k in b:
                     for x in (like[k] if it % 2 else [k]):
                         key[x] += d
-        new = packed(key) + ([ops[k]["q"] for k in free],)
-        if new[0] <= cur[0] + PAR["HEAT"] * rnd() * (1 - it / PAR["TURNS"]):
+        new = packed(key, cur[0] + PAR["BAR"]) + ([ops[k]["q"] for k in free],)
+        if new[0] <= cur[0] + PAR["HEAT"] * rnd() * (turns - it) / PAR["TURNS"]:
             cur = new
             if new[0] < best[0]:
                 best = new
         else:
             for k, q in zip(free, cur[2]):
                 assign(k, q)
+    if sig not in DONE:
+        for k, q in zip(free, best[2]):
+            assign(k, q)
+        best = refine(ops, lag, busy, best, free, assign, rnd, turns * PAR["FINE"])
     DONE[sig] = best
+    DONE.setdefault("first", ([best[1][k] for k in own], best[2]))
     for k, q in zip(free, best[2]):
         assign(k, q)
     for k in range(n):
         ops[k]["t0"] = best[1][k]
     return sorted(range(n), key=lambda k: (best[1][k], k))
+
+
+def refine(ops, lag, busy, best, free, assign, rnd, turns):
+    n = len(ops)
+    seq = sorted(range(n), key=lambda k: (best[1][k], k))
+    last = range(n - 40, n)
+
+    def times(seq, lo, t, by):
+        t, by, fr, who = list(t), list(by), {q: 0.0 for q in "VAPGSR"}, {q: -1 for q in "VAPGSR"}
+        left = 5
+        for k in seq[lo - 1::-1] if lo else ():
+            q = ops[k]["q"]
+            if who[q] < 0 and busy[k]:
+                who[q], fr[q] = k, t[k] + busy[k]
+                left -= 1
+                if not left:
+                    break
+        for k in seq[lo:]:
+            a, b = 0.0, -1
+            for x, d in lag[k].items():
+                d += t[x]
+                if d > a:
+                    a, b = d, x
+            w = busy[k]
+            if w:
+                q = ops[k]["q"]
+                if fr[q] > a:
+                    a, b = fr[q], -2 - who[q]
+                fr[q], who[q] = a + w, k
+            t[k], by[k] = a, b
+        return max((t[k] + ops[k]["cost"], k) for k in last), t, by
+    (end, top), t, by = times(seq, 0, [0.0] * n, [-1] * n)
+    best = (end, t, [ops[k]["q"] for k in free])
+    held = None
+    for it in range(turns):
+        if held is None:
+            held, k = [], top
+            while k != -1:
+                b = by[k]
+                if b < -1:
+                    b = -2 - b
+                    held.append((k, b))
+                k = b
+            pos = {k: i for i, k in enumerate(seq)}
+        k, p = held[int(rnd() * len(held))]
+        a = (k, p)[rnd() < 0.5]
+        i, j = pos[p], pos[k]
+        was = None
+        if "alt" in ops[a] and rnd() < 0.4:
+            qs = [q for q in sorted(ops[a]["alt"]) if q != ops[a]["q"]]
+            was = ops[a]["q"]
+            assign(a, qs[int(rnd() * len(qs))])
+            new, lo = seq, pos[a]
+        elif a == k:
+            i = max(0, i - int(rnd() * rnd() * PAR["FAR"]))
+            up = {k}
+            for x in seq[j - 1:i - 1 if i else None:-1]:
+                if any(x in lag[y] for y in up):
+                    up.add(x)
+            part = seq[i:j + 1]
+            new, lo = seq[:i] + [x for x in part if x in up] + [x for x in part if x not in up] + seq[j + 1:], i
+        else:
+            j = min(n - 1, j + int(rnd() * rnd() * PAR["FAR"]))
+            down = {p}
+            for x in seq[i + 1:j + 1]:
+                if any(y in down for y in lag[x]):
+                    down.add(x)
+            part = seq[i:j + 1]
+            new, lo = seq[:i] + [x for x in part if x not in down] + [x for x in part if x in down] + seq[j + 1:], i
+        (e, tp), t2, by2 = times(new, lo, t, by)
+        if e <= end + PAR["WARM"] * rnd() * rnd() * (turns - it) / turns:
+            end, top, t, by, held = e, tp, t2, by2, None
+            seq = sorted(new, key=lambda k: t[k])
+            if e < best[0]:
+                best = (e, t, [ops[k]["q"] for k in free])
+        elif was:
+            assign(a, was)
+    return best
 
 
 def emit(g, T, ops, seq):

import math
import numpy as np
import comms_topo
from concourse.bass import DstId, RemoteDMATransfer
from concourse.mybir import dt, AluOpType, AxisListType, ActivationFunctionType

OP = AluOpType
AF = ActivationFunctionType
NV, W, ZC, TH, TH2 = 4, 4096, 1536, 1082, 820
NB = 144
NC = 128
WX = W + 16
SW = 16 + 256
R16 = 1.5 * 2 ** 27
R4096 = 1.5 * 2 ** 35
CAP = 32 * (TH - 1) + 224
PAR = dict(
    SYNC=100, PE=0.5, GN=1.56, RECV=2500, SEND=1000,
    YS=["AAAA", "AAAA"],
    VS=["AAAA", "AAAA"],
    TQ="AA",
    FILL=["VVVVVVVVVVGGGGGG", "VVVVVVVVVVGGGGGG"],
    BI={}, TURNS=3000, TAIL=64, SEED=1, HEAT=500, LOG=(20000, 34000, 48000), XP=1, MW=512, BAR=2500, GF=12, SL=(1, 0), LOAD=(2000, 4000, 5800), PICK=[["AAAA"] * 4] * 4, FINE=12, WARM=600, FAR=24, COPY=0.05, TIED=0.3, RND=(1, 1), OFFQ="AV", DQ="AV", EM=((0, 96), (96, 128)), MOVE=(0.5, 0.7),
)
PAR.update(SYNC=290, SEND=1200, RECV=1800, LOG=(19000, 33000, 47000), TURNS=9000, HEAT=1000, MOVE=(0.6, 0.75), EM=[((0, 128),)] * 2, RND=(1, 0), FINE=1, WARM=300,
           SEED=5, TIED=0.6, COPY=0.07, BAR=1000)
PAR.update({'YS': ['AAAV', 'AAVA'], 'VS': ['AAAA', 'AVAA'], 'TQ': 'AA', 'FILL': ['VVVVVVVVVAAAAGGG', 'VVVVVVVAAAAGGGGG'], 'BI': {'N1': -6577, 'P': 10849, 'C0': -18109, 'Y0': 29548, 'Q0': 35775, 'L0': 13704, 'B1': 36812, 'Z': 24811, 'Y1': -3215, 'M0': -37336, 'L1': -10511, 'V0': 72407, 'V1': 3110, 'Q1': 34840, 'F1': -67990, 'D1': -9648, 'B0': -34734, 'C1': -90901, 'c': -20085, 'X': 44139, 'F0': -56967, 'S0': -49337, 'E1': -42699, 'S1': 26460, 'T0': 3205, 'M1': -40204, 'D0': -15280, 'N0': 48304, 'E0': -62395, 'T1': -16593}})

SCRATCH = {}
DONE = {}


def _b(name, cols, dtype, where="sbuf", rows=128):
    SCRATCH[name] = (where, [rows, cols], dtype)


for _v in range(4):
    _b("XL%d" % _v, WX, "bfloat16")
    _b("CF%d" % _v, 256, "int32")
    _b("SX%d" % _v, SW, "float32")
    _b("SR%d" % (_v + 1), SW, "float32")
for _n, _c, _d in (("S0I", 256, "int32"), ("TL", 512, "bfloat16"), ("TT", 512, "bfloat16"), ("YSO", 256, "float32"),
                   ("SROT0", 256, "float32"), ("SROT1", 256, "float32"), ("D0", 256, "float16"), ("D1", 256, "float16"),
                   ("WN4", 512, "bfloat16"), ("NCT", 48, "float32"), ("LI", 32, "int32"), ("LJ", 32, "int32"),
                   ("LOS", 32, "uint16"), ("KT", 8, "bfloat16"), ("WJ4", 512, "bfloat16"), ("WF4", 512, "float32"), ("WF4n", 512, "float32"), ("P4", 4, "float32")):
    _b(_n, _c, _d)
VIRT = {}
for _p, _c, _d, _l in (("PF", 1, "float32", "rg rr pp rp1 rp2 rp4 ra rb p8 p32 pb wa wb wc"), ("PI", 1, "int32", "rowI rrI p8I p32I"),
                       ("PJ", 16, "int32", "c16"), ("PG", 128, "float32", "colF IDn32 BLKs BLKsn EXa EXb EXbn i16 WF GP"),
                       ("PB", 128, "bfloat16", "cg cr B64 BM MROW DROW IDbn ID16 ONE CROW WJ WC WE BE RM"),
                       ("PH", 128, "float16", "IDh EXz W1 W9 W0 WM WM2 W1n W9n W0n"), ("PA", 24, "float16", "GA")):
    for _k, _n in enumerate(_l.split()):
        VIRT[_n] = (_p, _k * _c, _c)
    _b(_p, _c * len(_l.split()), _d)
_b("Z8I", 256, "int32", rows=8)
_b("YZ", 256, "float32", rows=8)
for _k in range(2):
    for _n, _c, _d in (("MASK", NC, "bfloat16"), ("OH0", NC, "float16"), ("OH1", NC, "float16"), ("DS0", NC, "float16"), ("XS0", NC, "float32"),
                       ("DS1", NC, "float16"), ("XS1", NC, "float32"), ("GE", NC, "bfloat16"),
                       ("FI", NC, "int32"), ("FJ", NC, "int32"), ("OFL", NC, "uint16"), ("OFQ", NC, "uint16"), ("Z", 32 * NC, "bfloat16"),
                       ("MX", 32 * NC, "bfloat16"), ("V", 16 * NC, "bfloat16"), ("MV", 16 * NC, "bfloat16"), ("SC", 128, "float32"),
                       ("RR", 8, "float32"), ("SM", 32, "bfloat16"), ("PR", 32, "float32"),
                       ("NS", 32, "bfloat16"), ("NZ", 144, "bfloat16"), ("TO", 16, "uint16")):
        _b("%s_%d" % (_n, _k), _c, _d)
    _b("ST_%d" % _k, NC, "float16", rows=8)
    _b("SN_%d" % _k, NC, "float16", rows=8)
    _b("SM_%dT" % _k, 32, "bfloat16")
    _b("PR_%dT" % _k, 32, "float32")
    _b("NS_%dT" % _k, 32, "bfloat16")
    SCRATCH["OV_%d" % _k] = ("sbuf", [128, 8, 16], "bfloat16")
    for _n in ("U", "K", "E", "F"):
        _b("p%s%d" % (_n, _k), 512, "float32", where="psum")
    SCRATCH["pE%d" % _k] = ("psum", [128, 32, 16], "float32")

SEMAPHORES = ["sV", "sA", "sP", "sG", "h0", "h1", "lh0", "lh1"]
SEMAPHORES += ["d_" + n for n in ("s0", "cf", "z0", "t0", "xa", "xb", "ys", "yz", "ya0", "ya1", "yb0", "yb1")]
for _v in range(1, 4):
    SEMAPHORES += ["%s%d" % (n, _v) for n in ("rca", "rla", "rlb", "lca", "lla", "llb", "lcf", "llf")]
for _v in range(1, 5):
    SEMAPHORES += ["%s%d%d" % (n, _v, c) for n in ("rs", "ls") for c in range(2)]


def pieces(s):
    out, lo = [], 0
    for x in s:
        out.append((x.upper(), lo, lo + (32 if x.isupper() else 16)))
        lo = out[-1][2]
    return out


def engines(topo, src, dst, upper=0):
    e = topo.engines(src, dst)
    if dst in topo.cores_of(src):
        return e[len(e) // 2:] if upper else e[:len(e) // 2]
    return e


def way_of(T, topo, rank, v):
    n = len(T.cores)
    far = [x for x in range(1, NV) if T.cores[(rank - x) % n] not in topo.cores_of(T.cores[rank])]
    return "near" if v not in far else "far" if v == far[0] else "on"


def helper(T, topo, rank):
    c = T.cores[rank]
    return [x for x in topo.cores_of(c) if x not in T.cores and topo.die(x) != topo.die(c)][0]


def hand_on(g, core, T, topo, rank):
    v = [x for x in range(1, NV) if way_of(T, topo, rank, x) == "far"][0]
    dst = T.cores[(rank - v) % len(T.cores)]
    rid, pid = topo.addr(dst, core)
    for k in range(2):
        g.wait_ge(T.sem["h%d" % k], len(engines(topo, T.cores[rank], core, 1)))
        lo, hi = k * W // 4, (k + 1) * W // 4
        g.remote_dma(T["XL%d" % v][:, lo:hi], T.XL0[:, lo:hi], T.sem["rla%d" % v], T.sem["lh0"], pid, rid, topo.mask(core, dst))
    g.wait_ge(T.sem["lh0"], 2 * len(topo.engines(core, dst)))


def plan(g, core, T, topo):
    rank = T.rank_of(core)
    n = len(T.cores)
    ops = []
    tag = ["c", 0]

    def B(name, lo=0, hi=None, step=1, rows=128):
        p, o, c = VIRT[name] if name in VIRT else (name, 0, SCRATCH[name][1][1])
        return (p, o + lo, o + (c if hi is None else hi), step, min(rows, SCRATCH[p][1][0]))

    def op(q, fns, reads, writes, cost, kind="c", sem=None, cnt=0, cls=None):
        ops.append(dict(tag=tag[0], blk=(tag[0], tag[1]), q=q, fns=fns, r=reads, w=writes, cost=cost, kind=kind, sem=sem, cnt=cnt, cls=cls or q))
        return len(ops) - 1

    def ap(x):
        p = x[5] if len(x) > 5 else 0
        if len(SCRATCH[x[0]][1]) == 3:
            if len(x) > 6:
                return T[x[0]][p:x[4], x[1] // 16:x[2] // 16, x[6]:x[6] + 2]
            if x[3] == 16:
                return T[x[0]][p:x[4], x[1] // 16:x[2] // 16, x[1] % 16]
            if x[2] - x[1] < 16:
                return T[x[0]][p:x[4], x[1] // 16, x[1] % 16:x[1] % 16 + x[2] - x[1]]
            return T[x[0]][p:x[4], x[1] // 16:x[2] // 16, :]
        if x[3] == 1:
            return T[x[0]][p:x[4], x[1]:x[2]]
        return T[x[0]][p:x[4], x[1]:x[2]:x[3]]

    def width(x):
        return -(-(x[2] - x[1]) // x[3])

    def psum(x):
        return SCRATCH[x[0]][0] == "psum"

    def cyc(*xs):
        two = all(SCRATCH[x[0]][2] in ("bfloat16", "float16", "uint16") for x in xs)
        return max(64, width(xs[0]) * (0.5 if two else 1))

    def tt(o, a, b, alu):
        c = width(o) * (1 if psum(a) or psum(b) else 2)
        op("V", [lambda: g.vector.tensor_tensor(ap(o), ap(a), ap(b), alu)], [a, b], [o], max(64, c))

    def sc(x):
        return T[x[0]][0:x[4], x[1]:x[2]] if isinstance(x, tuple) else x

    def ts(o, a, s1, op0, s2=None, op1=None):
        s1, s2 = [s[:4] + (o[4],) if isinstance(s, tuple) else s for s in (s1, s2)]
        rd = [a] + [s for s in (s1, s2) if isinstance(s, tuple)]
        if op1 is None:
            f = [lambda: g.vector.tensor_scalar(ap(o), ap(a), sc(s1), None, op0)]
        else:
            f = [lambda: g.vector.tensor_scalar(ap(o), ap(a), sc(s1), sc(s2), op0, op1)]
        op("V", f, rd, [o], cyc(o, a))

    def cp(o, a, q="V"):
        if q == "V":
            op("V", [lambda: g.vector.tensor_copy(ap(o), ap(a))], [a], [o], cyc(o, a))
        elif q == "A":
            op("A", [lambda: g.scalar.activation(ap(o), ap(a), AF.Copy)], [a], [o], max(64, width(o)))
        else:
            select(o, a, [[0, width(o)]], OP.is_ge, 0, 0)

    def ms(o, val):
        op("V", [lambda: g.vector.memset(ap(o), val)], [], [o], cyc(o))

    def scan(o, a, b, init, op0, op1):
        op("V", [lambda: g.vector.tensor_tensor_scan(ap(o), ap(a), ap(b), init, op0, op1)], [a, b], [o], cyc(o, a, b))

    def gather(q, o, win, off, scale=1.0, bias=0.0):
        if q == "V":
            f = lambda: g.vector.tensor_copy(ap(o), ap(win).indirect(ap(off)))
            if scale != 1.0 or bias != 0.0:
                f = lambda: g.vector.tensor_scalar(ap(o), ap(win).indirect(ap(off)), scale, bias, OP.mult, OP.add)
        else:
            f = lambda: g.scalar.activation(ap(o), ap(win).indirect(ap(off)), AF.Copy)
            if scale != 1.0 or bias != 0.0:
                f = lambda: g.scalar.activation(ap(o), ap(win).indirect(ap(off)), AF.Identity, bias=bias, scale=scale)
        op(q, [f], [win, off], [o], 60 + PAR["GN"] * width(o), cls="gather")

    def join(k):
        for o in [ops.pop() for _ in range(k - 1)]:
            for x in ("fns", "r", "w", "cost"):
                ops[-1][x] += o[x]

    def either(first, qs, make):
        alt = {}
        for q in [x for x in qs if x != first] + [first]:
            make(q)
            alt[q] = (ops[-1]["fns"], ops[-1]["cost"])
            if q != first:
                ops.pop()
        ops[-1]["alt"] = alt

    def mm(items, start=True, stop=True, each=False):
        fns, rd, wr, cost = [], [], [], 0
        for k, (o, l, r) in enumerate(items):
            fns.append(lambda o=o, l=l, r=r, k=k: g.tensor.matmul(ap(o), ap(l), ap(r), each or start and k == 0, each or stop and k == len(items) - 1))
            rd += [l, r]
            wr.append(o)
            cost += max(min(64, width(l)), width(r)) * (4 if SCRATCH[l[0]][2] == "float32" else 1) * PAR["PE"]
        op("P", fns, rd, wr, cost)

    def dma(q, o, a, rd, wr, sem, cost):
        eng = g.sync if q == "S" else g.scalar
        op(q, [lambda: eng.dma_start(o, a)], rd, wr, cost, kind="dma", sem=sem)

    def send(dst, out, src, rs, ls, upper=0):
        rid, pid = topo.addr(dst, core)
        e = engines(topo, core, dst, upper)
        return op("G", [lambda: g.remote_dma(ap(out), ap(src), T.sem[rs], T.sem[ls], pid, rid, sum(1 << x for x in e))], [src], [], PAR["SEND"],
                  kind="send", sem=ls, cnt=len(e))

    def recv(o, e, rs, cost, after=None):
        op("R", [], [], [o], cost, kind="recv", sem=rs, cnt=len(e))
        if after is not None:
            ops[-1]["after"] = after

    def iota(o, pat, base, cm):
        if SCRATCH[o[0]][2] == "int32":
            f = [lambda: g.iota(ap(o), pat, base, cm)]
        else:
            f = [lambda: g.iota(ap(o), pat, base, cm, allow_small_or_imprecise_dtypes=True)]
        op("G", f, [], [o], 150 + 2 * width(o))

    def select(o, a, pat, cmp, base, cm, fill=0.0):
        op("G", [lambda: g.affine_select(ap(o), ap(a), pat, cmp, fill, base, cm)], [a], [o], 190 + 2 * width(o))

    def act(o, a, bias, scale, fn=AF.Identity):
        op("A", [lambda: g.scalar.activation(ap(o), ap(a), fn, bias=sc(bias), scale=sc(scale))],
           [a] + [x for x in (bias, scale) if isinstance(x, tuple)], [o], max(64, width(o)))

    H = W // 2
    ld = PAR["LOAD"]
    dma("S", ap(B("S0I")), T.s0[:, :], [], [B("S0I")], "d_s0", ld[0])
    dma("A", ap(B("Z8I")), T.z0[:, :], [], [B("Z8I")], "d_z0", ld[0])
    dma("A", ap(B("CF0")), T.cf[:, :], [], [B("CF0")], "d_cf", ld[0])
    dma("S", ap(B("XL0", 0, H)), T.xl[:, H:W], [], [B("XL0", 0, H)], "d_xa", ld[1])
    dma("S", ap(B("XL0", H, WX)), T.xl[:, 0:WX - H], [], [B("XL0", H, WX)], "d_xb", ld[2])
    dma("A", ap(B("TL")), T.t0[:, :], [], [B("TL")], "d_t0", ld[1])
    AND = OP.bitwise_and
    iota(B("rowI"), [[0, 1]], 0, 1)
    iota(B("c16"), [[16, 16]], 0, 0)
    iota(B("pp"), [[0, 1]], 0, 1)
    iota(B("cg"), [[1, 8], [0, 16]], 0, 0)
    iota(B("colF"), [[1, 128]], 0, 0)
    iota(B("cr"), [[0, 8], [1, 16]], 0, 0)
    ts(B("rrI"), B("rowI"), 15, AND)
    cp(B("rr"), B("rrI"))
    ts(B("LI", 0, 16), B("c16"), B("rr"), OP.add, 5.0, OP.mult)
    ts(B("LJ", 0, 16), B("LI", 0, 16), 255, AND)
    cp(B("LOS", 0, 16), B("LJ", 0, 16))
    ts(B("rg"), B("pp"), B("rr"), OP.subtract, 1.0 / 16, OP.mult)
    ts(B("B64"), B("cg"), B("rg"), OP.is_equal, 64.0, OP.mult)
    ts(B("IDn32"), B("colF"), B("pp"), OP.is_equal, -1.0, OP.mult)
    ts(B("EXz"), B("cg"), B("pp"), OP.is_equal)
    for c in range(2):
        ts(B("ST_%d" % c, rows=8), B("Z8I", c * NC, c * NC + NC), 1.0 - ZC, OP.add)
    gather("V", B("SROT0"), B("S0I"), B("LOS", 0, 16), 1.0, -float(ZC))
    gather("V", B("D0"), B("CF0"), B("LOS", 0, 16), -2.0, -1.0)
    act(B("rp1"), B("rr"), 64.0, 64.0)
    act(B("rp2"), B("rr"), -14.0 * 64, 128.0)
    act(B("rp4"), B("rr"), 4.0 * 96, 256.0)
    for k in range(2):
        ms(B("RM", 64 * k, 64 * k + 64, rows=1), (1 - 2 * k) * R4096)
    act(B("WM"), B("cr"), -9.5 / 64, -1.0 / 64)
    scan(B("W1"), B("B64"), B("WM"), 0.0, OP.max, OP.mult)
    act(B("W0"), B("B64"), 0.0, -18.5 / 64)
    act(B("BLKs"), B("B64"), 0.0, -1.0 / 64)
    if max(PAR["RND"]):
        for x in ("W1", "W0", "BLKs"):
            act(B(x + "n"), B(x), 0.0, -1.0)
    act(B("IDh", 0, 16), B("IDn32", 0, 16), 0.0, -1.0)
    act(B("BM"), B("B64"), 0.0, -0.5)
    act(B("ID16"), B("IDn32"), 0.0, -16.0)
    act(B("WM2"), B("cr"), -18.5 / 64, -1.0 / 64)
    scan(B("W9"), B("B64"), B("WM2"), 0.0, OP.max, OP.mult)
    iota(B("CROW", rows=1), [[0, 8], [1, 16]], 201, 0)
    select(B("CROW", rows=1), B("CROW", rows=1), [[0, 8], [-1, 16]], OP.is_ge, 14, 0, float(CAP))
    select(B("BE"), B("BM"), [[0, 8], [-1, 16]], OP.is_ge, 14, 0)
    ms(B("ONE"), 1.0)
    for x, bits in (("p8", 7), ("p32", 31)):
        ts(B(x + "I"), B("rowI"), bits, AND)
        cp(B(x), B(x + "I"))
    ts(B("WJ"), B("cg"), B("p32"), OP.is_equal)
    ts(B("wb"), B("p32"), B("p8"), OP.subtract, 16.0, OP.is_equal)
    ts(B("wa"), B("p32"), 16.0, OP.is_lt)
    ts(B("wc"), B("wb"), 18.5, OP.mult, B("wa"), OP.add)
    ts(B("WC"), B("cr"), B("wb"), OP.mult, B("wc"), OP.add)
    ts(B("WE"), B("cg"), B("p8"), OP.is_equal)
    tt(B("WF"), B("WC"), B("WE"), OP.mult)
    ts(B("pb"), B("pp"), B("p32"), OP.subtract)
    ts(B("P4"), B("colF", 0, 128, 32), B("pb"), OP.is_equal)
    for x in ("WJ", "WF"):
        for a in range(4):
            act(B(x + "4", 128 * a, 128 * a + 128), B(x), 0.0, B("P4", a, a + 1))
    if PAR["RND"][1]:
        act(B("W9n"), B("W9"), 0.0, -1.0)
        act(B("WF4n"), B("WF4"), 0.0, -1.0)
    for k, f in enumerate((-1.0, 1.0, -1.0)):
        act(B("GA", 8 * k, 8 * k + 8), B("B64", 0, 128, 16), 0.0, f / 64)
    act(B("GP", 0, 8), B("B64", 0, 128, 16), 0.0, 1.0 / 64)
    for c in range(2):
        iota(B("SM_%d" % c, 24, 32), [[0, 8]], 0, 0)
        iota(B("PR_%d" % c, 24, 32), [[0, 8]], 0, 0)
    act(B("EXa"), B("EXz"), 0.0, 1.0)
    act(B("EXb"), B("EXz"), 0.0, 205.0)
    act(B("EXbn"), B("EXz"), 0.0, -205.0)
    act(B("ra"), B("rr"), NB - 2.0, 16.0)
    act(B("rb"), B("rr"), NB - 1.0, 16.0)
    ts(B("i16", 0, 16), B("c16"), B("rr"), OP.add)
    for k, f in enumerate((5.0, 1.0, 205.0)):
        act(B("NCT", 16 * k, 16 * k + 16), B("i16", 0, 16), 0.0, -f)
    for v in range(NV):
        iota(B("SX%d" % v, 0, 16), [[0, 16]], 0, 0)

    def send_logs(t):
        for v in range(1, NV):
            dst = T.cores[(rank - v) % n]
            how = way_of(T, topo, rank, v)
            if how == "near" and t == min(v - 1, 1):
                send(dst, B("CF%d" % v), B("CF0"), "rca%d" % v, "lca%d" % v, 1)
                send(dst, B("XL%d" % v), B("XL0"), "rla%d" % v, "lla%d" % v, 1)
            if how == "far" and t == v - 1:
                send(dst, B("CF%d" % v), B("CF0"), "rca%d" % v, "lca%d" % v)
                for k in range(2):
                    x = B("XL0", k * H // 2, (k + 1) * H // 2)
                    send(helper(T, topo, rank), x, x, "h%d" % k, "lh%d" % k, 1)
                send(dst, B("XL%d" % v, H, WX), B("XL0", H, WX), "rlb%d" % v, "llb%d" % v)
        if 0 < t < NV - 1 and way_of(T, topo, (rank + t) % n, t + 1) == "on":
            dst = T.cores[(rank - 1) % n]
            send(dst, B("CF%d" % (t + 1)), B("CF%d" % t), "rca%d" % (t + 1), "lcf%d" % t, 1)
            send(dst, B("XL%d" % (t + 1)), B("XL%d" % t), "rla%d" % (t + 1), "llf%d" % t, 1)

    for v in range(1, NV):
        own = (rank + v) % n
        at = PAR["LOG"][v - 1]
        if way_of(T, topo, own, v) == "far":
            recv(B("CF%d" % v), engines(topo, T.cores[own], core), "rca%d" % v, at - 4000)
            recv(B("XL%d" % v, 0, H), 2 * engines(topo, helper(T, topo, own), core), "rla%d" % v, at)
            recv(B("XL%d" % v, H, WX), engines(topo, T.cores[own], core), "rlb%d" % v, at)
        else:
            e = engines(topo, T.cores[(rank + 1) % n if way_of(T, topo, own, v) == "on" else own], core, 1)
            recv(B("CF%d" % v), e, "rca%d" % v, at - 4000)
            recv(B("XL%d" % v), e, "rla%d" % v, at)
    send_logs(0)
    iota(B("MROW"), [[0, 8], [-1, 16]], NB, 0)
    iota(B("DROW", rows=1), [[0, 128]], NB - 16 - 32 * TH2, 0)
    select(B("DROW", rows=1), B("DROW", rows=1), [[0, 8], [1, 16]], OP.is_gt, 0, 0, NB - 16.0)
    for c in range(2):
        iota(B("NS_%d" % c, 8, 32), [[0, 24]], 0, 0)
        iota(B("NZ_%d" % c), [[0, 144]], 0, 0)
    act(B("WN4"), B("WJ4"), 0.0, -1.0)
    act(B("IDbn"), B("IDn32"), 0.0, 1.0)
    iota(B("KT", rows=1), [[256, 8]], 0, 0)

    def lists(t, c, u, zz, new):
        D = B("D%d" % (t % 2), c * NC, c * NC + NC)
        M, oh, DS, XS = [B(x + "_%d" % c) for x in ("MASK", "OH%d" % new, "DS%d" % new, "XS%d" % new)]
        cnt, f, xp = B("pK%d" % c, new * NC, new * NC + NC), B("pF%d" % c, new * NC, new * NC + NC), B("pU%d" % c, 256, 384)
        if new:
            act(M, u, 0.5, 1.0, AF.Sign)
        else:
            tt(M, B("SROT%d" % (t % 2), c * NC, c * NC + NC), zz, OP.is_lt)
        mm([(cnt, B("B64"), M)])
        pre = PAR["XP"] and not new
        if pre:
            tt(xp, u, D, OP.mult)
        if new:
            ts(oh, cnt, -14.0 * 64, OP.max, B("rp2"), OP.is_equal)
        else:
            ts(oh, cnt, 64.0, OP.max, B("rp1"), OP.is_equal)
        scan(DS, oh, D, 0.0, OP.max, OP.mult)
        if pre:
            tt(XS, xp, oh, OP.mult)
        else:
            tt(XS, u, DS, OP.mult)
        if not new:
            ge = B("GE_%d" % c)
            either("A", "AV", lambda q: ts(ge, cnt, B("rp1"), OP.is_le) if q == "V" else act(ge, cnt, B("rp4"), -4.0, AF.Sigmoid))
        if not PAR["RND"][new]:
            mm([(f, B(("W1", "W9")[new]), DS), (f, B("W0"), oh)], True, False)
            mm([(f, B("BLKs"), XS)], False, not new)
            return
        for h in range(2):
            mm(terms(c, new, h, "n")[:2], True, False)
        for h in range(2):
            if new:
                mm(terms(c, new, h, "n")[2:], False, False)
            else:
                mm(terms(c, new, h, "n")[2:] + rounded(c, h) + terms(c, new, h, "")[::-1], False, True)

    def half(c, h):
        return B(("pF%d", "pU%d")[h] % c, 256 * h, 256 * h + 64)

    def terms(c, new, h, s):
        return [(half(c, h), B(w + s), B(x % (new, c), 64 * h, 64 * h + 64)) for w, x in ((("W1", "W9")[new], "DS%d_%d"), ("W0", "OH%d_%d"), ("BLKs", "XS%d_%d"))]

    def rounded(c, h):
        return [(half(c, h), B("ONE", rows=1), B("RM", 64 * k, 64 * k + 64, rows=1)) for k in range(2)]

    def rest(c, off):
        for h in range(2):
            o, r = (off[0], 64 * h, 64 * h + 64) + off[3:], half(c, h)
            either("V", PAR["OFFQ"], lambda q: ts(o, r, float(H), OP.add) if q == "V" else act(o, r, float(H), 1.0))

    def offsets(c, f, off):
        FI, FJ = B("FI_%d" % c), B("FJ_%d" % c)
        w = PAR["TAIL"]
        parts = [[(x[0], x[1] + a, x[1] + a + w) + x[3:] for x in (f, FI, FJ, off)] for a in range(0, NC, w)]
        for x in parts:
            ts(x[1], x[0], float(H), OP.add)
        for x in parts:
            ts(x[2], x[1], W - 1, AND)
            cp(x[3], x[2])

    for t in range(NV):
        P = t % 2
        last = t == NV - 1
        tag[1] = t

        def tm(c, a):
            return B("TL", 256 * a + NC * c, 256 * a + NC * c + NC) if t == 0 else B("TT", 256 * c + NC * a, 256 * c + NC * a + NC)
        for c in range(2):
            tag[0] = "L%d" % c
            S, st = B("SROT%d" % P, c * NC, c * NC + NC), B("ST_%d" % c, rows=8)
            ua, ub = B("pU%d" % c, 0, NC), B("pU%d" % c, NC, 2 * NC)
            z1 = B("pK%d" % c, 384, 512)
            for o in (z1, ua):
                x = [[(o, B("EXz", rows=8), st)]]
                if t:
                    x.append([((o[0], o[1] + a, o[1] + a + 32) + o[3:], B("WN4", 4 * a, 4 * a + 128), B("NS_%dT" % c)) for a in range(0, NC, 32)])
                if o == ua:
                    x.insert(len(x) if PAR["SL"][c] else 0, [(ua, B("IDn32"), S)])
                for k, y in enumerate(x):
                    mm(y, k == 0, k == len(x) - 1)
            lists(t, c, ua, z1, 0)
            if PAR["RND"][0]:
                rest(c, B("OFL_%d" % c))
            else:
                offsets(c, B("pF%d" % c, 0, NC), B("OFL_%d" % c))
            tag[0] = "H%d" % c
            rows, sn = B("pK%d" % c, 256, 384, rows=8), B("SN_%d" % c)
            mm([(rows, B("IDh", 0, 8, rows=8), st), (rows, B("NS_%d" % c, 0, 8), B("IDbn"))][:1 + (t > 0)])
            ts(sn, rows, -17.0, OP.add, -float(ZC), OP.max)
            mm([(ub, B("IDn32"), S), (ub, B("EXz", rows=8), sn)])
            lists(t, c, ub, z1, 1)
            x = "pK%d" % c
            mm([(B(x, 256, 280), B("DS0_%d" % c), B("GA")), (B(x, 272, 280), B("DS1_%d" % c), B("GA", 8, 16)),
                (B(x, 264, 272), B("XS0_%d" % c), B("BLKs", 0, 128, 16)), (B(x, 264, 272), B("XS1_%d" % c), B("GP", 0, 8))])
            tag[0] = "F%d" % c
            def fill(q, ms):
                for m in ms:
                    cp(B("Z_%d" % c, 2 * m, 32 * NC, 32), tm(c, m % 2), q)
                join(len(ms))
            for m in range(0, 16, 2):
                either("V" if m < 8 or t == 0 else "A", "VAG" if m >= PAR["GF"] else "VA", lambda q: fill(q, [m, m + 1]))
            er = B("pE%d" % c, 0, 128)
            mm([(er, tm(c, 0), B("BE")), (er, B("ONE", rows=1), B("CROW", rows=1)), (er, tm(c, 1), B("BE"))], True, False)
        for c in range(2):
            Z, MX = "Z_%d" % c, "MX_%d" % c
            for q, lo, hi in pieces(PAR["PICK"][t][c]):
                tag[0] = "Y%d" % c
                either(q, "AV", lambda q: gather(q, B(Z, 32 * lo + 1, 32 * hi, 2), B("XL%d" % t), B("OFL_%d" % c, lo, hi)))
                ops[-1]["row"] = (c, 0)
                tag[0] = "M%d" % c
                w = PAR["MW"]
                for a in range(32 * lo, 32 * hi, w):
                    scan(B(MX, a + 1, a + w), B(Z, a, a + w - 1), B(Z, a + 1, a + w), 256.0, OP.min, OP.max)
        for c in range(2):
            i0 = c * NC
            E, K, Z, MX = "pE%d" % c, "pK%d" % c, "Z_%d" % c, "MX_%d" % c
            tag[0] = "E%d" % c
            for lo, hi in PAR["EM"][c]:
                for m0 in range(0, 16 * (hi == NC), 4):
                    mm([(B(E, 0, 128) + (0, m - 1) if m % 15 else B(E, m * 14 // 15, 128, 16), B(Z, 2 * m + 1, 32 * NC, 32), B("BM", 0, 128, 8 if m % 15 else 16))
                        for m in range(m0, m0 + 4)], False, False)
                for j0 in range(0, 15, 5):
                    mm([(B(E, j, 128, 16, rows=hi) + (lo,), B(MX, 32 * lo + 2 * (j + a) + 1 + j % 2, 32 * hi, 32), B("B64", 0, 128, 16))
                        for j in range(j0, j0 + 5) for a in range(2)], False, j0 == 10 and hi == NC)
            tag[0] = "C%d" % c
            st, sm, pr = B("ST_%d" % c), "SM_%d" % c, "PR_%d" % c
            key = B("SC_%d" % c, 0, 8)
            op("V", [lambda key=key, E=E: g.vector.tensor_reduce(ap(key), ap(B(E, 0, 128)), AxisListType.X, OP.min)], [B(E, 0, 128)], [key], 128)
            ts(B("RR_%d" % c), key, R16, OP.add, R16, OP.subtract)
            for a in (8, 16):
                ts(B(sm, a, a + 8), key, float(CAP - 4), OP.is_lt)
            tt(B(sm, 0, 8), key, B("RR_%d" % c), OP.subtract)

            def spread(o, w, x, start):
                op("V", [lambda: g.vector.transpose(ap(B(x + "T")), ap(B(x)))], [B(x)], [B(x + "T")], 64)
                mm([((o[0], o[1] + a, o[1] + a + 32) + o[3:], B(w + "4", 4 * a, 4 * a + 128), B(x + "T")) for a in range(0, NC, 32)], start, True, start)
            tag[0] = "S%d" % c
            dl, gd = B(E, 384, 512), B(E, 256, 384)
            spread(dl, "WJ", sm, True)
            tt(gd, dl, B("GE_%d" % c), OP.mult)
            tt(B("SX%d" % t, 16 + i0, 16 + i0 + NC), B("SROT%d" % P, i0, i0 + NC), gd, OP.subtract)
            lo, hi = (0, 16 + NC) if c == 0 else (16 + NC, SW)
            sr = B("SR%d" % (t + 1), lo, hi)
            s = send(T.cores[(rank - 1) % n], sr, B("SX%d" % t, lo, hi), "rs%d%d" % (t + 1, c), "ls%d%d" % (t + 1, c))
            recv(sr, engines(topo, T.cores[(rank + 1) % n], core), "rs%d%d" % (t + 1, c), PAR["RECV"], s)
            tag[0] = "Q%d" % c
            tt(B(pr, 0, 24), B(sm, 0, 24), B(K, 256, 280), OP.mult)
            if PAR["RND"][1]:
                op("V", [lambda pr=pr: g.vector.transpose(ap(B(pr + "T")), ap(B(pr)))], [B(pr)], [B(pr + "T")], 64)
                for h in range(2):
                    o = half(c, h)
                    late = [[((o[0], o[1] + a, o[1] + a + 32) + o[3:], B(w, 256 * h + 4 * a, 256 * h + 4 * a + 128), B(pr + "T")) for a in (0, 32)]
                            for w in ("WF4n", "WF4")]
                    x = terms(c, 1, h, "")
                    mm(late[0] + rounded(c, h) + x[2:] + late[1] + x[:2], False, True)
                rest(c, B("OFQ_%d" % c))
            else:
                spread(B("pF%d" % c, NC, 2 * NC), "WF", pr, False)
                offsets(c, B("pF%d" % c, NC, 2 * NC), B("OFQ_%d" % c))
            tag[0] = "R%d" % c
            rows = B(K, 384, 512, rows=8)
            mm([(rows, B("IDh", 0, 8, rows=8), st), (rows, B(sm, 8, 16), B("ID16")), (rows, B("NS_%d" % c, 0, 8), B("IDbn"))][:2 + (t > 0)])
            ts(st, rows, NB - 17.0, OP.add, NB - ZC, OP.max)
        tag[0] = "X"
        send_logs(t + 1)
        if not last:
            tag[0] = "P"
            an, own, far = B("pU0", 256, 272, rows=8), B("SX%d" % (t + 1), 0, 16, rows=8), B("SR%d" % (t + 1), 0, 16, rows=8)
            mm([(an, B("SM_%d" % c, 8, 16), B("ONE", 0, 16)) for c in range(2)])
            either("V", "AV", lambda q: cp(own, an, q))
            mm([(B("pU0", 272, 304), B("IDn32"), B("NCT", 0, 32)), (B("pU0", 288, 304), B("EXbn", rows=8), far)], True, False)
            mm([(B("pU0", 272, 288), B("EXa", rows=8), own), (B("pU0", 288, 304), B("EXb", rows=8), own)], False, True)
            cp(B("LI"), B("pU0", 272, 304))
            ts(B("LJ"), B("LI"), 255, AND)
            cp(B("LOS"), B("LJ"))
            either("V", PAR["DQ"], lambda q: gather(q, B("D%d" % (1 - P)), B("CF%d" % (t + 1)), B("LOS", 0, 16), -2.0, -1.0))
            for c in range(2):
                either("V", "AV", lambda q: gather(q, B("SROT%d" % (1 - P), NC * c, NC * c + NC), B("SR%d" % (t + 1), 16, SW), B("LOS", 16 + 8 * c, 24 + 8 * c)))
        for c in range(2):
            V, MV = "V_%d" % c, "MV_%d" % c
            for q, lo, hi in pieces(PAR["PICK"][t][2 + c]):
                tag[0] = "V%d" % c
                either(q, "AV", lambda q: gather(q, B(V, 16 * lo, 16 * hi), B("XL%d" % t), B("OFQ_%d" % c, lo, hi)))
                ops[-1]["row"] = (c, 1)
                tag[0] = "D%d" % c
                scan(B(MV, 16 * lo + 1, 16 * hi), B(V, 16 * lo, 16 * hi - 1), B(V, 16 * lo + 1, 16 * hi), 256.0, OP.min, OP.max)
        for c in range(2):
            i0 = c * NC
            E, K, F, V, MV, st = "pE%d" % c, "pK%d" % c, "pF%d" % c, "V_%d" % c, "MV_%d" % c, B("ST_%d" % c, rows=8)
            tag[0] = "D%d" % c
            er, ns, ov = B(E, 0, 128), "NS_%d" % c, B("OV_%d" % c, 0, 128)
            mm([(er, B("ONE", rows=1), B("DROW", rows=1))], True, False)
            for m0 in (1, 6, 11):
                mm([(er + (0, m) if m < 15 else B(E, 15, 128, 16), B(V, m, 16 * NC, 16), B("BM", 0, 128, 8 if m < 15 else 16))
                    for m in range(m0, m0 + 5)], False, False)
            for m0 in (2, 9):
                mm([(B(E, m, 128, 16), B(MV, m, 16 * NC, 16), B("B64", 0, 128, 16)) for m in range(m0, m0 + 7)], False, m0 == 9)
            tag[0] = "N%d" % c
            tt(ov, er, B("MROW"), OP.min)
            nz = B("NZ_%d" % c, 16, 144, 16)
            x = nz if last else B(ns, 0, 8)
            op("V", [lambda x=x, ov=ov: g.vector.tensor_reduce(ap(x), ap(ov), AxisListType.X, OP.max)], [ov], [x], 128)
            if not last:
                op("V", [lambda ns=ns: g.vector.transpose(ap(B(ns + "T")), ap(B(ns)))], [B(ns)], [B(ns + "T")], 64)
            tag[0] = "T%d" % c
            if not last:
                either("A", "AV", lambda q: cp(nz, B(ns, 0, 8), q))
            tl = B(E, 128, 136)
            mm([(tl, B("ONE", rows=1), B("KT", rows=1))] + [(tl, B("NZ_%d" % c, 16 - p, 144 - p), B("IDbn", p, 128, 16)) for p in range(16)])

            def both(q):
                for a in range(2):
                    x, r = B("TO_%d" % c, 8 * a, 8 * a + 8), B(("ra", "rb")[a])
                    if q == "V":
                        ts(x, tl, r, OP.add)
                    else:
                        act(x, tl, r, 1.0)
                join(2)
            either("V", PAR["OFFQ"], both)
            either("A", "AV", lambda q: gather(q, B("TT", 256 * c, 256 * c + 256), B(V), B("TO_%d" % c)))
            if last:
                r8 = B(K, 256, 384, rows=8)
                mm([(r8, B("IDh", 0, 8, rows=8), st), (r8, nz, B("IDbn"))])
                ts(B("YZ", i0, i0 + NC), r8, float(ZC - 1), OP.add)
                for a in range(2):
                    x = B("TT", 256 * c + NC * a, 256 * c + NC * a + NC)
                    dma("SA"[a], T.yt[:, 256 * a + i0:256 * a + i0 + NC], ap(x), [x], [], "d_y%s%d" % ("ab"[a], c), 2500)
    tag[0] = "Z"
    dma("S", T.yz[:, :], ap(B("YZ")), [B("YZ")], [], "d_yz", 2000)
    fin = B("pU0", 272, 288)
    mm([(fin, B("IDn32"), B("NCT", 32, 48)), (fin, B("EXbn", rows=8), B("SR4", 0, 16, rows=8))])
    cp(B("LI", 0, 16), fin)
    ts(B("LJ", 0, 16), B("LI", 0, 16), 255, AND)
    cp(B("LOS", 0, 16), B("LJ", 0, 16))
    gather("V", B("YSO"), B("SR4", 16, SW), B("LOS", 0, 16), 1.0, float(ZC))
    dma("S", T.ys[:, :], ap(B("YSO")), [B("YSO")], [], "d_ys", 2500)
    return ops


def meet(a, b):
    return a[1] < b[2] and b[1] < a[2] and (a[1] - b[1]) % math.gcd(a[3], b[3]) == 0


def covers(a, b):
    return a[1] <= b[1] and b[2] <= a[2] and b[3] % a[3] == 0 and (b[1] - a[1]) % a[3] == 0 and b[4] <= a[4]


def link(ops):
    hist, turns, prev = {}, {}, {}
    for k, o in enumerate(ops):
        deps = {}

        def add(x, hard):
            deps[x] = deps.get(x, False) or hard
        if "after" in o:
            add(o["after"], False)
        if o["kind"] == "send" or o["kind"] == "dma" and o["w"]:
            if (o["q"], o["kind"]) in prev:
                add(prev[o["q"], o["kind"]], False)
            prev[o["q"], o["kind"]] = k
        acc = [(r, False) for r in o["r"]] + [(w, True) for w in o["w"]]
        for b in set(r[0] for r, wr in acc if SCRATCH[r[0]][0] == "psum"):
            was, now = turns.get(b, ([], []))
            if now and (ops[now[0]]["q"] != o["q"] or "alt" in o or "alt" in ops[now[0]]):
                was, now = now, []
            for x in was:
                add(x, True)
            if now and o["q"] == "P":
                add(now[-1], False)
            turns[b] = (was, now + [k])
        for r, wr in acc:
            for (x, r2, w2) in hist.get(r[0], ()):
                if (wr or w2) and meet(r, r2):
                    add(x, not (o["q"] == "P" and ops[x]["q"] == "P"))
        for r, wr in acc:
            h = hist.setdefault(r[0], [])
            if wr:
                h[:] = [y for y in h if y[0] == k or not covers(r, y[1])]
            h.append((k, r, wr))
        o["deps"] = deps


def order(ops):
    n = len(ops)
    sync = PAR["SYNC"]
    busy = [{"dma": 60.0, "recv": 0.0}.get(o["kind"], o["cost"]) for o in ops]
    lag = [{x: (ops[x]["cost"] + sync if h else busy[x]) for x, h in o["deps"].items()} for o in ops]
    succ = [{} for _ in range(n)]
    for k in range(n):
        for x, l in lag[k].items():
            succ[x][k] = l

    def place(key, back):
        first = succ if back else lag
        for k in (range(n - 1, -1, -1) if back else range(n)):
            a = key[k]
            for x in first[k]:
                if key[x] >= a:
                    a = key[x] + 1e-3
            key[k] = a
        slots, t0 = {q: [] for q in "VAPGSR"}, [0.0] * n
        for a, k in sorted(zip(key, range(n))):
            w = busy[k]
            if back:
                t = ops[k]["cost"]
                for x, d in first[k].items():
                    d += t0[x] + busy[x]
                    if d > t:
                        t = d
                t -= w
            else:
                t = 0.0
                for x, d in first[k].items():
                    d += t0[x]
                    if d > t:
                        t = d
            if w:
                l = slots[ops[k]["q"]]
                i = m = len(l)
                while i and l[i - 1][1] > t:
                    i -= 1
                while i < m and l[i][0] < t + w:
                    if l[i][1] > t:
                        t = l[i][1]
                    i += 1
                l.insert(i, (t, t + w))
            t0[k] = t
        if back:
            return [-a - b for a, b in zip(t0, busy)], 0
        return t0, max(t0[k] + ops[k]["cost"] for k in range(n - 40, n))
    way = [0.0] * n
    for k in range(n - 1, -1, -1):
        way[k] = max([ops[k]["cost"]] + [way[s] + d for s, d in succ[k].items()])
    seed = [PAR["SEED"]]

    def rnd():
        seed[0] = (seed[0] * 1103515245 + 12345) % 2 ** 31
        return seed[0] / 2 ** 31

    def assign(k, q):
        ops[k]["q"], ops[k]["fns"], ops[k]["cost"] = q, ops[k]["alt"][q][0], ops[k]["alt"][q][1]
        busy[k] = ops[k]["cost"]
        for s in succ[k]:
            succ[k][s] = lag[s][k] = busy[k] + sync

    def packed(key, bar=1e9):
        t0, end = place(key, False)
        if end > bar:
            return end, t0
        t1, e1 = place(place([-(t0[k] + busy[k]) for k in range(n)], True)[0], False)
        return (e1, t1) if e1 < end else (end, t0)
    free = [k for k in range(n) if "alt" in ops[k]]
    blocks = {}
    for k in range(n):
        blocks.setdefault(ops[k]["blk"], []).append(k)
    same = {}
    for b, l in blocks.items():
        for i, k in enumerate(l):
            same.setdefault((b[0], i, len(l)), []).append(k)
    like = {k: l for l in same.values() for k in l}
    mark = [blocks[("C0", t)][0] for t in range(NV)]
    blocks = list(blocks.values())

    def chain(t0):
        before = {(ops[k]["q"], round(t0[k] + busy[k], 3)): k for k in range(n) if busy[k]}
        k, held = max(range(n), key=lambda k: t0[k] + ops[k]["cost"]), []
        while t0[k] > 0:
            x = [x for x, d in lag[k].items() if t0[x] + d > t0[k] - 1e-3]
            if x:
                k = x[0]
            else:
                held.append((k, before[(ops[k]["q"], round(t0[k], 3))]))
                k = held[-1][1]
        return held
    sig = tuple((o["blk"], o["kind"], o["sem"]) for o in ops)
    own = [k for k in range(n) if ops[k]["kind"] in ("c", "dma")]
    key, turns = [-w for w in way], PAR["TURNS"]
    if "first" in DONE:
        key, turns = [0.0] * n, turns // 8
        for k, t in zip(own, DONE["first"][0]):
            key[k] = t
        for k, q in zip(free, DONE["first"][1]):
            assign(k, q)
    cur = best = DONE.get(sig) or packed(key) + ([ops[k]["q"] for k in free],)
    for it in range(0 if sig in DONE else turns):
        key = list(cur[1])
        r = rnd()
        if rnd() < PAR["COPY"]:
            a, b = int(rnd() * NV), int(rnd() * NV)
            d = key[mark[b]] - key[mark[a]]
            for l in same.values():
                x = {ops[k]["blk"][1]: k for k in l}
                if a in x and b in x:
                    key[x[b]] = key[x[a]] + d
                    if ops[x[a]]["q"] in ops[x[b]].get("alt", ""):
                        assign(x[b], ops[x[a]]["q"])
        elif r < PAR["MOVE"][0]:
            held = chain(cur[1])
            for _ in range(1 + int(2 * rnd())):
                k, p = held[int(rnd() * len(held))]
                a = p if "alt" in ops[p] and rnd() < 0.5 else k
                tied = rnd() < PAR["TIED"]
                if "alt" in ops[a] and rnd() < 0.6:
                    qs = [q for q in sorted(ops[a]["alt"]) if q != ops[a]["q"]]
                    q = qs[int(rnd() * len(qs))]
                    for x in (like[a] if tied else [a]):
                        assign(x, q)
                else:
                    a, d = (k, key[p] - key[k] - 300 * rnd()) if rnd() < 0.5 else (p, key[k] - key[p] + 1000 * rnd())
                    for x in (like[a] if tied else [a]):
                        key[x] += d
        elif r < PAR["MOVE"][1]:
            for _ in range(1 + int(2 * rnd())):
                k = free[int(rnd() * len(free))]
                qs = sorted(ops[k]["alt"])
                q = qs[int(rnd() * len(qs))]
                for x in (like[k] if rnd() < 0.5 else [k]):
                    assign(x, q)
        else:
            for _ in range(1 + int(3 * rnd())):
                d = (rnd() - 0.5) * (600, 2000, 6000)[int(3 * rnd())]
                b = blocks[int(rnd() * len(blocks))]
                for k in b:
                    for x in (like[k] if it % 2 else [k]):
                        key[x] += d
        new = packed(key, cur[0] + PAR["BAR"]) + ([ops[k]["q"] for k in free],)
        if new[0] <= cur[0] + PAR["HEAT"] * rnd() * (turns - it) / PAR["TURNS"]:
            cur = new
            if new[0] < best[0]:
                best = new
        else:
            for k, q in zip(free, cur[2]):
                assign(k, q)
    if sig not in DONE:
        for k, q in zip(free, best[2]):
            assign(k, q)
        best = refine(ops, lag, busy, best, free, assign, rnd, turns * PAR["FINE"])
    DONE[sig] = best
    DONE.setdefault("first", ([best[1][k] for k in own], best[2]))
    for k, q in zip(free, best[2]):
        assign(k, q)
    for k in range(n):
        ops[k]["t0"] = best[1][k]
    return sorted(range(n), key=lambda k: (best[1][k], k))


def refine(ops, lag, busy, best, free, assign, rnd, turns):
    n = len(ops)
    seq = sorted(range(n), key=lambda k: (best[1][k], k))
    last = range(n - 40, n)

    def times(seq, lo, t, by):
        t, by, fr, who = list(t), list(by), {q: 0.0 for q in "VAPGSR"}, {q: -1 for q in "VAPGSR"}
        left = 5
        for k in seq[lo - 1::-1] if lo else ():
            q = ops[k]["q"]
            if who[q] < 0 and busy[k]:
                who[q], fr[q] = k, t[k] + busy[k]
                left -= 1
                if not left:
                    break
        for k in seq[lo:]:
            a, b = 0.0, -1
            for x, d in lag[k].items():
                d += t[x]
                if d > a:
                    a, b = d, x
            w = busy[k]
            if w:
                q = ops[k]["q"]
                if fr[q] > a:
                    a, b = fr[q], -2 - who[q]
                fr[q], who[q] = a + w, k
            t[k], by[k] = a, b
        return max((t[k] + ops[k]["cost"], k) for k in last), t, by
    (end, top), t, by = times(seq, 0, [0.0] * n, [-1] * n)
    best = (end, t, [ops[k]["q"] for k in free])
    held = None
    for it in range(turns):
        if held is None:
            held, k = [], top
            while k != -1:
                b = by[k]
                if b < -1:
                    b = -2 - b
                    held.append((k, b))
                k = b
            pos = {k: i for i, k in enumerate(seq)}
        k, p = held[int(rnd() * len(held))]
        a = (k, p)[rnd() < 0.5]
        i, j = pos[p], pos[k]
        was = None
        if "alt" in ops[a] and rnd() < 0.4:
            qs = [q for q in sorted(ops[a]["alt"]) if q != ops[a]["q"]]
            was = ops[a]["q"]
            assign(a, qs[int(rnd() * len(qs))])
            new, lo = seq, pos[a]
        elif a == k:
            i = max(0, i - int(rnd() * rnd() * PAR["FAR"]))
            up = {k}
            for x in seq[j - 1:i - 1 if i else None:-1]:
                if any(x in lag[y] for y in up):
                    up.add(x)
            part = seq[i:j + 1]
            new, lo = seq[:i] + [x for x in part if x in up] + [x for x in part if x not in up] + seq[j + 1:], i
        else:
            j = min(n - 1, j + int(rnd() * rnd() * PAR["FAR"]))
            down = {p}
            for x in seq[i + 1:j + 1]:
                if any(y in down for y in lag[x]):
                    down.add(x)
            part = seq[i:j + 1]
            new, lo = seq[:i] + [x for x in part if x not in down] + [x for x in part if x in down] + seq[j + 1:], i
        (e, tp), t2, by2 = times(new, lo, t, by)
        if e <= end + PAR["WARM"] * rnd() * rnd() * (turns - it) / turns:
            end, top, t, by, held = e, tp, t2, by2, None
            seq = sorted(new, key=lambda k: t[k])
            if e < best[0]:
                best = (e, t, [ops[k]["q"] for k in free])
        elif was:
            assign(a, was)
    return best


def emit(g, T, ops, seq):
    queue = {"V": g.vector, "A": g.scalar, "P": g.tensor, "G": g, "S": g.sync}
    total = {"V": 0, "A": 0, "P": 0, "G": 0}
    know = {q: {} for q in queue}
    issued = []
    for k in seq:
        o = ops[k]
        q = o["q"]
        if o["kind"] == "recv":
            o["done"] = (o["sem"], o["cnt"])
            o["clock"] = {}
            issued.append(o["done"])
            continue
        eng = queue[q]
        for x in sorted(o["deps"], reverse=True):
            if not o["deps"][x]:
                continue
            d = ops[x]
            s, v = d["done"]
            if know[q].get(s, 0) >= v:
                continue
            eng.wait_ge(T.sem[s], v)
            know[q][s] = v
            for s2, v2 in d["clock"].items():
                if know[q].get(s2, 0) < v2:
                    know[q][s2] = v2
        if o["kind"] == "c":
            for f in o["fns"]:
                f().then_inc(T.sem["s" + q], 1)
            total[q] += len(o["fns"])
            o["done"] = ("s" + q, total[q])
        elif o["kind"] == "dma":
            for f in o["fns"]:
                f().then_inc(T.sem[o["sem"]], 16)
            o["done"] = (o["sem"], 16)
        else:
            for f in o["fns"]:
                f()
            o["done"] = (o["sem"], o["cnt"])
        o["clock"] = dict(know[q])
        if o["kind"] != "c":
            issued.append(o["done"])
    for q in total:
        if total[q]:
            issued.append(("s" + q, total[q]))
    for s, v in issued:
        if know["G"].get(s, 0) < v:
            g.wait_ge(T.sem[s], v)


def rank_program(g, core, T, topo):
    if T.rank_of(core) is None:
        for r in range(len(T.cores)):
            if core == helper(T, topo, r):
                hand_on(g, core, T, topo, r)
        return
    ops = plan(g, core, T, topo)
    link(ops)
    emit(g, T, ops, order(ops))
